import numpy as np, ml_dtypes
CORES = [5,29,101,125,133,157,229,253]
N = 8
import mx_ref
BF = ml_dtypes.bfloat16
def gcols(t, e):
    v = np.concatenate([t.reshape(8, 16, -1, 4), np.zeros((8, 16, 1, 4), BF)], axis=2)
    return np.ascontiguousarray(np.stack([v[g][:, e[g]] for g in range(8)])).reshape(128, -1)
def tile(rs):
    return np.stack(rs, axis=2).reshape(128, -1).astype(BF)
def cut(t, i, w=512):
    return t[:, w * i:w * i + w]
def pick(q, e):
    c = np.concatenate([q[0].reshape(128, -1, 4), np.zeros((128, 1, 4), np.uint8)], axis=1); s = np.concatenate([q[1], np.ones((16, 1), np.uint8)], axis=1)
    return (np.ascontiguousarray(c[:, e].reshape(128, -1)), np.ascontiguousarray(s[:, e]))
def join(*qs):
    return (np.concatenate([q[0] for q in qs], axis=1), np.concatenate([q[1] for q in qs], axis=1))
def put(q, e, v):
    c, s = q[0].reshape(128, -1, 4).copy(), q[1].copy(); c[:, e] = v[0].reshape(128, -1, 4); s[:, e] = v[1]
    return (c.reshape(128, -1), s)
def pk(c, s):
    return (np.ascontiguousarray(c), mx_ref.live(s))
def emit(q):
    return q[0], q[1]
def packed(v, rng):
    q = [mx_ref.quantize(np.ascontiguousarray(v[r])) for r in range(N)]
    return np.stack([a for a, b in q]), np.stack([mx_ref.plane(b, rng) for a, b in q])
def values_of_codes():
    e, c = np.zeros((128, 128, 4), np.float32), np.zeros((128, 2, 4), np.uint8)
    e[np.arange(128), np.arange(128), 0] = 1
    c[:127, :, 0] = np.arange(256).reshape(2, 128).T[:127]
    return mx_ref.matmul(mx_ref.quantize(e.reshape(128, 512).astype(BF)), (c.reshape(128, 8), np.full((16, 2), 127, np.uint8))).T.reshape(-1).astype(np.float64)
CODE_VALUE, SCALE_VALUE = values_of_codes(), 2.0 ** (np.arange(256) - 127.0)
def decode(q):
    return (CODE_VALUE[q[0]].reshape(16, 8, -1, 4) * SCALE_VALUE[q[1]][:, None, :, None] + 0.0).reshape(128, -1).astype(np.float32)
def f(rng, *shape):
    return mx_ref.flush((rng.standard_normal(shape, dtype=np.float32) * np.exp2(rng.integers(-2, 3, shape[:-1] + (1,)))).astype(BF))
def wide(rng, *shape, cols=0):
    v = rng.standard_normal(shape, dtype=np.float32) * np.exp2(rng.integers(-12, 13, shape)).astype(np.float32)
    if cols: v *= np.repeat(np.exp2(rng.integers(-cols, cols + 1, shape[:-2] + (1, shape[-1] // 4))) * (rng.random(shape[:-2] + (1, shape[-1] // 4)) > 0.0625), 4, axis=-1).astype(np.float32)
    return mx_ref.flush(v.astype(BF))
C, L, R = 448, 128, 3
def order(p, s):
    return np.lexsort((-(s + np.float32(0.0)), -p))
def pairs(p):
    a, b = np.zeros((8, C // 2), np.int64), np.zeros((8, C // 2), np.int64)
    for g in range(8):
        end = [int(np.sum(p[g] >= k)) // 2 * 2 for k in range(3 + R, -1, -1)]
        for i, k in zip(end, end[1:]):
            m = (k - i) // 2
            a[g, i // 2:k // 2] = np.arange(i, i + m)
            b[g, i // 2:k // 2] = np.arange(i + m, k)
    return a, b
def gput(t, e, h):
    a, b = t.reshape(8, 16, -1, 4).copy(), h.reshape(8, 16, -1, 4)
    for g in range(8): a[g][:, e[g]] = b[g]
    return a.reshape(128, -1)
def big(v):
    v = v.astype(np.float32)
    v[np.abs(v) < np.float32(2.0 ** -16)] = 0
    return v.astype(BF)
def numbers_of(rng):
    return {"x": big(f(rng, N, 128, 4 * C)), "u": np.array(f(rng, N, 128, 512)), "v": np.array(f(rng, N, 128, 512))}
def layers(rng):
    return big(f(rng, N, 128, 2048)).reshape(N, 8, 16, 4, 8, 16, 4)
def weights(rng, w):
    c, p = packed(np.ascontiguousarray(w).reshape(N, 128, 2048), rng)
    return {"wc": c, "ws": p}
def signs(rng):
    return np.stack([rng.permutation(8) % 2 * 2.0 - 1.0 for r in range(N)])
def setup_inputs(rng):
    return {**numbers_of(rng), **weights(rng, layers(rng))}
def setup_inputs_ties(rng):
    d = numbers_of(rng)
    e = rng.permutation(N)
    x = d["x"].reshape(N, 8, 16, C, 4)
    for r in range(N):
        k = np.zeros(C, int) if r == e[0] else rng.permutation(C) % 3
        a = x[r][:, :8, :3].copy()
        a[:, :, 2] = 0
        x[r][:, :8] = a[:, :, k]
    x[e[1]] = 0
    u = d["u"].reshape(N, 8, 16, 8, 16, 4)
    u[:, :, 8:, :, :4] = 0
    w = layers(rng)
    w[:, :, 8:, :, :, :8] = 0
    return {"x": x.reshape(N, 128, 4 * C), "u": u.reshape(N, 128, 512), "v": d["v"], **weights(rng, w)}
def setup_inputs_near(rng):
    d = numbers_of(rng)
    x = np.zeros((N, 8, 16, C, 4), np.float32)
    u = d["u"].reshape(N, 128, 128, 4)
    for m in range(4): u[:, :, m::16] = 0
    o, c = rng.permutation(N) % 4, signs(rng)
    upper = np.arange(C) // (C // 2)
    for r in range(N):
        i = (np.arange(C) + rng.integers(0, C, (8, 1))) % C
        if o[r] == 3: i = i % (C // 2) * 2 + upper
        s = (i + 1) // 2
        size = 1.0 if o[r] < 2 else 2.0 ** -4
        g = ((s[:, :, None] >> np.arange(8)) & 1) * np.exp2(np.arange(8) - 23.0) * size
        if o[r] < 2: x[r, :, 0, :, 0] = c[r][:, None]
        if o[r] == 3:
            x[r, :, 0, :, 0] = (8 + upper) * 2.0 ** -33
            x[r, :, 1, :, 0] = (9 - upper) * 2.0 ** -33
        x[r, :, 8] = g[:, :, :4]
        x[r, :, 9] = g[:, :, 4:]
        x[r, :, 10:] = rng.integers(4, 8, (8, 6, C, 4)) * 2.0 ** -20 * size
        x[r, :, 11, :, 0] = rng.integers(-1, 2, (8, C)) * 2.0 ** -18 * size
        x[r, :, 12, :, 0] = 0
        same = (rng.permutation(8) % 2 == 0)[:, None, None]
        x[r, :, 13:, :, 0] = np.where(same, rng.integers(-1, 2, (8, 3, 1)), rng.integers(-1, 2, (8, 3, C))) * 2.0 ** -18 * size
        k = 1.0 if o[r] == 0 else 2.0 ** -30
        for h in range(0, 128, 16):
            u[r, h, h, 0] = 1.125 * k if o[r] == 3 else k
            u[r, h + 1, h, 0] = k
            u[r, h + 8:h + 10, h] = k
            u[r, h + 12, h, 0] = k
            for m in range(3): u[r, h + 13 + m, h + 1 + m, 0] = k
    w = layers(rng)
    w[:, :, :10] = 0
    w[:, :, :, :, :, :2] = 0
    w[:, :, :, :, :, 8:] = 0
    for g in range(8): w[:, g, 11, 0, g, 12, 0] = 0.25
    return {"x": x.reshape(N, 128, 4 * C).astype(BF), "u": u.reshape(N, 128, 512), "v": d["v"], **weights(rng, w)}
def setup_inputs_brackets(rng):
    d = numbers_of(rng)
    x = d["x"].reshape(N, 8, 16, C, 4)
    x[:, :, :8] = 0
    x[:, :, 12] = 0
    q = rng.integers(-1, 2, (N, 8, C))
    for g, m in enumerate(rng.permutation(8)):
        if m < 3: q[:, g] = m - 1
    x[:, :, 13, :, 0] = q.astype(np.float32).astype(BF)
    small = rng.permutation(N) < N // 2
    for r in range(N):
        i, j, k = 2 * rng.integers(0, C // 8, 3) + 1
        n = rng.permutation(np.array([[0, 0, 0, C], [C, 0, 0, 0], [1, 0, 0, C - 1], [C - 1, 0, 0, 1], [1, 1, 1, C - 3], [C - 2 * L, 0, 0, 2 * L], [0, 3, 0, C - 3], [i, j, k, C - i - j - k]]))
        unit = 2.0 ** -30 if small[r] else 0.125
        for g in range(8):
            p = rng.permutation(np.repeat([3, 2, 1, 0], n[g]))
            on = np.argsort(rng.random((3, C)), axis=0) < p
            a = np.where(on, 1.0, -1.0 * rng.integers(0, 2, (3, C)))
            x[r, g, :3, :, 0] = ((8 + np.maximum(a, 0)) * unit).astype(np.float32).astype(BF)
            x[r, g, 3:6, :, 0] = ((8 + np.maximum(-a, 0)) * unit).astype(np.float32).astype(BF)
    u = d["u"].reshape(N, 8, 16, 8, 16, 4)
    b = u.copy()
    s = np.where(small, 2.0 ** -30, 1.0).astype(np.float32)
    u[:, :, :, :, :4] = 0
    w = layers(rng)
    w[:, :, :, :, :, 8:] = 0
    for g in range(8):
        u[:, g, 8:11, g, 0] = b[:, g, 8:11, g, 0]
        u[:, g, 12, g, 0, 0] = 1
        for m in range(3):
            u[:, g, m, g, 1 + m, 0] = s.astype(BF)
            u[:, g, 3 + m, g, 1 + m, 0] = (-s).astype(BF)
        w[:, g, 13, 0, g, 12, 0] = 1
    return {"x": x.reshape(N, 128, 4 * C), "u": u.reshape(N, 128, 512), "v": d["v"], **weights(rng, w)}
def setup_inputs_huge(rng):
    d = numbers_of(rng)
    c = np.stack([rng.permutation(C) % 2 * 2.0 - 1.0 for r in range(N)])
    c[rng.permutation(N) < N // 2] = -1
    x = 2.0 ** 30 * (0.55 + 0.2 * rng.random((N, 128, C, 4))) * c[:, None, :, None]
    u = d["u"].reshape(N, 128, 8, 16, 4)
    k = rng.choice([-1.0, 1.0], (N, 8, 4))
    k[:, :, 0] = signs(rng)
    a = 2.0 ** 30 * (1 - 0.1 * rng.random((N, 128, 8, 4, 4))) * k[:, None, :, :, None]
    u[:, :, :, :4] = a.astype(np.float32).astype(BF)
    w = np.zeros((N, 128, 4, 128, 4), np.float32)
    i = np.arange(128)
    for b in range(4): w[:, i, b, i, b] = -1
    return {"x": x.astype(np.float32).reshape(N, 128, 4 * C).astype(BF), "u": u.reshape(N, 128, 512), "v": d["v"], **weights(rng, w.astype(BF))}
def setup_inputs_spread(rng):
    d = setup_inputs(rng)
    d["x"] = big(wide(rng, N, 128, 4 * C, cols=6))
    return d
def check_inputs(d):
    b = []
    for k in ("x", "u", "v"):
        a = np.abs(d[k].astype(np.float32))
        if not (np.isfinite(a).all() and ((a == 0) | (a >= 2.0 ** -30) & (a <= 2.0 ** 30)).all()): b.append("a value of " + k)
    none, least, most = [emit(mx_ref.quantize(np.full((128, 16), k, np.float32).astype(BF)))[1][0, 0] for k in (0.0, 2.0 ** -30, 2.0 ** 30)]
    for r in range(N):
        if ((d["wc"][r] == 0x7F) | (d["wc"][r] == 0xFF)).any(): b.append("wc: a code that is no number")
        s = mx_ref.live(d["ws"][r])
        if ((s != none) & ((s < least) | (s > most))).any(): b.append("ws: a scale out of range")
    return b
def reference(x, u, v, wc, ws):
    qu = [mx_ref.quantize(u[r]) for r in range(N)]
    lay = [pk(wc[r], ws[r]) for r in range(N)]
    now = [x[r] for r in range(N)]
    points = []
    for t in range(R):
        sent, gone, moved = [], [], []
        for r in range(N):
            s = mx_ref.matmul(qu[r], mx_ref.quantize(now[r]))
            if t == 0: points.append(np.sum(s.reshape(8, 16, C)[:, 1:4] > 0, axis=1))
            o = order(points[r], s[::16])
            i, k = pairs(points[r])
            a, b = np.take_along_axis(o, i, 1), np.take_along_axis(o, k, 1)
            first, second = gcols(now[r], a).astype(np.float32), gcols(now[r], b).astype(np.float32)
            q = mx_ref.quantize(((first + second) * np.float32(0.5)).astype(BF))
            h = tile([mx_ref.matmul(pick(lay[r], np.arange(128 * m, 128 * m + 128)), q) * np.float32(0.03125) for m in range(4)])
            won = mx_ref.matmul(qu[r], mx_ref.quantize(h))[::16] > 0
            h = h.astype(np.float32)
            now[r] = gput(gput(now[r], a, (first + h).astype(BF)), b, (second - h).astype(BF))
            gain = np.zeros((8, C), np.int64)
            np.put_along_axis(gain, a, won.astype(np.int64), 1)
            np.put_along_axis(gain, b, (~won).astype(np.int64), 1)
            points[r] = points[r] + gain
            back = np.take_along_axis(points[r], o, 1)[:, ::-1]
            e = np.take_along_axis(o, C - 1 - np.argsort(back, axis=1, kind="stable")[:, :L], 1)
            gone.append(e)
            moved.append(np.take_along_axis(points[r], e, 1))
            sent.append(mx_ref.quantize(gcols(now[r], e)))
        came = decode(join(*sent)).astype(BF)
        for r in range(N):
            p = (r - 1) % N
            now[r] = gput(now[r], gone[r], cut(came, p, 4 * L))
            np.put_along_axis(points[r], gone[r], moved[p], 1)
    y, pts = np.zeros((N, 128, C), np.float32), np.zeros((N, 8, C), np.float32)
    oc, osc = np.zeros((N, 128, 4 * C), np.uint8), np.zeros((N, 16, C), np.uint8)
    for r in range(N):
        q = mx_ref.quantize(now[r])
        y[r] = mx_ref.matmul(mx_ref.quantize(v[r]), q)
        pts[r] = points[r]
        oc[r], osc[r] = emit(q)
    return {"y": y, "pts": pts, "oc": oc, "osc": osc}

@@ -1,0 +1,537 @@
+import numpy as np
+from concourse.bass import DstId, RemoteDMATransfer
+from concourse.mybir import dt, AluOpType, ActivationFunctionType
+
+C, L, R = 448, 128, 3
+HALF = C // 2
+NB = C // 16
+NVS = (20, 19, 19)
+B0 = (C - HALF - L) // 16
+P0 = 16 * B0
+BIG = 2.0 ** 80
+F = 2.0 ** 14
+TW = [128] + [64 * (m + 1) for m in range(1, 7)]
+TO = [sum(TW[:m]) for m in range(7)]
+RS = 8 * (NB - 1)
+X4, B2, F4, I4, U2, U1 = "float8_e4m3fn_x4", "bfloat16", "float32", "int32", "uint16", "uint8"
+
+_S = {
+    B2: dict(x0=4 * C, xs=4 * C, xh=4 * C, ut=512, vt=512, em=528, ones=528, cst=512, cpt=512, g64=512, pf=4 * C, fl=4 * sum(TW),
+             cm=C, ck=C, k16=C, k4=C, kx=C, seg=C, k5=560, sg=2 * C, rsc=RS * 9, sgn=256, dsc=C, exb=3 * C, win=6 * C, so=6 * C,
+             clr=C, clp=C, eqr=C + 16, lh=560, lo=560, bh=2 * C, ab=4 * C, zt=2 * C, ht=2 * C, xn=4 * (C + L), gr=C, gb=C,
+             lrg=3 * C, st=4 * L, ptr=C),
+    F4: dict(pc=16, tab=128, cnt=C + L, jw=112, cw=NB, yy=C, hd=C, rs=NB, poff=NB, base=NB, wf=384, ex=C, ef=32,
+             plr=C, orow=C, abr=C, fr=C, lr=C, nxr=C),
+    I4: dict(pi=16, ei=16),
+    U2: dict(ulu=8, qo=NB, o1=NB, plw=NB, fiw=NB, fw=NB, clw=NB, jlw=NB, m2w=NB, nx1=NB, ab4=4 * NB, nx4=4 * NB, l4=32, l1=8),
+    X4: dict(wq=512, uq=128, urq=128, vq=128, xq=C, eq4=512, csq=128, cpq=128, pfq=C, flq=sum(TW), zq=HALF, hq=HALF),
+    U1: dict(wp=512, up=128, urp=128, vp=128, xp=C, ep4=512, csp=128, cpp=128, pfp=C, flp=sum(TW), zp=HALF),
+}
+for _t in range(R):
+    _S[X4].update({"sq%d" % _t: L, "rq%d" % _t: L, "aq%d" % _t: L})
+    _S[U1].update({"sp%d" % _t: L + HALF, "rp%d" % _t: 2 * L, "ap%d" % _t: L})
+    _S[B2].update({"sn%d" % _t: L, "rn%d" % _t: L, "pw%d" % _t: C + L})
+SCRATCH = {n: ("sbuf", [128, w], d) for d in _S for n, w in _S[d].items()}
+SCRATCH["ps"] = ("psum", [128, 4096], F4)
+SEMAPHORES = (["qv", "qs", "qp", "qg", "sent", "lu", "lx", "lw", "lv", "out"]
+              + ["%s%d" % (n, t) for t in range(R) for n in ("hop", "arc", "arp")])
+
+OP = AluOpType
+AF = ActivationFunctionType
+
+
+def _relays(rank_core, nxt, topo):
+    c = [k for k in topo.cores_of(rank_core) if k != rank_core and topo.may_write(k, nxt)]
+    return sorted(c, key=lambda k: topo.die(k) != topo.die(rank_core))[:4]
+
+
+def _mask(engs):
+    return sum(1 << e for e in engs)
+
+
+def hand_on(g, core, T, topo, nxt, k):
+    rid, pid = topo.addr(nxt, core)
+    m = topo.mask(core, nxt)
+    for t in range(R):
+        g.wait_ge(T.sem["hop%d" % t], 4)
+        if k < 2:
+            a, b = 64 * k, 64 * k + 64
+            dst, src, sem = T["aq%d" % t][:, a:b].bitcast(dt.uint8), T["rq%d" % t][:, a:b].bitcast(dt.uint8), "arc%d" % t
+        elif k == 2:
+            dst, src, sem = T["ap%d" % t][:, 0:L], T["rp%d" % t][:, 0:L], "arc%d" % t
+        else:
+            dst, src, sem = T["pw%d" % t][:, C:C + L], T["rn%d" % t][:, 0:L], "arp%d" % t
+        g.remote_dma(dst, src, T.sem[sem], T.sem.sent, pid, rid, m)
+    g.wait_ge(T.sem.sent, len(topo.engines(core, nxt)) * R)
+
+
+def rank_program(g, core, T, topo):
+    cores = list(T.cores)
+    rank = T.rank_of(core)
+    if rank is None:
+        for r, c in enumerate(cores):
+            nxt = cores[(r + 1) % len(cores)]
+            rl = _relays(c, nxt, topo)
+            if core in rl:
+                hand_on(g, core, T, topo, nxt, rl.index(core))
+        return
+    relays = _relays(core, cores[(rank + 1) % len(cores)], topo)
+    n_in = [len(topo.engines(k, core)) for k in _relays(cores[rank - 1], core, topo)]
+
+    Q = {"v": g.vector, "s": g.scalar, "p": g.tensor, "g": g, "y": g.sync}
+    QS = {"v": "qv", "s": "qs", "p": "qp", "g": "qg"}
+    count = {}
+    known = {q: {} for q in Q}
+    lastw, lastr = {}, {}
+    V, S = g.vector, g.scalar
+
+    def A(name, a=0, b=None, s=1):
+        n = SCRATCH[name][1][1]
+        b = n if b is None else b
+        return (T[name][:, a:b:s] if s != 1 else T[name][:, a:b], name, np.arange(n)[a:b:s])
+
+    def bank(k, n):
+        return (T.ps[:, 512 * k:512 * k + n], "ps", np.array([k]))
+
+    def need(q, reads, writes):
+        w = {}
+
+        def look(d, name, idx, skip=None):
+            for sem, arr in d.get(name, {}).items():
+                if sem != skip:
+                    w[sem] = max(w.get(sem, 0), int(arr[idx].max()))
+        for _, name, idx in reads:
+            look(lastw, name, idx)
+            if name == "ps":
+                look(lastr, name, idx, QS.get(q))
+        for _, name, idx in writes:
+            look(lastw, name, idx, "qp" if q == "p" else None)
+            look(lastr, name, idx)
+        for sem, val in w.items():
+            if val > known[q].get(sem, 0):
+                Q[q].wait_ge(T.sem[sem], val)
+                known[q][sem] = val
+
+    def mark(sem, val, reads, writes):
+        count[sem] = val
+        for d, xs in ((lastr, reads), (lastw, writes)):
+            for _, name, idx in xs:
+                d.setdefault(name, {}).setdefault(sem, np.zeros(SCRATCH[name][1][1], np.int64))[idx] = val
+
+    def op(q, reads, writes, call):
+        reads = [x for x in reads if isinstance(x, tuple)]
+        writes = [x for x in writes if isinstance(x, tuple)]
+        need(q, reads, writes)
+        call().then_inc(T.sem[QS[q]], 1)
+        mark(QS[q], count.get(QS[q], 0) + 1, reads, writes)
+
+    def raw(x):
+        return x[0] if isinstance(x, tuple) else x
+
+    def ind(win, by):
+        return win[0].indirect(by[0]) if by else win[0]
+
+    def memset(o, c):
+        op("v", [], [o], lambda: V.memset(o[0], c))
+
+    def ts(o, i, s1, op0, s2=None, op1=None):
+        more = () if op1 is None else (op1,)
+        op("v", [i, s1, s2], [o], lambda: V.tensor_scalar(o[0], i[0], raw(s1), raw(s2), op0, *more))
+
+    def tt(o, a, b, o_, by=None):
+        op("v", [a, b, by], [o], lambda: V.tensor_tensor(o[0], ind(a, by), b[0], o_))
+
+    def cp(o, i, by=None):
+        op("v", [i, by], [o], lambda: V.tensor_copy(o[0], ind(i, by)))
+
+    def scatter(win, by, i):
+        op("v", [i, by], [win], lambda: V.tensor_copy(ind(win, by), i[0]))
+
+    def scan(o, d0, d1, init, op0, op1):
+        op("v", [d0, d1], [o], lambda: V.tensor_tensor_scan(o[0], d0[0], d1[0], init, op0, op1))
+
+    def act(o, i, f=AF.Copy, bias=None, scale=1.0, acc=None, by=None):
+        kw = {"scale": raw(scale)}
+        if bias is not None:
+            kw["bias"] = raw(bias)
+        if acc:
+            kw["accum_out"] = acc[0]
+        op("s", [i, bias, scale, by], [o, acc], lambda: S.activation(o[0], ind(i, by), f, **kw))
+
+    def quant2(p, i):
+        op("v", [i], p, lambda: V.quantize_mx(p[0][0], p[1][0], i[0]))
+
+    def pair(n, a=0, b=None):
+        return [A(n + "q", a, b), A(n + "p", a, b)]
+
+    def quant(n, i, a=0, b=None):
+        quant2(pair(n, a, b), i)
+
+    def mm(o, l, r, start=True, stop=True):
+        op("p", l + r, [o], lambda: g.tensor.matmul_mx(o[0], l[0][0], l[1][0], r[0][0], r[1][0], start, stop))
+
+    def iota(o, pattern, base=0, cm=0):
+        kw = {} if SCRATCH[o[1]][2] == I4 else {"allow_small_or_imprecise_dtypes": True}
+        op("g", [], [o], lambda: g.iota(o[0], pattern, base, cm, **kw))
+
+    def fill(o, c):
+        iota(o, [[0, len(o[2])]], c)
+
+    def dma(q, sem, total, out, in_, reads, writes):
+        need(q, reads, writes)
+        Q[q].dma_start(out, in_).then_inc(T.sem[sem], 16)
+        mark(sem, total, reads, writes)
+
+    CQ, CQ1, CQ4, CQ41, CG, CS16, CS4, CT4, CQ2, CP, CF16 = [A("pc", k, k + 1) for k in range(11)]
+
+    def W(k, n=NB):
+        return A("wf", 32 * k, 32 * k + n)
+
+    def keep16(row, n):
+        scan(A("ex", 0, n), A("k16", 0, n), row, 0.0, OP.mult, OP.add)
+
+    def read16(dst, n):
+        ts(dst, A("ex", 15, n, 16), CS16, OP.mult, -0.26, OP.add)
+
+    def wrap4(row, n, dst, a=0):
+        scan(A("ex", a, a + n), A("k4", 0, n), row, 0.0, OP.mult, OP.add)
+        ts(dst, A("ex", a + 3, a + n, 4), CS4, OP.mult, CT4, OP.add)
+
+    def hold(row, k, n):
+        scan(A("exb", k * n, k * n + n), row, A("kx", 0, n), -512.0, OP.max, OP.add)
+
+    dma("y", "lu", 16, T.ut[:], T.u[:], [], [A("ut")])
+    dma("s", "lx", 32, T.x0[:, 0:2 * C], T.x[:, 0:2 * C], [], [A("x0", 0, 2 * C)])
+    dma("y", "lx", 32, T.x0[:, 2 * C:4 * C], T.x[:, 2 * C:4 * C], [], [A("x0", 2 * C, 4 * C)])
+    dma("y", "lw", 32, T.wq[:].bitcast(dt.uint8), T.wc[:], [], [A("wq")])
+    dma("y", "lw", 32, T.wp[:], T.ws[:], [], [A("wp")])
+    dma("y", "lv", 16, T.vt[:], T.v[:], [], [A("vt")])
+
+    def pi(k):
+        return A("pi", k, k + 1)
+
+    def tab(k):
+        return A("tab", 16 * k, 16 * k + 16)
+
+    def zone(m):
+        fill(A("fl", 4 * (TO[m] + (400 if m == 6 else 64 * m + 16)), 4 * (TO[m] + TW[m])), 0)
+
+    iota(pi(0), [[0, 1]], 0, 1)
+    iota(tab(0), [[1, 16]])
+    iota(A("cw"), [[16, NB]])
+    iota(A("pi", 8, 16), [[16, 8]])
+    iota(tab(1), [[0, 4], [1, 4]])
+    iota(A("jw", 14, 42), [[8, NB]])
+    iota(A("g64"), [[1, 8], [0, 64]])
+    zone(6)
+    zone(4)
+    iota(A("seg"), [[0, NB], [64, 16]])
+    for m in (3, 5, 2, 1, 0):
+        zone(m)
+    fill(A("ones"), 1)
+    fill(A("win", 0, 4 * C), 0)
+    iota(A("cnt"), [[1, C + L]])
+    iota(A("k5"), [[0, 112], [256, 5]])
+    fill(A("lh"), 0)
+    op("g", [A("ones")], [A("em")], lambda: g.affine_select(T.em[:], T.ones[:], [[-1, 528]], OP.is_equal, 0.0, 3, 4))
+
+    memset(A("eqr", 0, 2), 0.0)
+    memset(A("eqr", C, C + 2), 0.0)
+    memset(A("rs", 0, 1), 0.0)
+    ts(pi(1), pi(0), 15, OP.bitwise_and)
+    ts(pi(2), pi(0), 4, OP.arith_shift_right)
+    cp(CQ, pi(1))
+    ts(pi(3), pi(1), 2, OP.arith_shift_right)
+    ts(pi(4), pi(1), 3, OP.bitwise_and)
+    ts(A("qo"), A("cw"), 0.0, OP.mult, CQ, OP.add)
+    ts(tab(2), tab(0), CQ, OP.is_equal, 2 * BIG, OP.mult)
+    ts(tab(3), tab(0), CQ, OP.is_gt, 2 * BIG, OP.mult)
+    ts(CQ1, pi(1), 1.0, OP.add)
+    ts(tab(2), tab(2), -BIG, OP.add)
+    ts(tab(3), tab(3), -BIG, OP.add)
+    act(A("cm"), tab(2), by=A("qo"))
+    act(A("ck"), tab(3), by=A("qo"))
+    ts(tab(4), tab(0), CQ, OP.is_lt, -512.0, OP.mult)
+    ts(tab(5), tab(0), CQ, OP.is_equal, 256.0, OP.mult)
+    ts(tab(6), tab(0), 15.0, OP.is_equal, -512.0, OP.mult)
+    ts(tab(7), tab(0), CQ1, OP.is_equal, F, OP.mult)
+    tt(tab(4), tab(4), tab(5), OP.add)
+    ts(tab(0), tab(0), CQ, OP.not_equal)
+    cp(A("ulu"), A("pi", 8, 16))
+    tt(tab(4), tab(4), tab(6), OP.add)
+    tt(tab(7), tab(7), tab(0), OP.max)
+    act(A("kx"), tab(4), by=A("qo"))
+    act(A("k16"), tab(7), by=A("qo"))
+    memset(A("pf"), 0.0)
+    ts(pi(5), pi(1), 1, OP.arith_shift_right)
+    cp(CG, pi(2))
+    cp(CQ4, pi(3))
+    ts(CQ41, pi(3), 1.0, OP.add)
+    ts(CP, pi(1), 2.0, OP.subtract)
+    ts(CT4, pi(4), -0.2, OP.add)
+    cp(CQ2, pi(5))
+    tt(CP, CP, CP, OP.mult)
+    ts(CS16, pi(1), 15.0, OP.is_equal, 1.0 - 1.0 / F, OP.mult)
+    ts(CF16, pi(1), 15.0, OP.not_equal, F - 1.0, OP.mult)
+    ts(CS4, pi(3), 3.0, OP.is_equal, 4.0 - 4.0 / F, OP.mult)
+    ts(CP, CP, 1.0, OP.is_le)
+    ts(CS16, CS16, 1.0 / F, OP.add)
+    ts(CF16, CF16, 1.0, OP.add)
+    ts(CS4, CS4, 4.0 / F, OP.add)
+    quant("u", A("ut"))
+    op("v", [A("uq"), A("ulu")], [A("urq")], lambda: V.tensor_copy(
+        T.urq[:, 0:128].bitcast(dt.uint32), T.uq[:, 0:128].bitcast(dt.uint32).indirect(T.ulu[:, 0:8])))
+    op("v", [A("up"), A("ulu")], [A("urp")], lambda: V.tensor_copy(T.urp[:, 0:128], T.up[:, 0:128].indirect(T.ulu[:, 0:8])))
+    ts(A("cpt"), A("g64"), CG, OP.is_equal, CP, OP.mult)
+    ts(A("cst"), A("g64"), CG, OP.is_equal)
+    ts(A("jw", 42, 70), A("cw"), CQ, OP.add)
+    ts(tab(5), tab(1), CQ41, OP.is_equal, F, OP.mult)
+    ts(tab(1), tab(1), CQ4, OP.not_equal)
+    quant("cp", A("cpt"))
+    quant("cs", A("cst"))
+    ts(A("cw"), A("cw"), CQ, OP.subtract, 15.0, OP.add)
+    ts(A("jw", 14, 42), A("jw", 14, 42), CQ2, OP.add)
+    cp(A("jw", 0, 14), A("jw", 42, 56))
+    ts(A("jw", 70, 84), A("jw", 42, 56), float(HALF), OP.add)
+    ts(A("jw", 84, 112), A("jw", 42, 70), -1.0, OP.mult, C - 1.0, OP.add)
+    tt(tab(5), tab(5), tab(1), OP.max)
+    cp(W(8, B0), A("jw", 84, 84 + B0))
+
+    def slot(b):
+        m = (b - 1) // 4
+        return 4 * TO[m] + 4 * m + 4 - b
+
+    def qtile(m):
+        a, b = TO[m], TO[m] + TW[m]
+        quant("fl", A("fl", 4 * a, 4 * b), a, b)
+        mm(bank(2, TW[m]), pair("cs"), pair("fl", a, b), m == 6, m == 0)
+
+    for t in range(R):
+        K = 4 + t
+        NV = NVS[t]
+        xb = "x0" if t == 0 else "xs"
+        sq, sp, sn, pw = "sq%d" % t, "sp%d" % t, "sn%d" % t, "pw%d" % t
+        quant("x", A(xb))
+        mm(bank(0, C), pair("ur"), pair("x"))
+        if t == 0:
+            mm(bank(3, C), pair("u"), pair("x"))
+        mm(bank(1, C), pair("ur"), pair("x"))
+        if t == 0:
+            act(A("sg", 0, C), bank(3, C), AF.Sign)
+            act(A("pf", 0, 4 * C, 4), A("sg", 0, C), AF.Relu)
+        else:
+            act(A("ptr"), A("pw%d" % (t - 1)), by=A("nx1"))
+            hold(A("ptr"), 0, C)
+        tt(A("yy"), bank(0, C), A("cm"), OP.min)
+        scan(A("hd"), A("ck"), A("yy"), 0.0, OP.min, OP.max)
+
+        def s_sign(b):
+            h = (b % 2) * C
+            act(A("sg", h, h + 16 * b), bank(1, 16 * b), AF.Sign, bias=A("hd", 16 * b + 15, 16 * b + 16), scale=-1.0)
+
+        def s_relu(b):
+            h = (b % 2) * C
+            act(A("fl", slot(b), slot(b) + 64 * b, 4), A("sg", h, h + 16 * b), AF.Relu, acc=A("rs", b, b + 1))
+
+        def v_cmp(b):
+            ts(A("fl", slot(b), slot(b) + 64 * b, 4), bank(0, 16 * b), A("hd", 16 * b + 15, 16 * b + 16), OP.is_lt)
+
+        def v_sum(b):
+            e = RS * (b - NV + 1)
+            scan(A("rsc", e - 8 * b, e), A("fl", slot(b), slot(b) + 32 * b, 4), A("fl", slot(b) + 32 * b, slot(b) + 64 * b, 4),
+                 -float(HALF), OP.add, OP.add)
+
+        s_sign(NV - 1)
+        for b in range(NV - 1, 0, -1):
+            if b > 1:
+                s_sign(b - 1)
+            s_relu(b)
+        if t == 0:
+            act(A("k4"), tab(5), by=A("qo"))
+        act(A("xh"), A(xb), scale=0.5)
+        diag = A("fl", 4 * TO[6], 4 * TO[6] + 4 * C, 4)
+        tt(diag, bank(0, C), A("hd"), OP.is_le)
+        if t == 0:
+            quant("pf", A("pf"))
+            mm(bank(4, C), pair("cp"), pair("pf"))
+        v_cmp(NB - 1)
+        scan(A("dsc"), A("seg"), diag, 0.0, OP.min, OP.add)
+        for b in range(NB - 1, NV - 1, -1):
+            if b - 1 >= NV:
+                v_cmp(b - 1)
+            v_sum(b)
+            if b == 26 and t == 0:
+                hold(bank(4, C), 0, C)
+            if b == 25:
+                qtile(6)
+                ts(A("poff"), A("exb", 15, C, 16), -float(C), OP.mult, float(C * (K - 1 - 256)), OP.add)
+            if b == 24:
+                tt(A("base"), A("cw"), A("dsc", 15, C, 16), OP.subtract)
+            if b == 23:
+                tt(A("base"), A("base"), A("poff"), OP.add)
+            if b == 22:
+                qtile(3)
+            if b == 21:
+                qtile(5)
+        ts(A("rs", NV, NB), A("rsc", RS - 1, RS * (NB - NV), RS), float(HALF), OP.add)
+        qtile(4)
+        qtile(2)
+        qtile(1)
+        qtile(0)
+        tt(A("base"), A("base"), A("rs"), OP.subtract)
+        ts(A("base"), A("base"), CF16, OP.mult)
+        keep16(bank(2, C), C)
+        tt(W(0), A("ex", 15, C, 16), A("base"), OP.add)
+        ts(A("o1"), W(0), CS16, OP.mult, -0.26, OP.add)
+        n = K * C
+        scatter(A("win", 0, n), A("o1"), A("ones", 0, C))
+        scan(A("so", 0, n), A("win", 0, n), A("win", 0, n), -C - 2.0, OP.add, OP.add)
+        act(A("plr"), A("so", 0, n), AF.Identity, bias=float(HALF), scale=0.5, by=A("o1"))
+        if t + 1 < R:
+            fill(A("win", 0, n + C), 0)
+        ends = A("so", C - 1, C * (K - 1), C)
+        k1 = K - 1
+        ts(A("ei", 0, k1), ends, 0.5, OP.mult, HALF + 1.0, OP.add)
+        ts(A("ef", 0, k1), ends, 0.5, OP.mult, HALF + 1.0, OP.add)
+        ts(A("ei", 8, 8 + k1), A("ei", 0, k1), 1, OP.arith_shift_right)
+        for k in range(k1):
+            ts(A("lh", 420 + k, 560, 5), A("jw", 42, 70), A("ef", k, k + 1), OP.is_lt, float(k1 - k), OP.mult)
+            if k == 0:
+                ts(A("ef", 24, 24 + k1), A("ei", 8, 8 + k1), -1.0, OP.mult, 0.5, OP.add)
+                cp(A("ef", 8, 8 + k1), A("ei", 8, 8 + k1))
+                ts(A("ef", 16, 16 + k1), A("ei", 8, 8 + k1), -float(HALF), OP.add)
+        for k in range(k1):
+            act(A("sgn", 42 * k, 42 * k + 42), A("jw", 0, 42), AF.Sign, bias=A("ef", 24 + k, 25 + k))
+        for k in range(k1):
+            act(A("lh", k, 210, 5), A("sgn", 42 * k, 42 * k + 42), scale=A("ef", 8 + k, 9 + k))
+            act(A("lh", 210 + k, 420, 5), A("sgn", 42 * k, 42 * k + 42), scale=A("ef", 16 + k, 17 + k))
+        keep16(A("plr"), C)
+        scan(A("lo", 420, 560), A("k5", 420, 560), A("lh", 420, 560), 0.0, OP.min, OP.max)
+        read16(A("plw"), C)
+        cp(A("clw"), A("lo", 424, 560, 5))
+        scatter(A("orow"), A("plw"), A("cnt", 0, C))
+        act(A("clr"), A("cnt", 0, 16), by=A("clw"))
+        scan(A("lo", 0, 420), A("k5", 0, 420), A("lh", 0, 420), 0.0, OP.min, OP.max)
+        tt(A("wf", 46, 60), A("jw", 70, 84), A("lo", 214, 280, 5), OP.subtract)
+        tt(A("wf", 32, 46), A("jw", 0, 14), A("lo", 4, 70, 5), OP.add)
+        cp(A("fiw"), W(1))
+        act(A("abr", HALF, C), A("orow"), by=A("fiw", 14, 28))
+        cp(A("abr", 0, HALF), A("orow"), by=A("fiw", 0, 14))
+        wrap4(A("abr", HALF, C), HALF, A("ab4", 2 * NB, 4 * NB), HALF)
+        wrap4(A("abr", 0, HALF), HALF, A("ab4", 0, 2 * NB))
+        lo_, hi_ = A("lo", 74, 210, 5), A("lo", 284, 420, 5)
+        tt(W(2), A("jw", 42, 70), lo_, OP.subtract)
+        for k in range(4):
+            act(A("bh", HALF * k, HALF * k + HALF), A("xh"), by=A("ab4", 2 * NB + 14 * k, 2 * NB + 14 * k + 14))
+        for k in range(4):
+            tt(A("zt", HALF * k, HALF * k + HALF), A("xh"), A("bh", HALF * k, HALF * k + HALF), OP.add, by=A("ab4", 14 * k, 14 * k + 14))
+        act(A("ab", 0, 2 * C), A(xb), by=A("ab4", 0, 2 * NB))
+        quant("z", A("zt"))
+        for b in range(4):
+            mm(bank(3 + b, HALF), pair("w", 128 * b, 128 * b + 128), pair("z"))
+        tt(A("eqr", 1, C), A("clr", 1, C), A("clr", 0, C - 1), OP.is_equal)
+        ts(A("ht", 0, 2 * C, 4), bank(3, HALF), 0.03125, OP.mult)
+        ts(A("ht", 1, 2 * C, 4), bank(4, HALF), 0.03125, OP.mult)
+        for b in (2, 3):
+            act(A("ht", b, 2 * C, 4), bank(3 + b, HALF), scale=0.03125)
+        tt(W(3), lo_, hi_, OP.add)
+        tt(W(4), W(2), hi_, OP.add)
+        qh = [A("hq"), A(sp, L, L + HALF)]
+        quant2(qh, A("ht"))
+        mm(bank(7, HALF), pair("ur"), qh)
+        act(A("ab", 2 * C, 4 * C), A("bh"), scale=2.0)
+        ts(W(4), W(4), float(HALF), OP.is_ge)
+        tt(W(4), W(4), W(3), OP.mult)
+        tt(W(7), W(4), W(2), OP.add)
+        ts(A("gr", 0, HALF), bank(7, HALF), 0.0, OP.is_gt)
+        cp(A("fw"), W(7))
+        ts(A("gr", HALF, C), bank(7, HALF), 0.0, OP.is_le)
+        act(A("gb"), A("gr"), AF.Identity, bias=1.0, scale=-1.0, by=A("fw"))
+        act(A("lrg", 2 * C + P0, 3 * C), A("gb", P0, C), AF.Identity, bias=1.0, scale=-1.0)
+        act(A("fr", P0, C), A("cnt", 0, C), by=A("fw", B0, NB))
+        tt(A("xn", 0, 2 * C), A("ab", 0, 2 * C), A("ht"), OP.add)
+        scan(A("lrg", 0, C), A("eqr", 0, C), A("gb"), 0.0, OP.mult, OP.add)
+        hold(A("lrg", P0, C), 0, C - P0)
+        scan(A("lrg", 2 * C - 1, C + P0 - 1, -1), A("eqr", C, P0, -1), A("lrg", 3 * C - 1, 2 * C + P0 - 1, -1), 0.0, OP.mult, OP.add)
+        hold(A("lrg", 2 * C + P0, 3 * C), 2, C - P0)
+        hold(A("lrg", C + P0, 2 * C), 1, C - P0)
+        w = NB - B0
+        ts(A("wf", 288, 288 + 3 * w), A("exb", 15, 3 * (C - P0), 16), 256.0, OP.add)
+        lg, rg, gm = [A("wf", 288 + w * k, 288 + w * k + w) for k in range(3)]
+        jl = A("wf", 256 + B0, 256 + NB)
+        tt(W(5, w), lg, rg, OP.add)
+        tt(W(6, w), A("jw", 84 + B0, 112), rg, OP.subtract)
+        tt(W(5, w), W(5, w), gm, OP.mult)
+        tt(jl, W(5, w), W(6, w), OP.add)
+        cp(A("jlw", 0, w), jl)
+        scatter(A("lr"), A("jlw", 0, w), A("fr", P0, C))
+        scan(A("ex", 0, L), A("k4", 0, L), A("lr", 0, L), 0.0, OP.mult, OP.add)
+        tt(A("xn", 2 * C, 4 * C), A("ab", 2 * C, 4 * C), A("ht"), OP.subtract)
+        ts(A("l4"), A("ex", 3, L, 4), CS4, OP.mult, CT4, OP.add)
+        act(A("st", 2 * L, 4 * L), A("xn", 0, 4 * C), by=A("l4", 16, 32))
+        cp(A("st", 0, 2 * L), A("xn", 0, 4 * C), by=A("l4", 0, 16))
+        quant2([A(sq), A(sp, 0, L)], A("st"))
+        need("g", [A(sq), A(sp)], [])
+        tr = []
+        for k in range(3):
+            rid, pid = topo.addr(relays[k], core)
+            if k < 2:
+                src, dst = T[sq][:, 64 * k:64 * k + 64].bitcast(dt.uint8), T["rq%d" % t][:, 64 * k:64 * k + 64].bitcast(dt.uint8)
+            else:
+                src, dst = T[sp][:, 0:2 * L], T["rp%d" % t][:, 0:2 * L]
+            tr.append(RemoteDMATransfer(dst_ids=[DstId(rid=rid, pnc=pid)], dma_engine_mask=_mask(topo.engines(core, relays[k])[4 * k:4 * k + 4]),
+                                        remote_sem=T.sem["hop%d" % t], src=src, dst=dst))
+        g.remote_dma_fused(tr, local_sem=T.sem.sent)
+        act(A("clp"), A("clr"), by=A("fiw"))
+        tt(W(5), W(8), W(7), OP.subtract)
+        ts(W(6), W(8), float(L), OP.is_lt)
+        keep16(A("lr", 0, L), L)
+        ts(W(5), W(5), float(C), OP.add)
+        read16(A("l1"), L)
+        tt(W(5), W(5), W(6), OP.mult)
+        tt(W(5), W(5), W(7), OP.add)
+        cp(A("m2w"), W(5))
+        act(A("abr"), A("cnt"), by=A("m2w"))
+        act(A("nxr"), A("abr"), by=A("plw"))
+        tt(A(pw, 0, C), A("clp"), A("gr"), OP.add)
+        cp(A(sn), A(pw, 0, C), by=A("l1"))
+        need("g", [A(sn)], [])
+        rid, pid = topo.addr(relays[3], core)
+        g.remote_dma(T["rn%d" % t][:, 0:L], T[sn][:, 0:L], T.sem["hop%d" % t], T.sem.sent, pid, rid,
+                     _mask(topo.engines(core, relays[3])[12:16]))
+        if t == 0:
+            quant("v", A("vt"))
+            for b in range(4):
+                quant2([A("eq4", 128 * b, 128 * b + 128), A("ep4", 128 * b, 128 * b + 128)], A("em", 3 - b, 515 - b))
+        wrap4(A("nxr"), C, A("nx4"))
+        keep16(A("nxr"), C)
+        read16(A("nx1"), C)
+        came = [A("aq%d" % t), A("ap%d" % t)]
+        mark("arc%d" % t, n_in[0] + n_in[1] + n_in[2], [], came)
+        mark("arp%d" % t, n_in[3], [], [A(pw, C, C + L)])
+        for b in (0, 2, 1, 3):
+            mm(bank(3 + b, L), [A("eq4", 128 * b, 128 * b + 128), A("ep4", 128 * b, 128 * b + 128)], came)
+        for b in range(2):
+            cp(A("xn", 4 * C + b, 4 * (C + L), 4), bank(3 + b, L))
+            act(A("xn", 4 * C + 2 + b, 4 * (C + L), 4), bank(5 + b, L))
+        act(A("xs", 2 * C, 4 * C), A("xn"), by=A("nx4", 2 * NB, 4 * NB))
+        cp(A("xs", 0, 2 * C), A("xn"), by=A("nx4", 0, 2 * NB))
+
+    total = 16 * 8
+    quant("x", A("xs"))
+    for k in range(2):
+        mm(bank(k, HALF), pair("v"), pair("x", HALF * k, HALF * k + HALF))
+    dma("y", "out", total, T.oc[:], T.xq[:].bitcast(dt.uint8), [A("xq")], [])
+    act(A("plr"), A("pw%d" % (R - 1)), by=A("nx1"))
+    cp(A("orow", 0, HALF), bank(0, HALF))
+    act(A("orow", HALF, C), bank(1, HALF))
+    for k in range(2):
+        dma("y", "out", total, T.osc[4 * k:4 * k + 4, :], T.xp[32 * k:32 * k + 4, :], [A("xp")], [])
+    dma("y", "out", total, T.y[:, 0:HALF], T.orow[:, 0:HALF], [A("orow", 0, HALF)], [])
+    dma("s", "out", total, T.y[:, HALF:C], T.orow[:, HALF:C], [A("orow", HALF, C)], [])
+    dma("s", "out", total, T.pts[:], T.plr[0:128:16, :], [A("plr")], [])
+    for k in range(2, 4):
+        dma("s" if k % 2 else "y", "out", total, T.osc[4 * k:4 * k + 4, :], T.xp[32 * k:32 * k + 4, :], [A("xp")], [])
+    count["sent"] = 16 * R
+    for sem, val in count.items():
+        g.wait_ge(T.sem[sem], val)

@@ -17,7 +17,7 @@ X4, B2, F4, I4, U2, U1 = "float8_e4m3fn_x4", "bfloat16", "float32", "int32", "ui
 
 _S = {
     B2: dict(x0=4 * C, xs=4 * C, xh=4 * C, ut=512, vt=512, em=528, ones=528, cst=512, cpt=512, g64=512, pf=4 * C, fl=4 * sum(TW),
-             cm=C, ck=C, k16=C, k4=C, kx=C, seg=C, k5=560, sg=2 * C, rsc=RS * 9, sgn=256, dsc=C, exb=3 * C, win=6 * C, so=6 * C,
+             cm=C, ck=C, k16=C, k4=C, kx=C, seg=C, k5=560, sg=3200 + C, rsc=RS * 9, sgn=256, dsc=C, exb=3 * C, win=6 * C, so=6 * C,
              clr=C, clp=C, eqr=C + 16, lh=560, lo=560, bh=2 * C, ab=4 * C, zt=2 * C, ht=2 * C, xn=4 * (C + L), gr=C, gb=C,
              lrg=3 * C, st=4 * L, ptr=C),
     F4: dict(pc=16, tab=128, cnt=C + L, jw=112, cw=NB, yy=C, hd=C, rs=NB, poff=NB, base=NB, wf=384, ex=C, ef=32,
@@ -38,6 +38,67 @@ SEMAPHORES = (["qv", "qs", "qp", "qg", "sent", "lu", "lx", "lw", "lv", "out"]
 
 OP = AluOpType
 AF = ActivationFunctionType
+_PLAN = {}
+WAKE = 80
+TRIES = 120
+
+
+def _schedule(ops, tol):
+    n = len(ops)
+    before = [o[1] + o[2] for o in ops]
+    prio = [0.0] * n
+    for i in range(n - 1, -1, -1):
+        prio[i] += ops[i][4]
+        for d in before[i]:
+            prio[d] = max(prio[d], prio[i] + WAKE)
+    todo = {}
+    for i in sorted(range(n), key=lambda k: -prio[k]):
+        todo.setdefault(ops[i][0], []).append(i)
+    end, free, order = {}, {q: 0.0 for q in todo}, []
+
+    def ready(i, memo):
+        if i not in memo:
+            r = free[ops[i][0]]
+            for d in ops[i][1]:
+                e = end[d] if d in end else ready(d, memo) + ops[d][4]
+                r = max(r, e + (0 if ops[i][0] == ops[d][0] == "p" else WAKE))
+            memo[i] = r
+        return memo[i]
+
+    while len(order) < n:
+        memo, pick, spare = {}, None, None
+        for q, lst in todo.items():
+            can = [i for i in lst[:24] if all(d in end for d in before[i])]
+            if not can:
+                continue
+            top = lst[0]
+            fit = [i for i in can if i == top or ready(i, memo) + ops[i][6] <= ready(top, memo) + tol[i]]
+            if fit:
+                i = min(fit, key=lambda k: (ready(k, memo), -prio[k]))
+                if pick is None or ready(i, memo) < ready(pick, memo):
+                    pick = i
+            if spare is None or prio[can[0]] > prio[spare]:
+                spare = can[0]
+        i = spare if pick is None else pick
+        r = ready(i, memo)
+        end[i], free[ops[i][0]] = r + ops[i][4], r + ops[i][6]
+        todo[ops[i][0]].remove(i)
+        order.append(i)
+    return max(end.values()), order
+
+
+def _plan(ops):
+    rng = np.random.default_rng(1)
+    tol = np.full(len(ops), 60.0)
+    best = _schedule(ops, tol)
+    for _ in range(TRIES):
+        new = tol.copy()
+        k = rng.integers(0, len(ops), 60)
+        new[k] = rng.choice([0.0, 60.0, 200.0, 500.0], 60)
+        r = _schedule(ops, new)
+        if r[0] <= best[0]:
+            best, tol = r, new
+    return best[1]
 
 
 def _relays(rank_core, nxt, topo):
@@ -80,10 +141,8 @@ def rank_program(g, core, T, topo):
 
     Q = {"v": g.vector, "s": g.scalar, "p": g.tensor, "g": g, "y": g.sync}
     QS = {"v": "qv", "s": "qs", "p": "qp", "g": "qg"}
-    count = {}
-    known = {q: {} for q in Q}
-    lastw, lastr = {}, {}
     V, S = g.vector, g.scalar
+    ops, lastw, readers = [], {}, {}
 
     def A(name, a=0, b=None, s=1):
         n = SCRATCH[name][1][1]
@@ -93,37 +152,29 @@ def rank_program(g, core, T, topo):
     def bank(k, n):
         return (T.ps[:, 512 * k:512 * k + n], "ps", np.array([k]))
 
-    def need(q, reads, writes):
-        w = {}
-
-        def look(d, name, idx, skip=None):
-            for sem, arr in d.get(name, {}).items():
-                if sem != skip:
-                    w[sem] = max(w.get(sem, 0), int(arr[idx].max()))
-        for _, name, idx in reads:
-            look(lastw, name, idx)
-            if name == "ps":
-                look(lastr, name, idx, QS.get(q))
-        for _, name, idx in writes:
-            look(lastw, name, idx, "qp" if q == "p" else None)
-            look(lastr, name, idx)
-        for sem, val in w.items():
-            if val > known[q].get(sem, 0):
-                Q[q].wait_ge(T.sem[sem], val)
-                known[q][sem] = val
-
-    def mark(sem, val, reads, writes):
-        count[sem] = val
-        for d, xs in ((lastr, reads), (lastw, writes)):
-            for _, name, idx in xs:
-                d.setdefault(name, {}).setdefault(sem, np.zeros(SCRATCH[name][1][1], np.int64))[idx] = val
-
-    def op(q, reads, writes, call):
+    def op(q, reads, writes, call, ns, token=None, after=(), busy=None):
         reads = [x for x in reads if isinstance(x, tuple)]
         writes = [x for x in writes if isinstance(x, tuple)]
-        need(q, reads, writes)
-        call().then_inc(T.sem[QS[q]], 1)
-        mark(QS[q], count.get(QS[q], 0) + 1, reads, writes)
+        me, deps = len(ops), set()
+        for _, name, idx in reads + writes:
+            deps.update(int(d) for d in np.unique(lastw.setdefault(name, np.full(SCRATCH[name][1][1], -1))[idx]) if d >= 0)
+        for _, name, idx in reads:
+            if name == "ps":
+                deps.update(d for d, m in readers.get(name, []) if m[idx].any() and ops[d][0] != q)
+        for _, name, idx in writes:
+            for d, m in readers.get(name, []):
+                if m[idx].any():
+                    deps.add(d)
+                    m[idx] = False
+            readers[name] = [x for x in readers.get(name, []) if x[1].any()]
+            lastw[name][idx] = me
+        for _, name, idx in reads:
+            m = np.zeros(SCRATCH[name][1][1], bool)
+            m[idx] = True
+            readers.setdefault(name, []).append((me, m))
+        deps.discard(me)
+        ops.append((q, sorted(deps), list(after), call, ns, token, ns if busy is None else busy))
+        return me
 
     def raw(x):
         return x[0] if isinstance(x, tuple) else x
@@ -131,24 +182,30 @@ def rank_program(g, core, T, topo):
     def ind(win, by):
         return win[0].indirect(by[0]) if by else win[0]
 
+    def ns_of(o, xs, by=None, k=1.0):
+        if by:
+            return 60 + 1.4 * len(o[2])
+        two = all(SCRATCH[x[1]][2] in (B2, U2) for x in [o] + xs)
+        return 60 + 0.9 * k * len(o[2]) * (0.5 if two else 1)
+
     def memset(o, c):
-        op("v", [], [o], lambda: V.memset(o[0], c))
+        op("v", [], [o], lambda: V.memset(o[0], c), ns_of(o, []))
 
     def ts(o, i, s1, op0, s2=None, op1=None):
         more = () if op1 is None else (op1,)
-        op("v", [i, s1, s2], [o], lambda: V.tensor_scalar(o[0], i[0], raw(s1), raw(s2), op0, *more))
+        op("v", [i, s1, s2], [o], lambda: V.tensor_scalar(o[0], i[0], raw(s1), raw(s2), op0, *more), ns_of(o, [i]))
 
     def tt(o, a, b, o_, by=None):
-        op("v", [a, b, by], [o], lambda: V.tensor_tensor(o[0], ind(a, by), b[0], o_))
+        op("v", [a, b, by], [o], lambda: V.tensor_tensor(o[0], ind(a, by), b[0], o_), ns_of(o, [a, b], by, 1 if a[1] == "ps" else 2))
 
     def cp(o, i, by=None):
-        op("v", [i, by], [o], lambda: V.tensor_copy(o[0], ind(i, by)))
+        op("v", [i, by], [o], lambda: V.tensor_copy(o[0], ind(i, by)), ns_of(o, [i], by))
 
     def scatter(win, by, i):
-        op("v", [i, by], [win], lambda: V.tensor_copy(ind(win, by), i[0]))
+        op("v", [i, by], [win], lambda: V.tensor_copy(ind(win, by), i[0]), 60 + 3.2 * len(i[2]))
 
     def scan(o, d0, d1, init, op0, op1):
-        op("v", [d0, d1], [o], lambda: V.tensor_tensor_scan(o[0], d0[0], d1[0], init, op0, op1))
+        op("v", [d0, d1], [o], lambda: V.tensor_tensor_scan(o[0], d0[0], d1[0], init, op0, op1), ns_of(o, [d0, d1]))
 
     def act(o, i, f=AF.Copy, bias=None, scale=1.0, acc=None, by=None):
         kw = {"scale": raw(scale)}
@@ -156,10 +213,10 @@ def rank_program(g, core, T, topo):
             kw["bias"] = raw(bias)
         if acc:
             kw["accum_out"] = acc[0]
-        op("s", [i, bias, scale, by], [o, acc], lambda: S.activation(o[0], ind(i, by), f, **kw))
+        op("s", [i, bias, scale, by], [o, acc], lambda: S.activation(o[0], ind(i, by), f, **kw), 75 + (1.4 if by else 0.9) * len(o[2]))
 
     def quant2(p, i):
-        op("v", [i], p, lambda: V.quantize_mx(p[0][0], p[1][0], i[0]))
+        op("v", [i], p, lambda: V.quantize_mx(p[0][0], p[1][0], i[0]), 15 + 0.25 * len(i[2]))
 
     def pair(n, a=0, b=None):
         return [A(n + "q", a, b), A(n + "p", a, b)]
@@ -168,19 +225,44 @@ def rank_program(g, core, T, topo):
         quant2(pair(n, a, b), i)
 
     def mm(o, l, r, start=True, stop=True):
-        op("p", l + r, [o], lambda: g.tensor.matmul_mx(o[0], l[0][0], l[1][0], r[0][0], r[1][0], start, stop))
+        op("p", l + r, [o], lambda: g.tensor.matmul_mx(o[0], l[0][0], l[1][0], r[0][0], r[1][0], start, stop), 60 + 0.6 * len(r[0][2]))
 
     def iota(o, pattern, base=0, cm=0):
         kw = {} if SCRATCH[o[1]][2] == I4 else {"allow_small_or_imprecise_dtypes": True}
-        op("g", [], [o], lambda: g.iota(o[0], pattern, base, cm, **kw))
+        op("g", [], [o], lambda: g.iota(o[0], pattern, base, cm, **kw), 130 + 1.8 * len(o[2]))
 
     def fill(o, c):
         iota(o, [[0, len(o[2])]], c)
 
-    def dma(q, sem, total, out, in_, reads, writes):
-        need(q, reads, writes)
-        Q[q].dma_start(out, in_).then_inc(T.sem[sem], 16)
-        mark(sem, total, reads, writes)
+    last_dma = {}
+
+    def dma(q, sem, total, out, in_, reads, writes, ns=2500):
+        last_dma[q] = op(q, reads, writes, lambda: Q[q].dma_start(out, in_).then_inc(T.sem[sem], 16), ns, (sem, total),
+                         [last_dma[q]] if q in last_dma else [], 60)
+
+    def emit():
+        if "order" not in _PLAN:
+            _PLAN["order"] = _plan(ops)
+        count, known, token = {}, {}, {}
+        for i in _PLAN["order"]:
+            q, deps, _, call, _, tok, _ = ops[i]
+            if q != "net":
+                w = {}
+                for d in deps:
+                    if not (q == "p" and ops[d][0] == "p"):
+                        w[token[d][0]] = max(w.get(token[d][0], 0), token[d][1])
+                for sem, val in w.items():
+                    if val > known.get((q, sem), 0):
+                        Q[q].wait_ge(T.sem[sem], val)
+                        known[(q, sem)] = val
+                r = call()
+                if tok is None:
+                    tok = (QS[q], count.get(QS[q], 0) + 1)
+                    r.then_inc(T.sem[tok[0]], 1)
+            token[i] = tok
+            count[tok[0]] = tok[1]
+        for sem, val in count.items():
+            g.wait_ge(T.sem[sem], val)
 
     CQ, CQ1, CQ4, CQ41, CG, CS16, CS4, CT4, CQ2, CP, CF16 = [A("pc", k, k + 1) for k in range(11)]
 
@@ -201,8 +283,8 @@ def rank_program(g, core, T, topo):
         scan(A("exb", k * n, k * n + n), row, A("kx", 0, n), -512.0, OP.max, OP.add)
 
     dma("y", "lu", 16, T.ut[:], T.u[:], [], [A("ut")])
-    dma("s", "lx", 32, T.x0[:, 0:2 * C], T.x[:, 0:2 * C], [], [A("x0", 0, 2 * C)])
-    dma("y", "lx", 32, T.x0[:, 2 * C:4 * C], T.x[:, 2 * C:4 * C], [], [A("x0", 2 * C, 4 * C)])
+    dma("s", "lx", 32, T.x0[:, 0:2 * C], T.x[:, 0:2 * C], [], [A("x0", 0, 2 * C)], 3500)
+    dma("y", "lx", 32, T.x0[:, 2 * C:4 * C], T.x[:, 2 * C:4 * C], [], [A("x0", 2 * C, 4 * C)], 3500)
     dma("y", "lw", 32, T.wq[:].bitcast(dt.uint8), T.wc[:], [], [A("wq")])
     dma("y", "lw", 32, T.wp[:], T.ws[:], [], [A("wp")])
     dma("y", "lv", 16, T.vt[:], T.v[:], [], [A("vt")])
@@ -213,9 +295,6 @@ def rank_program(g, core, T, topo):
     def tab(k):
         return A("tab", 16 * k, 16 * k + 16)
 
-    def zone(m):
-        fill(A("fl", 4 * (TO[m] + (400 if m == 6 else 64 * m + 16)), 4 * (TO[m] + TW[m])), 0)
-
     iota(pi(0), [[0, 1]], 0, 1)
     iota(tab(0), [[1, 16]])
     iota(A("cw"), [[16, NB]])
@@ -223,17 +302,15 @@ def rank_program(g, core, T, topo):
     iota(tab(1), [[0, 4], [1, 4]])
     iota(A("jw", 14, 42), [[8, NB]])
     iota(A("g64"), [[1, 8], [0, 64]])
-    zone(6)
-    zone(4)
     iota(A("seg"), [[0, NB], [64, 16]])
-    for m in (3, 5, 2, 1, 0):
-        zone(m)
+    for m in range(7):
+        fill(A("fl", 4 * (TO[m] + (400 if m == 6 else 64 * m + 16)), 4 * (TO[m] + TW[m])), 0)
     fill(A("ones"), 1)
     fill(A("win", 0, 4 * C), 0)
     iota(A("cnt"), [[1, C + L]])
     iota(A("k5"), [[0, 112], [256, 5]])
     fill(A("lh"), 0)
-    op("g", [A("ones")], [A("em")], lambda: g.affine_select(T.em[:], T.ones[:], [[-1, 528]], OP.is_equal, 0.0, 3, 4))
+    op("g", [A("ones")], [A("em")], lambda: g.affine_select(T.em[:], T.ones[:], [[-1, 528]], OP.is_equal, 0.0, 3, 4), 1100)
 
     memset(A("eqr", 0, 2), 0.0)
     memset(A("eqr", C, C + 2), 0.0)
@@ -280,8 +357,8 @@ def rank_program(g, core, T, topo):
     ts(CS4, CS4, 4.0 / F, OP.add)
     quant("u", A("ut"))
     op("v", [A("uq"), A("ulu")], [A("urq")], lambda: V.tensor_copy(
-        T.urq[:, 0:128].bitcast(dt.uint32), T.uq[:, 0:128].bitcast(dt.uint32).indirect(T.ulu[:, 0:8])))
-    op("v", [A("up"), A("ulu")], [A("urp")], lambda: V.tensor_copy(T.urp[:, 0:128], T.up[:, 0:128].indirect(T.ulu[:, 0:8])))
+        T.urq[:, 0:128].bitcast(dt.uint32), T.uq[:, 0:128].bitcast(dt.uint32).indirect(T.ulu[:, 0:8])), 240)
+    op("v", [A("up"), A("ulu")], [A("urp")], lambda: V.tensor_copy(T.urp[:, 0:128], T.up[:, 0:128].indirect(T.ulu[:, 0:8])), 240)
     ts(A("cpt"), A("g64"), CG, OP.is_equal, CP, OP.mult)
     ts(A("cst"), A("g64"), CG, OP.is_equal)
     ts(A("jw", 42, 70), A("cw"), CQ, OP.add)
@@ -296,6 +373,10 @@ def rank_program(g, core, T, topo):
     ts(A("jw", 84, 112), A("jw", 42, 70), -1.0, OP.mult, C - 1.0, OP.add)
     tt(tab(5), tab(5), tab(1), OP.max)
     cp(W(8, B0), A("jw", 84, 84 + B0))
+    act(A("k4"), tab(5), by=A("qo"))
+    quant("v", A("vt"))
+    for b in range(4):
+        quant2([A("eq4", 128 * b, 128 * b + 128), A("ep4", 128 * b, 128 * b + 128)], A("em", 3 - b, 515 - b))
 
     def slot(b):
         m = (b - 1) // 4
@@ -313,71 +394,38 @@ def rank_program(g, core, T, topo):
         sq, sp, sn, pw = "sq%d" % t, "sp%d" % t, "sn%d" % t, "pw%d" % t
         quant("x", A(xb))
         mm(bank(0, C), pair("ur"), pair("x"))
-        if t == 0:
-            mm(bank(3, C), pair("u"), pair("x"))
         mm(bank(1, C), pair("ur"), pair("x"))
         if t == 0:
-            act(A("sg", 0, C), bank(3, C), AF.Sign)
-            act(A("pf", 0, 4 * C, 4), A("sg", 0, C), AF.Relu)
+            mm(bank(3, C), pair("u"), pair("x"))
+            act(A("sg", 3200, 3200 + C), bank(3, C), AF.Sign)
+            act(A("pf", 0, 4 * C, 4), A("sg", 3200, 3200 + C), AF.Relu)
+            quant("pf", A("pf"))
+            mm(bank(4, C), pair("cp"), pair("pf"))
+            hold(bank(4, C), 0, C)
         else:
             act(A("ptr"), A("pw%d" % (t - 1)), by=A("nx1"))
             hold(A("ptr"), 0, C)
+        ts(A("poff"), A("exb", 15, C, 16), -float(C), OP.mult, float(C * (K - 1 - 256)), OP.add)
         tt(A("yy"), bank(0, C), A("cm"), OP.min)
         scan(A("hd"), A("ck"), A("yy"), 0.0, OP.min, OP.max)
-
-        def s_sign(b):
-            h = (b % 2) * C
-            act(A("sg", h, h + 16 * b), bank(1, 16 * b), AF.Sign, bias=A("hd", 16 * b + 15, 16 * b + 16), scale=-1.0)
-
-        def s_relu(b):
-            h = (b % 2) * C
-            act(A("fl", slot(b), slot(b) + 64 * b, 4), A("sg", h, h + 16 * b), AF.Relu, acc=A("rs", b, b + 1))
-
-        def v_cmp(b):
-            ts(A("fl", slot(b), slot(b) + 64 * b, 4), bank(0, 16 * b), A("hd", 16 * b + 15, 16 * b + 16), OP.is_lt)
-
-        def v_sum(b):
-            e = RS * (b - NV + 1)
-            scan(A("rsc", e - 8 * b, e), A("fl", slot(b), slot(b) + 32 * b, 4), A("fl", slot(b) + 32 * b, slot(b) + 64 * b, 4),
-                 -float(HALF), OP.add, OP.add)
-
-        s_sign(NV - 1)
         for b in range(NV - 1, 0, -1):
-            if b > 1:
-                s_sign(b - 1)
-            s_relu(b)
-        if t == 0:
-            act(A("k4"), tab(5), by=A("qo"))
+            h = A("sg", 8 * b * (b - 1), 8 * b * (b + 1))
+            act(h, bank(1, 16 * b), AF.Sign, bias=A("hd", 16 * b + 15, 16 * b + 16), scale=-1.0)
+            act(A("fl", slot(b), slot(b) + 64 * b, 4), h, AF.Relu, acc=A("rs", b, b + 1))
         act(A("xh"), A(xb), scale=0.5)
         diag = A("fl", 4 * TO[6], 4 * TO[6] + 4 * C, 4)
         tt(diag, bank(0, C), A("hd"), OP.is_le)
-        if t == 0:
-            quant("pf", A("pf"))
-            mm(bank(4, C), pair("cp"), pair("pf"))
-        v_cmp(NB - 1)
         scan(A("dsc"), A("seg"), diag, 0.0, OP.min, OP.add)
         for b in range(NB - 1, NV - 1, -1):
-            if b - 1 >= NV:
-                v_cmp(b - 1)
-            v_sum(b)
-            if b == 26 and t == 0:
-                hold(bank(4, C), 0, C)
-            if b == 25:
-                qtile(6)
-                ts(A("poff"), A("exb", 15, C, 16), -float(C), OP.mult, float(C * (K - 1 - 256)), OP.add)
-            if b == 24:
-                tt(A("base"), A("cw"), A("dsc", 15, C, 16), OP.subtract)
-            if b == 23:
-                tt(A("base"), A("base"), A("poff"), OP.add)
-            if b == 22:
-                qtile(3)
-            if b == 21:
-                qtile(5)
+            ts(A("fl", slot(b), slot(b) + 64 * b, 4), bank(0, 16 * b), A("hd", 16 * b + 15, 16 * b + 16), OP.is_lt)
+            e = RS * (b - NV + 1)
+            scan(A("rsc", e - 8 * b, e), A("fl", slot(b), slot(b) + 32 * b, 4), A("fl", slot(b) + 32 * b, slot(b) + 64 * b, 4),
+                 -float(HALF), OP.add, OP.add)
+        tt(A("base"), A("cw"), A("dsc", 15, C, 16), OP.subtract)
+        tt(A("base"), A("base"), A("poff"), OP.add)
         ts(A("rs", NV, NB), A("rsc", RS - 1, RS * (NB - NV), RS), float(HALF), OP.add)
-        qtile(4)
-        qtile(2)
-        qtile(1)
-        qtile(0)
+        for m in (6, 3, 5, 4, 2, 1, 0):
+            qtile(m)
         tt(A("base"), A("base"), A("rs"), OP.subtract)
         ts(A("base"), A("base"), CF16, OP.mult)
         keep16(bank(2, C), C)
@@ -394,15 +442,12 @@ def rank_program(g, core, T, topo):
         ts(A("ei", 0, k1), ends, 0.5, OP.mult, HALF + 1.0, OP.add)
         ts(A("ef", 0, k1), ends, 0.5, OP.mult, HALF + 1.0, OP.add)
         ts(A("ei", 8, 8 + k1), A("ei", 0, k1), 1, OP.arith_shift_right)
+        ts(A("ef", 24, 24 + k1), A("ei", 8, 8 + k1), -1.0, OP.mult, 0.5, OP.add)
+        cp(A("ef", 8, 8 + k1), A("ei", 8, 8 + k1))
+        ts(A("ef", 16, 16 + k1), A("ei", 8, 8 + k1), -float(HALF), OP.add)
         for k in range(k1):
             ts(A("lh", 420 + k, 560, 5), A("jw", 42, 70), A("ef", k, k + 1), OP.is_lt, float(k1 - k), OP.mult)
-            if k == 0:
-                ts(A("ef", 24, 24 + k1), A("ei", 8, 8 + k1), -1.0, OP.mult, 0.5, OP.add)
-                cp(A("ef", 8, 8 + k1), A("ei", 8, 8 + k1))
-                ts(A("ef", 16, 16 + k1), A("ei", 8, 8 + k1), -float(HALF), OP.add)
-        for k in range(k1):
             act(A("sgn", 42 * k, 42 * k + 42), A("jw", 0, 42), AF.Sign, bias=A("ef", 24 + k, 25 + k))
-        for k in range(k1):
             act(A("lh", k, 210, 5), A("sgn", 42 * k, 42 * k + 42), scale=A("ef", 8 + k, 9 + k))
             act(A("lh", 210 + k, 420, 5), A("sgn", 42 * k, 42 * k + 42), scale=A("ef", 16 + k, 17 + k))
         keep16(A("plr"), C)
@@ -421,57 +466,58 @@ def rank_program(g, core, T, topo):
         wrap4(A("abr", 0, HALF), HALF, A("ab4", 0, 2 * NB))
         lo_, hi_ = A("lo", 74, 210, 5), A("lo", 284, 420, 5)
         tt(W(2), A("jw", 42, 70), lo_, OP.subtract)
+        tt(W(3), lo_, hi_, OP.add)
+        tt(W(4), W(2), hi_, OP.add)
+        ts(W(4), W(4), float(HALF), OP.is_ge)
+        tt(W(4), W(4), W(3), OP.mult)
+        tt(W(7), W(4), W(2), OP.add)
+        cp(A("fw"), W(7))
         for k in range(4):
             act(A("bh", HALF * k, HALF * k + HALF), A("xh"), by=A("ab4", 2 * NB + 14 * k, 2 * NB + 14 * k + 14))
-        for k in range(4):
             tt(A("zt", HALF * k, HALF * k + HALF), A("xh"), A("bh", HALF * k, HALF * k + HALF), OP.add, by=A("ab4", 14 * k, 14 * k + 14))
-        act(A("ab", 0, 2 * C), A(xb), by=A("ab4", 0, 2 * NB))
+        for k in range(2):
+            act(A("ab", C * k, C * k + C), A(xb), by=A("ab4", NB * k, NB * k + NB))
+            act(A("ab", 2 * C + C * k, 3 * C + C * k), A("bh", C * k, C * k + C), scale=2.0)
         quant("z", A("zt"))
         for b in range(4):
             mm(bank(3 + b, HALF), pair("w", 128 * b, 128 * b + 128), pair("z"))
         tt(A("eqr", 1, C), A("clr", 1, C), A("clr", 0, C - 1), OP.is_equal)
-        ts(A("ht", 0, 2 * C, 4), bank(3, HALF), 0.03125, OP.mult)
-        ts(A("ht", 1, 2 * C, 4), bank(4, HALF), 0.03125, OP.mult)
-        for b in (2, 3):
-            act(A("ht", b, 2 * C, 4), bank(3 + b, HALF), scale=0.03125)
-        tt(W(3), lo_, hi_, OP.add)
-        tt(W(4), W(2), hi_, OP.add)
+        for b in range(2):
+            ts(A("ht", b, 2 * C, 4), bank(3 + b, HALF), 0.03125, OP.mult)
+            act(A("ht", 2 + b, 2 * C, 4), bank(5 + b, HALF), scale=0.03125)
         qh = [A("hq"), A(sp, L, L + HALF)]
         quant2(qh, A("ht"))
         mm(bank(7, HALF), pair("ur"), qh)
-        act(A("ab", 2 * C, 4 * C), A("bh"), scale=2.0)
-        ts(W(4), W(4), float(HALF), OP.is_ge)
-        tt(W(4), W(4), W(3), OP.mult)
-        tt(W(7), W(4), W(2), OP.add)
         ts(A("gr", 0, HALF), bank(7, HALF), 0.0, OP.is_gt)
-        cp(A("fw"), W(7))
         ts(A("gr", HALF, C), bank(7, HALF), 0.0, OP.is_le)
+        for k in range(2):
+            tt(A("xn", C * k, C * k + C), A("ab", C * k, C * k + C), A("ht", C * k, C * k + C), OP.add)
+            tt(A("xn", 2 * C + C * k, 3 * C + C * k), A("ab", 2 * C + C * k, 3 * C + C * k), A("ht", C * k, C * k + C), OP.subtract)
         act(A("gb"), A("gr"), AF.Identity, bias=1.0, scale=-1.0, by=A("fw"))
         act(A("lrg", 2 * C + P0, 3 * C), A("gb", P0, C), AF.Identity, bias=1.0, scale=-1.0)
         act(A("fr", P0, C), A("cnt", 0, C), by=A("fw", B0, NB))
-        tt(A("xn", 0, 2 * C), A("ab", 0, 2 * C), A("ht"), OP.add)
         scan(A("lrg", 0, C), A("eqr", 0, C), A("gb"), 0.0, OP.mult, OP.add)
         hold(A("lrg", P0, C), 0, C - P0)
         scan(A("lrg", 2 * C - 1, C + P0 - 1, -1), A("eqr", C, P0, -1), A("lrg", 3 * C - 1, 2 * C + P0 - 1, -1), 0.0, OP.mult, OP.add)
         hold(A("lrg", 2 * C + P0, 3 * C), 2, C - P0)
         hold(A("lrg", C + P0, 2 * C), 1, C - P0)
         w = NB - B0
-        ts(A("wf", 288, 288 + 3 * w), A("exb", 15, 3 * (C - P0), 16), 256.0, OP.add)
-        lg, rg, gm = [A("wf", 288 + w * k, 288 + w * k + w) for k in range(3)]
+        lg, rg, gm = [A("exb", 15 + (C - P0) * k, (C - P0) * (k + 1), 16) for k in range(3)]
         jl = A("wf", 256 + B0, 256 + NB)
-        tt(W(5, w), lg, rg, OP.add)
-        tt(W(6, w), A("jw", 84 + B0, 112), rg, OP.subtract)
-        tt(W(5, w), W(5, w), gm, OP.mult)
-        tt(jl, W(5, w), W(6, w), OP.add)
+        ts(W(9, w), gm, 256.0, OP.add)
+        ts(W(10, w), lg, 256.0, OP.add)
+        tt(W(10, w), W(10, w), W(9, w), OP.mult)
+        ts(W(11, w), gm, -1.0, OP.mult, -255.0, OP.add)
+        tt(W(10, w), W(10, w), A("jw", 84 + B0, 112), OP.add)
+        ts(W(5, w), rg, 256.0, OP.add)
+        tt(W(5, w), W(5, w), W(11, w), OP.mult)
+        tt(jl, W(10, w), W(5, w), OP.subtract)
         cp(A("jlw", 0, w), jl)
         scatter(A("lr"), A("jlw", 0, w), A("fr", P0, C))
-        scan(A("ex", 0, L), A("k4", 0, L), A("lr", 0, L), 0.0, OP.mult, OP.add)
-        tt(A("xn", 2 * C, 4 * C), A("ab", 2 * C, 4 * C), A("ht"), OP.subtract)
-        ts(A("l4"), A("ex", 3, L, 4), CS4, OP.mult, CT4, OP.add)
+        wrap4(A("lr", 0, L), L, A("l4"))
         act(A("st", 2 * L, 4 * L), A("xn", 0, 4 * C), by=A("l4", 16, 32))
         cp(A("st", 0, 2 * L), A("xn", 0, 4 * C), by=A("l4", 0, 16))
         quant2([A(sq), A(sp, 0, L)], A("st"))
-        need("g", [A(sq), A(sp)], [])
         tr = []
         for k in range(3):
             rid, pid = topo.addr(relays[k], core)
@@ -481,13 +527,13 @@ def rank_program(g, core, T, topo):
                 src, dst = T[sp][:, 0:2 * L], T["rp%d" % t][:, 0:2 * L]
             tr.append(RemoteDMATransfer(dst_ids=[DstId(rid=rid, pnc=pid)], dma_engine_mask=_mask(topo.engines(core, relays[k])[4 * k:4 * k + 4]),
                                         remote_sem=T.sem["hop%d" % t], src=src, dst=dst))
-        g.remote_dma_fused(tr, local_sem=T.sem.sent)
+        s1 = op("g", [A(sq), A(sp)], [], lambda tr=tr: g.remote_dma_fused(tr, local_sem=T.sem.sent), 300, ("sent", 16 * R))
         act(A("clp"), A("clr"), by=A("fiw"))
         tt(W(5), W(8), W(7), OP.subtract)
         ts(W(6), W(8), float(L), OP.is_lt)
-        keep16(A("lr", 0, L), L)
+        scan(A("ex", L, 2 * L), A("k16", 0, L), A("lr", 0, L), 0.0, OP.mult, OP.add)
         ts(W(5), W(5), float(C), OP.add)
-        read16(A("l1"), L)
+        ts(A("l1"), A("ex", L + 15, 2 * L, 16), CS16, OP.mult, -0.26, OP.add)
         tt(W(5), W(5), W(6), OP.mult)
         tt(W(5), W(5), W(7), OP.add)
         cp(A("m2w"), W(5))
@@ -495,20 +541,15 @@ def rank_program(g, core, T, topo):
         act(A("nxr"), A("abr"), by=A("plw"))
         tt(A(pw, 0, C), A("clp"), A("gr"), OP.add)
         cp(A(sn), A(pw, 0, C), by=A("l1"))
-        need("g", [A(sn)], [])
         rid, pid = topo.addr(relays[3], core)
-        g.remote_dma(T["rn%d" % t][:, 0:L], T[sn][:, 0:L], T.sem["hop%d" % t], T.sem.sent, pid, rid,
-                     _mask(topo.engines(core, relays[3])[12:16]))
-        if t == 0:
-            quant("v", A("vt"))
-            for b in range(4):
-                quant2([A("eq4", 128 * b, 128 * b + 128), A("ep4", 128 * b, 128 * b + 128)], A("em", 3 - b, 515 - b))
+        s2 = op("g", [A(sn)], [], lambda a=(T["rn%d" % t][:, 0:L], T[sn][:, 0:L], T.sem["hop%d" % t], T.sem.sent, pid, rid,
+                                            _mask(topo.engines(core, relays[3])[12:16])): g.remote_dma(*a), 300, ("sent", 16 * R), [s1])
         wrap4(A("nxr"), C, A("nx4"))
         keep16(A("nxr"), C)
         read16(A("nx1"), C)
         came = [A("aq%d" % t), A("ap%d" % t)]
-        mark("arc%d" % t, n_in[0] + n_in[1] + n_in[2], [], came)
-        mark("arp%d" % t, n_in[3], [], [A(pw, C, C + L)])
+        op("net", [A(sq)], came, None, 5000, ("arc%d" % t, n_in[0] + n_in[1] + n_in[2]), [s1], 0)
+        op("net", [A(sn)], [A(pw, C, C + L)], None, 5000, ("arp%d" % t, n_in[3]), [s2], 0)
         for b in (0, 2, 1, 3):
             mm(bank(3 + b, L), [A("eq4", 128 * b, 128 * b + 128), A("ep4", 128 * b, 128 * b + 128)], came)
         for b in range(2):
@@ -525,13 +566,9 @@ def rank_program(g, core, T, topo):
     act(A("plr"), A("pw%d" % (R - 1)), by=A("nx1"))
     cp(A("orow", 0, HALF), bank(0, HALF))
     act(A("orow", HALF, C), bank(1, HALF))
-    for k in range(2):
-        dma("y", "out", total, T.osc[4 * k:4 * k + 4, :], T.xp[32 * k:32 * k + 4, :], [A("xp")], [])
+    dma("s", "out", total, T.pts[:], T.plr[0:128:16, :], [A("plr")], [])
+    for k in range(4):
+        dma("s" if k == 3 else "y", "out", total, T.osc[4 * k:4 * k + 4, :], T.xp[32 * k:32 * k + 4, :], [A("xp")], [])
     dma("y", "out", total, T.y[:, 0:HALF], T.orow[:, 0:HALF], [A("orow", 0, HALF)], [])
     dma("s", "out", total, T.y[:, HALF:C], T.orow[:, HALF:C], [A("orow", HALF, C)], [])
-    dma("s", "out", total, T.pts[:], T.plr[0:128:16, :], [A("plr")], [])
-    for k in range(2, 4):
-        dma("s" if k % 2 else "y", "out", total, T.osc[4 * k:4 * k + 4, :], T.xp[32 * k:32 * k + 4, :], [A("xp")], [])
-    count["sent"] = 16 * R
-    for sem, val in count.items():
-        g.wait_ge(T.sem[sem], val)
+    emit()

@@ -39,8 +39,8 @@ SEMAPHORES = (["qv", "qs", "qp", "qg", "sent", "lu", "lx", "lw", "lv", "out"]
 OP = AluOpType
 AF = ActivationFunctionType
 _PLAN = {}
-WAKE = 80
-TRIES = 120
+WAKE = 180
+TRIES = 200
 
 
 def _schedule(ops, tol):
@@ -68,7 +68,7 @@ def _schedule(ops, tol):
     while len(order) < n:
         memo, pick, spare = {}, None, None
         for q, lst in todo.items():
-            can = [i for i in lst[:24] if all(d in end for d in before[i])]
+            can = [i for i in lst[:32] if all(d in end for d in before[i])]
             if not can:
                 continue
             top = lst[0]
@@ -94,7 +94,7 @@ def _plan(ops):
     for _ in range(TRIES):
         new = tol.copy()
         k = rng.integers(0, len(ops), 60)
-        new[k] = rng.choice([0.0, 60.0, 200.0, 500.0], 60)
+        new[k] = rng.choice([0.0, 40.0, 120.0, 300.0], 60)
         r = _schedule(ops, new)
         if r[0] <= best[0]:
             best, tol = r, new
@@ -149,8 +149,8 @@ def rank_program(g, core, T, topo):
         b = n if b is None else b
         return (T[name][:, a:b:s] if s != 1 else T[name][:, a:b], name, np.arange(n)[a:b:s])
 
-    def bank(k, n):
-        return (T.ps[:, 512 * k:512 * k + n], "ps", np.array([k]))
+    def bank(k, n, a=0):
+        return (T.ps[:, 512 * k + a:512 * k + n], "ps", np.array([k]))
 
     def op(q, reads, writes, call, ns, token=None, after=(), busy=None):
         reads = [x for x in reads if isinstance(x, tuple)]
@@ -184,16 +184,16 @@ def rank_program(g, core, T, topo):
 
     def ns_of(o, xs, by=None, k=1.0):
         if by:
-            return 60 + 1.4 * len(o[2])
+            return 60 + 1.3 * len(o[2])
         two = all(SCRATCH[x[1]][2] in (B2, U2) for x in [o] + xs)
-        return 60 + 0.9 * k * len(o[2]) * (0.5 if two else 1)
+        return 60 + 0.85 * k * len(o[2]) * (0.5 if two else 1)
 
     def memset(o, c):
         op("v", [], [o], lambda: V.memset(o[0], c), ns_of(o, []))
 
-    def ts(o, i, s1, op0, s2=None, op1=None):
+    def ts(o, i, s1, op0, s2=None, op1=None, by=None):
         more = () if op1 is None else (op1,)
-        op("v", [i, s1, s2], [o], lambda: V.tensor_scalar(o[0], i[0], raw(s1), raw(s2), op0, *more), ns_of(o, [i]))
+        op("v", [i, s1, s2, by], [o], lambda: V.tensor_scalar(o[0], ind(i, by), raw(s1), raw(s2), op0, *more), ns_of(o, [i], by))
 
     def tt(o, a, b, o_, by=None):
         op("v", [a, b, by], [o], lambda: V.tensor_tensor(o[0], ind(a, by), b[0], o_), ns_of(o, [a, b], by, 1 if a[1] == "ps" else 2))
@@ -202,7 +202,7 @@ def rank_program(g, core, T, topo):
         op("v", [i, by], [o], lambda: V.tensor_copy(o[0], ind(i, by)), ns_of(o, [i], by))
 
     def scatter(win, by, i):
-        op("v", [i, by], [win], lambda: V.tensor_copy(ind(win, by), i[0]), 60 + 3.2 * len(i[2]))
+        op("v", [i, by], [win], lambda: V.tensor_copy(ind(win, by), i[0]), 60 + 3.0 * len(i[2]))
 
     def scan(o, d0, d1, init, op0, op1):
         op("v", [d0, d1], [o], lambda: V.tensor_tensor_scan(o[0], d0[0], d1[0], init, op0, op1), ns_of(o, [d0, d1]))
@@ -213,10 +213,10 @@ def rank_program(g, core, T, topo):
             kw["bias"] = raw(bias)
         if acc:
             kw["accum_out"] = acc[0]
-        op("s", [i, bias, scale, by], [o, acc], lambda: S.activation(o[0], ind(i, by), f, **kw), 75 + (1.4 if by else 0.9) * len(o[2]))
+        op("s", [i, bias, scale, by], [o, acc], lambda: S.activation(o[0], ind(i, by), f, **kw), 75 + (1.3 if by else 0.85) * len(o[2]))
 
     def quant2(p, i):
-        op("v", [i], p, lambda: V.quantize_mx(p[0][0], p[1][0], i[0]), 15 + 0.25 * len(i[2]))
+        op("v", [i], p, lambda: V.quantize_mx(p[0][0], p[1][0], i[0]), 15 + 0.24 * len(i[2]))
 
     def pair(n, a=0, b=None):
         return [A(n + "q", a, b), A(n + "p", a, b)]
@@ -265,15 +265,16 @@ def rank_program(g, core, T, topo):
             g.wait_ge(T.sem[sem], val)
 
     CQ, CQ1, CQ4, CQ41, CG, CS16, CS4, CT4, CQ2, CP, CF16 = [A("pc", k, k + 1) for k in range(11)]
+    HALVES = ((0, HALF), (HALF, C))
 
     def W(k, n=NB):
         return A("wf", 32 * k, 32 * k + n)
 
-    def keep16(row, n):
-        scan(A("ex", 0, n), A("k16", 0, n), row, 0.0, OP.mult, OP.add)
+    def keep16(row, a, b):
+        scan(A("ex", a, b), A("k16", a, b), row, 0.0, OP.mult, OP.add)
 
-    def read16(dst, n):
-        ts(dst, A("ex", 15, n, 16), CS16, OP.mult, -0.26, OP.add)
+    def read16(dst, a, b):
+        ts(dst, A("ex", a + 15, b, 16), CS16, OP.mult, -0.26, OP.add)
 
     def wrap4(row, n, dst, a=0):
         scan(A("ex", a, a + n), A("k4", 0, n), row, 0.0, OP.mult, OP.add)
@@ -406,16 +407,19 @@ def rank_program(g, core, T, topo):
             act(A("ptr"), A("pw%d" % (t - 1)), by=A("nx1"))
             hold(A("ptr"), 0, C)
         ts(A("poff"), A("exb", 15, C, 16), -float(C), OP.mult, float(C * (K - 1 - 256)), OP.add)
-        tt(A("yy"), bank(0, C), A("cm"), OP.min)
-        scan(A("hd"), A("ck"), A("yy"), 0.0, OP.min, OP.max)
+        for a, b in HALVES:
+            tt(A("yy", a, b), bank(0, b, a), A("cm", a, b), OP.min)
+            scan(A("hd", a, b), A("ck", a, b), A("yy", a, b), 0.0, OP.min, OP.max)
         for b in range(NV - 1, 0, -1):
             h = A("sg", 8 * b * (b - 1), 8 * b * (b + 1))
             act(h, bank(1, 16 * b), AF.Sign, bias=A("hd", 16 * b + 15, 16 * b + 16), scale=-1.0)
             act(A("fl", slot(b), slot(b) + 64 * b, 4), h, AF.Relu, acc=A("rs", b, b + 1))
-        act(A("xh"), A(xb), scale=0.5)
-        diag = A("fl", 4 * TO[6], 4 * TO[6] + 4 * C, 4)
-        tt(diag, bank(0, C), A("hd"), OP.is_le)
-        scan(A("dsc"), A("seg"), diag, 0.0, OP.min, OP.add)
+        for a, b in HALVES:
+            act(A("xh", 4 * a, 4 * b), A(xb, 4 * a, 4 * b), scale=0.5)
+        for a, b in HALVES:
+            diag = A("fl", 4 * (TO[6] + a), 4 * (TO[6] + b), 4)
+            tt(diag, bank(0, b, a), A("hd", a, b), OP.is_le)
+            scan(A("dsc", a, b), A("seg", a, b), diag, 0.0, OP.min, OP.add)
         for b in range(NB - 1, NV - 1, -1):
             ts(A("fl", slot(b), slot(b) + 64 * b, 4), bank(0, 16 * b), A("hd", 16 * b + 15, 16 * b + 16), OP.is_lt)
             e = RS * (b - NV + 1)
@@ -428,13 +432,15 @@ def rank_program(g, core, T, topo):
             qtile(m)
         tt(A("base"), A("base"), A("rs"), OP.subtract)
         ts(A("base"), A("base"), CF16, OP.mult)
-        keep16(bank(2, C), C)
-        tt(W(0), A("ex", 15, C, 16), A("base"), OP.add)
-        ts(A("o1"), W(0), CS16, OP.mult, -0.26, OP.add)
+        for a, b in HALVES:
+            keep16(bank(2, b, a), a, b)
+            tt(A("wf", a // 16, b // 16), A("ex", a + 15, b, 16), A("base", a // 16, b // 16), OP.add)
+            ts(A("o1", a // 16, b // 16), A("wf", a // 16, b // 16), CS16, OP.mult, -0.26, OP.add)
         n = K * C
         scatter(A("win", 0, n), A("o1"), A("ones", 0, C))
         scan(A("so", 0, n), A("win", 0, n), A("win", 0, n), -C - 2.0, OP.add, OP.add)
-        act(A("plr"), A("so", 0, n), AF.Identity, bias=float(HALF), scale=0.5, by=A("o1"))
+        act(A("plr", HALF, C), A("so", 0, n), AF.Identity, bias=float(HALF), scale=0.5, by=A("o1", 14, NB))
+        ts(A("plr", 0, HALF), A("so", 0, n), 0.5, OP.mult, float(HALF), OP.add, A("o1", 0, 14))
         if t + 1 < R:
             fill(A("win", 0, n + C), 0)
         ends = A("so", C - 1, C * (K - 1), C)
@@ -450,18 +456,21 @@ def rank_program(g, core, T, topo):
             act(A("sgn", 42 * k, 42 * k + 42), A("jw", 0, 42), AF.Sign, bias=A("ef", 24 + k, 25 + k))
             act(A("lh", k, 210, 5), A("sgn", 42 * k, 42 * k + 42), scale=A("ef", 8 + k, 9 + k))
             act(A("lh", 210 + k, 420, 5), A("sgn", 42 * k, 42 * k + 42), scale=A("ef", 16 + k, 17 + k))
-        keep16(A("plr"), C)
+        for a, b in HALVES:
+            keep16(A("plr", a, b), a, b)
+            read16(A("plw", a // 16, b // 16), a, b)
         scan(A("lo", 420, 560), A("k5", 420, 560), A("lh", 420, 560), 0.0, OP.min, OP.max)
-        read16(A("plw"), C)
         cp(A("clw"), A("lo", 424, 560, 5))
         scatter(A("orow"), A("plw"), A("cnt", 0, C))
         act(A("clr"), A("cnt", 0, 16), by=A("clw"))
-        scan(A("lo", 0, 420), A("k5", 0, 420), A("lh", 0, 420), 0.0, OP.min, OP.max)
+        scan(A("lo", 210, 420), A("k5", 210, 420), A("lh", 210, 420), 0.0, OP.min, OP.max)
+        scan(A("lo", 0, 210), A("k5", 0, 210), A("lh", 0, 210), 0.0, OP.min, OP.max)
         tt(A("wf", 46, 60), A("jw", 70, 84), A("lo", 214, 280, 5), OP.subtract)
         tt(A("wf", 32, 46), A("jw", 0, 14), A("lo", 4, 70, 5), OP.add)
-        cp(A("fiw"), W(1))
-        act(A("abr", HALF, C), A("orow"), by=A("fiw", 14, 28))
-        cp(A("abr", 0, HALF), A("orow"), by=A("fiw", 0, 14))
+        cp(A("fiw", 14, NB), A("wf", 46, 60))
+        cp(A("fiw", 0, 14), A("wf", 32, 46))
+        cp(A("abr", HALF, C), A("orow"), by=A("fiw", 14, NB))
+        act(A("abr", 0, HALF), A("orow"), by=A("fiw", 0, 14))
         wrap4(A("abr", HALF, C), HALF, A("ab4", 2 * NB, 4 * NB), HALF)
         wrap4(A("abr", 0, HALF), HALF, A("ab4", 0, 2 * NB))
         lo_, hi_ = A("lo", 74, 210, 5), A("lo", 284, 420, 5)
@@ -481,7 +490,8 @@ def rank_program(g, core, T, topo):
         quant("z", A("zt"))
         for b in range(4):
             mm(bank(3 + b, HALF), pair("w", 128 * b, 128 * b + 128), pair("z"))
-        tt(A("eqr", 1, C), A("clr", 1, C), A("clr", 0, C - 1), OP.is_equal)
+        for a in range(1, C, 149):
+            tt(A("eqr", a, a + 149), A("clr", a, a + 149), A("clr", a - 1, a + 148), OP.is_equal)
         for b in range(2):
             ts(A("ht", b, 2 * C, 4), bank(3 + b, HALF), 0.03125, OP.mult)
             act(A("ht", 2 + b, 2 * C, 4), bank(5 + b, HALF), scale=0.03125)
@@ -490,33 +500,36 @@ def rank_program(g, core, T, topo):
         mm(bank(7, HALF), pair("ur"), qh)
         ts(A("gr", 0, HALF), bank(7, HALF), 0.0, OP.is_gt)
         ts(A("gr", HALF, C), bank(7, HALF), 0.0, OP.is_le)
-        for k in range(2):
-            tt(A("xn", C * k, C * k + C), A("ab", C * k, C * k + C), A("ht", C * k, C * k + C), OP.add)
-            tt(A("xn", 2 * C + C * k, 3 * C + C * k), A("ab", 2 * C + C * k, 3 * C + C * k), A("ht", C * k, C * k + C), OP.subtract)
-        act(A("gb"), A("gr"), AF.Identity, bias=1.0, scale=-1.0, by=A("fw"))
+        for a in range(0, 2 * C, L):
+            tt(A("xn", a, a + L), A("ab", a, a + L), A("ht", a, a + L), OP.add)
+            tt(A("xn", 2 * C + a, 2 * C + a + L), A("ab", 2 * C + a, 2 * C + a + L), A("ht", a, a + L), OP.subtract)
+        act(A("gb", HALF, C), A("gr"), AF.Identity, bias=1.0, scale=-1.0, by=A("fw", 14, NB))
+        ts(A("gb", 0, HALF), A("gr"), -1.0, OP.mult, 1.0, OP.add, A("fw", 0, 14))
         act(A("lrg", 2 * C + P0, 3 * C), A("gb", P0, C), AF.Identity, bias=1.0, scale=-1.0)
         act(A("fr", P0, C), A("cnt", 0, C), by=A("fw", B0, NB))
         scan(A("lrg", 0, C), A("eqr", 0, C), A("gb"), 0.0, OP.mult, OP.add)
         hold(A("lrg", P0, C), 0, C - P0)
         scan(A("lrg", 2 * C - 1, C + P0 - 1, -1), A("eqr", C, P0, -1), A("lrg", 3 * C - 1, 2 * C + P0 - 1, -1), 0.0, OP.mult, OP.add)
-        hold(A("lrg", 2 * C + P0, 3 * C), 2, C - P0)
+        hold(A("gb", P0, C), 2, C - P0)
         hold(A("lrg", C + P0, 2 * C), 1, C - P0)
         w = NB - B0
-        lg, rg, gm = [A("exb", 15 + (C - P0) * k, (C - P0) * (k + 1), 16) for k in range(3)]
+        lg, rg, lost = [A("exb", 15 + (C - P0) * k, (C - P0) * (k + 1), 16) for k in range(3)]
         jl = A("wf", 256 + B0, 256 + NB)
-        ts(W(9, w), gm, 256.0, OP.add)
+        ts(W(9, w), lost, -1.0, OP.mult, -255.0, OP.add)
+        ts(W(11, w), lost, 256.0, OP.add)
+        ts(W(6, w), lost, 256.0, OP.add, -256.0, OP.mult)
         ts(W(10, w), lg, 256.0, OP.add)
+        tt(W(6, w), W(6, w), A("jw", 84 + B0, 112), OP.add)
         tt(W(10, w), W(10, w), W(9, w), OP.mult)
-        ts(W(11, w), gm, -1.0, OP.mult, -255.0, OP.add)
-        tt(W(10, w), W(10, w), A("jw", 84 + B0, 112), OP.add)
-        ts(W(5, w), rg, 256.0, OP.add)
-        tt(W(5, w), W(5, w), W(11, w), OP.mult)
-        tt(jl, W(10, w), W(5, w), OP.subtract)
+        tt(W(5, w), rg, W(11, w), OP.mult)
+        tt(W(5, w), W(6, w), W(5, w), OP.subtract)
+        tt(jl, W(10, w), W(5, w), OP.add)
         cp(A("jlw", 0, w), jl)
         scatter(A("lr"), A("jlw", 0, w), A("fr", P0, C))
-        wrap4(A("lr", 0, L), L, A("l4"))
-        act(A("st", 2 * L, 4 * L), A("xn", 0, 4 * C), by=A("l4", 16, 32))
-        cp(A("st", 0, 2 * L), A("xn", 0, 4 * C), by=A("l4", 0, 16))
+        for k in range(2):
+            wrap4(A("lr", 64 * k, 64 * k + 64), 64, A("l4", 16 * k, 16 * k + 16), 64 * k)
+        act(A("st", 0, 2 * L), A("xn", 0, 4 * C), by=A("l4", 0, 16))
+        cp(A("st", 2 * L, 4 * L), A("xn", 0, 4 * C), by=A("l4", 16, 32))
         quant2([A(sq), A(sp, 0, L)], A("st"))
         tr = []
         for k in range(3):
@@ -531,25 +544,26 @@ def rank_program(g, core, T, topo):
         act(A("clp"), A("clr"), by=A("fiw"))
         tt(W(5), W(8), W(7), OP.subtract)
         ts(W(6), W(8), float(L), OP.is_lt)
-        scan(A("ex", L, 2 * L), A("k16", 0, L), A("lr", 0, L), 0.0, OP.mult, OP.add)
+        keep16(A("lr", 0, L), L, 2 * L)
         ts(W(5), W(5), float(C), OP.add)
-        ts(A("l1"), A("ex", L + 15, 2 * L, 16), CS16, OP.mult, -0.26, OP.add)
+        read16(A("l1"), L, 2 * L)
         tt(W(5), W(5), W(6), OP.mult)
         tt(W(5), W(5), W(7), OP.add)
         cp(A("m2w"), W(5))
         act(A("abr"), A("cnt"), by=A("m2w"))
         act(A("nxr"), A("abr"), by=A("plw"))
-        tt(A(pw, 0, C), A("clp"), A("gr"), OP.add)
+        for a in range(0, C, 112):
+            tt(A(pw, a, a + 112), A("clp", a, a + 112), A("gr", a, a + 112), OP.add)
         cp(A(sn), A(pw, 0, C), by=A("l1"))
         rid, pid = topo.addr(relays[3], core)
         s2 = op("g", [A(sn)], [], lambda a=(T["rn%d" % t][:, 0:L], T[sn][:, 0:L], T.sem["hop%d" % t], T.sem.sent, pid, rid,
                                             _mask(topo.engines(core, relays[3])[12:16])): g.remote_dma(*a), 300, ("sent", 16 * R), [s1])
         wrap4(A("nxr"), C, A("nx4"))
-        keep16(A("nxr"), C)
-        read16(A("nx1"), C)
+        keep16(A("nxr"), 0, C)
+        read16(A("nx1"), 0, C)
         came = [A("aq%d" % t), A("ap%d" % t)]
-        op("net", [A(sq)], came, None, 5000, ("arc%d" % t, n_in[0] + n_in[1] + n_in[2]), [s1], 0)
-        op("net", [A(sn)], [A(pw, C, C + L)], None, 5000, ("arp%d" % t, n_in[3]), [s2], 0)
+        op("net", [A(sq)], came, None, 4500, ("arc%d" % t, n_in[0] + n_in[1] + n_in[2]), [s1], 0)
+        op("net", [A(sn)], [A(pw, C, C + L)], None, 4500, ("arp%d" % t, n_in[3]), [s2], 0)
         for b in (0, 2, 1, 3):
             mm(bank(3 + b, L), [A("eq4", 128 * b, 128 * b + 128), A("ep4", 128 * b, 128 * b + 128)], came)
         for b in range(2):

@@ -1,109 +1,184 @@
 import numpy as np
 from concourse.bass import DstId, RemoteDMATransfer
-from concourse.mybir import dt, AluOpType, ActivationFunctionType
+from concourse.mybir import dt, AluOpType, ActivationFunctionType, AxisListType
 
 C, L, R = 448, 128, 3
 HALF = C // 2
 NB = C // 16
-NVS = (20, 19, 19)
+NV = 20
+LOW = 16 * NV
 B0 = (C - HALF - L) // 16
 P0 = 16 * B0
+XV_ = 192
 BIG = 2.0 ** 80
-F = 2.0 ** 14
-TW = [128] + [64 * (m + 1) for m in range(1, 7)]
-TO = [sum(TW[:m]) for m in range(7)]
-RS = 8 * (NB - 1)
+F = 2.0 ** 21
+LN = 6
 X4, B2, F4, I4, U2, U1 = "float8_e4m3fn_x4", "bfloat16", "float32", "int32", "uint16", "uint8"
 
+TILES = []
+_a = 0
+for _kind, _all in (("d", list(range(NV))), ("b", list(range(NB - 1, NV - 1, -1)))):
+    for _m in range(0, len(_all), 4):
+        _l = _all[_m:_m + 4]
+        _hi = (C if _m == 0 else LOW) if _kind == "d" else 16 * _l[0]
+        _lo = min(16 * _l[0], _hi - 128) if _kind == "d" else 0
+        TILES.append([_kind, _l, _lo, _hi, _a, 0])
+        _a += _hi - _lo
+FLW = _a
+ND = (NV + 3) // 4
+PAD = 64
+FLQ = 0
+for _m in list(range(ND - 1, -1, -1)) + list(range(ND, len(TILES))):
+    TILES[_m][5] = FLQ
+    FLQ += TILES[_m][3] + (PAD if _m == ND - 1 else 0)
+SUMS = (4, 3, 0, 1, 5, 2, 6)
+LAST_D = [TILES[_m][1][-1] for _m in SUMS if TILES[_m][0] == "d"][-1]
+SG = sum(16 * b for b in range(NV, NB))
+
 _S = {
-    B2: dict(x0=4 * C, xs=4 * C, xh=4 * C, ut=512, vt=512, em=528, ones=528, cst=512, cpt=512, g64=512, pf=4 * C, fl=4 * sum(TW),
-             cm=C, ck=C, k16=C, k4=C, kx=C, seg=C, k5=560, sg=3200 + C, rsc=RS * 9, sgn=256, dsc=C, exb=3 * C, win=6 * C, so=6 * C,
-             clr=C, clp=C, eqr=C + 16, lh=560, lo=560, bh=2 * C, ab=4 * C, zt=2 * C, ht=2 * C, xn=4 * (C + L), gr=C, gb=C,
-             lrg=3 * C, st=4 * L, ptr=C),
-    F4: dict(pc=16, tab=128, cnt=C + L, jw=112, cw=NB, yy=C, hd=C, rs=NB, poff=NB, base=NB, wf=384, ex=C, ef=32,
-             plr=C, orow=C, abr=C, fr=C, lr=C, nxr=C),
+    B2: dict(x0=4 * C, xs=4 * C, xh=4 * C, ut=512, vt=512, em=528, ones=528, cst=512, cpt=512, pf=512, fl=4 * FLW, zz=4 * 256,
+             cm=C, ck=C, k16=C, k4=C, kx=C, kr=C, kb=LOW, k5=420, k6=LN * NB, k6n=LN * NB, sg=SG + C, sgn=256, sge=256, exb=2 * C, exh=C,
+             win=6 * C, so=6 * C, cne=C, eqr=C, lh=420, lo=420, bh=2 * C, bb=2 * C, zt=2 * C, ht=2 * C, xn=4 * (C + L), gt=C + 16,
+             gb=C, la=C, st=4 * L, ptr=C, plr=C, orow=C, abr=C, fr=C, lr=C, el=LN * NB, eo=LN * NB, tl=LN * NB, to=LN * NB,
+             ttr=C, ptp=C),
+    F4: dict(pc=16, tab=224, g32=32, ex0=C // 4, cnt=C + L, jw=112, cw=NB, ky=C, yy=C, hd=C, hx=LOW, rs=NB, poff=NB, base=NB, wf=512, ex=C, xr=C, ev=16, vec=256,
+             nl=LN * NB, no=LN * NB, m2r=C, nxr=C, pout=C, yo=C),
     I4: dict(pi=16, ei=16),
-    U2: dict(ulu=8, qo=NB, o1=NB, plw=NB, fiw=NB, fw=NB, clw=NB, jlw=NB, m2w=NB, nx1=NB, ab4=4 * NB, nx4=4 * NB, l4=32, l1=8),
-    X4: dict(wq=512, uq=128, urq=128, vq=128, xq=C, eq4=512, csq=128, cpq=128, pfq=C, flq=sum(TW), zq=HALF, hq=HALF),
-    U1: dict(wp=512, up=128, urp=128, vp=128, xp=C, ep4=512, csp=128, cpp=128, pfp=C, flp=sum(TW), zp=HALF),
+    U2: dict(ulu=8, go=32, qo=NB, o1=NB, plw=NB, fiw=NB, fw=NB, jlw=NB, m2w=NB, eqw=NB, ttw=NB, ab4=4 * NB, nx4=4 * NB, l4=32, xi=2),
+    X4: dict(wq=512, uq=128, urq=128, vq=128, xq=C, eq4=512, csq=128, cpq=128, pfq=128, flq=FLQ, zq=HALF, hq=HALF),
+    U1: dict(wp=512, up=128, urp=128, vp=128, xp=C, ep4=512, csp=128, cpp=128, pfp=128, flp=FLQ),
 }
 for _t in range(R):
     _S[X4].update({"sq%d" % _t: L, "rq%d" % _t: L, "aq%d" % _t: L})
-    _S[U1].update({"sp%d" % _t: L + HALF, "rp%d" % _t: 2 * L, "ap%d" % _t: L})
-    _S[B2].update({"sn%d" % _t: L, "rn%d" % _t: L, "pw%d" % _t: C + L})
+    _S[U1].update({"sp%d" % _t: L + C, "rp%d" % _t: 4 * L, "ap%d" % _t: L})
+    _S[F4].update({"sn%d" % _t: 8, "rn%d" % _t: 8, "an%d" % _t: 8})
+PART = {}
+for _d, _b, _names in ((B2, "lanes", "k6 k6n el eo tl to sgn sge k5 lh lo"), (B2, "rows", "ttr ptp ptr"), (F4, "lanef", "nl no"),
+                       (U2, "lists", "o1 plw fiw fw jlw m2w eqw ttw xi")):
+    _o = 0
+    for _n in _names.split():
+        PART[_n] = (_b, _o, _S[_d].pop(_n))
+        _o += PART[_n][2]
+    _S[_d][_b] = _o
 SCRATCH = {n: ("sbuf", [128, w], d) for d in _S for n, w in _S[d].items()}
 SCRATCH["ps"] = ("psum", [128, 4096], F4)
-SEMAPHORES = (["qv", "qs", "qp", "qg", "sent", "lu", "lx", "lw", "lv", "out"]
-              + ["%s%d" % (n, t) for t in range(R) for n in ("hop", "arc", "arp")])
+SEMAPHORES = (["qv", "qs", "qp", "qg", "sent", "lu", "lx", "lw", "lv", "lz", "lf", "out", "acc"]
+              + ["%s%d" % (n, t) for t in range(R) for n in ("hop", "arc", "arn")])
 
 OP = AluOpType
 AF = ActivationFunctionType
 _PLAN = {}
-WAKE = 180
-TRIES = 200
+WAKE = 150
+SWEEPS, SPAN, TRIES, SOFT = 6, 100, 800, 30.0
+FIRST = "zz0 cm0 ck0 em0 urq0 xq0 go0 urp0 cst0 cpt0 k40 kb0 flq320 eq40 eq4128 eq4256 eq4384 pf0".split()
+STEPS = (-40.0, -12.0, -4.0, 4.0, 12.0, 40.0)
 
 
-def _schedule(ops, tol):
-    n = len(ops)
-    before = [o[1] + o[2] for o in ops]
-    prio = [0.0] * n
-    for i in range(n - 1, -1, -1):
-        prio[i] += ops[i][4]
-        for d in before[i]:
-            prio[d] = max(prio[d], prio[i] + WAKE)
-    todo = {}
-    for i in sorted(range(n), key=lambda k: -prio[k]):
-        todo.setdefault(ops[i][0], []).append(i)
-    end, free, order = {}, {q: 0.0 for q in todo}, []
-
-    def ready(i, memo):
-        if i not in memo:
-            r = free[ops[i][0]]
-            for d in ops[i][1]:
-                e = end[d] if d in end else ready(d, memo) + ops[d][4]
-                r = max(r, e + (0 if ops[i][0] == ops[d][0] == "p" else WAKE))
-            memo[i] = r
-        return memo[i]
-
-    while len(order) < n:
-        memo, pick, spare = {}, None, None
-        for q, lst in todo.items():
-            can = [i for i in lst[:32] if all(d in end for d in before[i])]
-            if not can:
-                continue
-            top = lst[0]
-            fit = [i for i in can if i == top or ready(i, memo) + ops[i][6] <= ready(top, memo) + tol[i]]
-            if fit:
-                i = min(fit, key=lambda k: (ready(k, memo), -prio[k]))
-                if pick is None or ready(i, memo) < ready(pick, memo):
-                    pick = i
-            if spare is None or prio[can[0]] > prio[spare]:
-                spare = can[0]
-        i = spare if pick is None else pick
-        r = ready(i, memo)
-        end[i], free[ops[i][0]] = r + ops[i][4], r + ops[i][6]
-        todo[ops[i][0]].remove(i)
-        order.append(i)
-    return max(end.values()), order
+def _place(ops, order, edges, start=None, free={}):
+    start, slots = list(start or [0.0] * len(ops)), {q: ([-1.0], [t]) for q, t in free.items()}
+    for i in order:
+        t = 0.0
+        for d, lag in edges[i]:
+            if start[d] + lag > t:
+                t = start[d] + lag
+        busy = ops[i][6]
+        if busy:
+            a, b = slots.setdefault(ops[i][0], ([], []))
+            lo, k = 0, len(b)
+            while lo < k:
+                m = (lo + k) // 2
+                if b[m] > t:
+                    k = m
+                else:
+                    lo = m + 1
+            while k < len(a) and a[k] < t + busy:
+                t = max(t, b[k])
+                k += 1
+            a.insert(k, t)
+            b.insert(k, t + busy)
+        start[i] = t
+    return start
 
 
 def _plan(ops):
+    n = len(ops)
+    fwd, bwd = [[] for _ in ops], [[] for _ in ops]
+    for i, o in enumerate(ops):
+        for d in o[1]:
+            w = 0 if o[0] == ops[d][0] == "p" else WAKE
+            fwd[i].append((d, ops[d][4] + w))
+            bwd[d].append((i, o[4] + w))
+        for d in o[2]:
+            fwd[i].append((d, ops[d][6]))
+            bwd[d].append((i, o[4] - ops[d][4] + ops[d][6]))
+    ns = np.array([o[4] for o in ops], float)
+
+    lag = {(d, i): w for i in range(n) for d, w in sorted(fwd[i])}
+
+    def moved(key, i, by, inside):
+        key, todo = key.copy(), [i]
+        key[i] += by
+        while todo:
+            j = todo.pop()
+            for d, _ in (fwd if by < 0 else bwd)[j]:
+                if (inside is None or d in inside) and (key[d] - key[j]) * by <= 0:
+                    key[d] = key[j] + (1e-3 if by > 0 else -1e-3)
+                    todo.append(d)
+        return key
+
     rng = np.random.default_rng(1)
-    tol = np.full(len(ops), 60.0)
-    best = _schedule(ops, tol)
-    for _ in range(TRIES):
-        new = tol.copy()
-        k = rng.integers(0, len(ops), 60)
-        new[k] = rng.choice([0.0, 40.0, 120.0, 300.0], 60)
-        r = _schedule(ops, new)
-        if r[0] <= best[0]:
-            best, tol = r, new
-    return best[1]
+    key = -(np.array(_place([o[:6] + (0,) for o in ops], range(n - 1, -1, -1), bwd)) + ns)
+    key = (key + 1e-4 * np.arange(n)).tolist()
+    for k, name in enumerate(FIRST):
+        i = [o[7] for o in ops].index(name)
+        key = moved(key, i, min(0.0, k - 1e7 - key[i]), None)
+    order = np.argsort(key, kind="stable").tolist()
+    start = _place(ops, order, fwd)
+    for sweep in range(SWEEPS):
+        for p0 in range((sweep % 2) * SPAN // 4, n, SPAN // 2):
+            rank = {i: k for k, i in enumerate(order)}
+            order.sort(key=lambda i: (start[i], rank[i]))
+            end = max(start[i] + ops[i][4] for i in order)
+            win, latest, nxt = order[p0:p0 + SPAN], {}, {}
+            inside = set(win)
+            for i in reversed(order[p0:]):
+                t = end - ops[i][4]
+                for u, _ in bwd[i]:
+                    if u not in inside:
+                        t = min(t, latest[u] - lag[i, u])
+                if ops[i][6]:
+                    t = min(t, nxt.get(ops[i][0], 1e18) - ops[i][6])
+                    if i not in inside:
+                        nxt[ops[i][0]] = t
+                latest[i] = t
+            free = {}
+            for i in order[:p0]:
+                free[ops[i][0]] = max(free.get(ops[i][0], 0.0), start[i] + ops[i][6])
+            last = np.array([latest[i] for i in win])
+
+            def run(key):
+                new = _place(ops, sorted(win, key=key.get), fwd, start, free)
+                return float(np.exp((np.array([new[i] for i in win]) - last) / SOFT).sum())
+
+            key = {i: float(k) for k, i in enumerate(win)}
+            best = run(key)
+            for _ in range(TRIES):
+                new = moved(key, win[int(rng.integers(len(win)))], float(rng.choice(STEPS)) * (0.1 + rng.random()), inside)
+                r = run(new)
+                if r <= best:
+                    best, key = r, new
+            trial = order[:p0] + sorted(win, key=key.get) + order[p0 + SPAN:]
+            new = _place(ops, trial, fwd)
+            if max(new[i] + ops[i][4] for i in order) <= end:
+                order, start = trial, new
+    _PLAN["ns"] = max(start[i] + ops[i][4] for i in order)
+    rank = {i: k for k, i in enumerate(order)}
+    return sorted(order, key=lambda i: (start[i], rank[i]))
 
 
 def _relays(rank_core, nxt, topo):
     c = [k for k in topo.cores_of(rank_core) if k != rank_core and topo.may_write(k, nxt)]
-    return sorted(c, key=lambda k: topo.die(k) != topo.die(rank_core))[:4]
+    return sorted(c, key=lambda k: topo.die(k) != topo.die(rank_core))[:3]
 
 
 def _mask(engs):
@@ -114,14 +189,13 @@ def hand_on(g, core, T, topo, nxt, k):
     rid, pid = topo.addr(nxt, core)
     m = topo.mask(core, nxt)
     for t in range(R):
-        g.wait_ge(T.sem["hop%d" % t], 4)
-        if k < 2:
-            a, b = 64 * k, 64 * k + 64
-            dst, src, sem = T["aq%d" % t][:, a:b].bitcast(dt.uint8), T["rq%d" % t][:, a:b].bitcast(dt.uint8), "arc%d" % t
-        elif k == 2:
+        g.wait_ge(T.sem["hop%d" % t], 8 if k < 2 else 16)
+        if k == 0:
+            dst, src, sem = T["aq%d" % t][:, 0:L].bitcast(dt.uint8), T["rq%d" % t][:, 0:L].bitcast(dt.uint8), "arc%d" % t
+        elif k == 1:
             dst, src, sem = T["ap%d" % t][:, 0:L], T["rp%d" % t][:, 0:L], "arc%d" % t
         else:
-            dst, src, sem = T["pw%d" % t][:, C:C + L], T["rn%d" % t][:, 0:L], "arp%d" % t
+            dst, src, sem = T["an%d" % t][:, 0:8], T["rn%d" % t][:, 0:8], "arn%d" % t
         g.remote_dma(dst, src, T.sem[sem], T.sem.sent, pid, rid, m)
     g.wait_ge(T.sem.sent, len(topo.engines(core, nxt)) * R)
 
@@ -142,38 +216,42 @@ def rank_program(g, core, T, topo):
     Q = {"v": g.vector, "s": g.scalar, "p": g.tensor, "g": g, "y": g.sync}
     QS = {"v": "qv", "s": "qs", "p": "qp", "g": "qg"}
     V, S = g.vector, g.scalar
-    ops, lastw, readers = [], {}, {}
+    ops, lastw, readers, chain = [], {}, {}, {}
 
     def A(name, a=0, b=None, s=1):
-        n = SCRATCH[name][1][1]
-        b = n if b is None else b
-        return (T[name][:, a:b:s] if s != 1 else T[name][:, a:b], name, np.arange(n)[a:b:s])
+        name, o, n = PART.get(name) or (name, 0, SCRATCH[name][1][1])
+        a, b = a + o, (n if b is None else b) + o
+        return (T[name][:, a:b:s] if s != 1 else T[name][:, a:b], name, np.arange(a, b, s))
 
     def bank(k, n, a=0):
-        return (T.ps[:, 512 * k + a:512 * k + n], "ps", np.array([k]))
+        return (T.ps[:, 512 * k + a:512 * k + n], "ps", np.array([k]), n - a)
 
     def op(q, reads, writes, call, ns, token=None, after=(), busy=None):
         reads = [x for x in reads if isinstance(x, tuple)]
         writes = [x for x in writes if isinstance(x, tuple)]
         me, deps = len(ops), set()
-        for _, name, idx in reads + writes:
-            deps.update(int(d) for d in np.unique(lastw.setdefault(name, np.full(SCRATCH[name][1][1], -1))[idx]) if d >= 0)
-        for _, name, idx in reads:
-            if name == "ps":
-                deps.update(d for d, m in readers.get(name, []) if m[idx].any() and ops[d][0] != q)
-        for _, name, idx in writes:
+        for x in reads + writes:
+            deps.update(int(d) for d in np.unique(lastw.setdefault(x[1], np.full(SCRATCH[x[1]][1][1], -1))[x[2]]) if d >= 0)
+        for x in reads:
+            if x[1] == "ps":
+                deps.update(d for d, m in readers.get("ps", []) if m[x[2]].any() and ops[d][0] != q)
+        for x in writes:
+            name, idx = x[1], x[2]
             for d, m in readers.get(name, []):
                 if m[idx].any():
                     deps.add(d)
                     m[idx] = False
-            readers[name] = [x for x in readers.get(name, []) if x[1].any()]
+            readers[name] = [y for y in readers.get(name, []) if y[1].any()]
             lastw[name][idx] = me
-        for _, name, idx in reads:
-            m = np.zeros(SCRATCH[name][1][1], bool)
-            m[idx] = True
-            readers.setdefault(name, []).append((me, m))
+        for x in reads:
+            m = np.zeros(SCRATCH[x[1]][1][1], bool)
+            m[x[2]] = True
+            readers.setdefault(x[1], []).append((me, m))
         deps.discard(me)
-        ops.append((q, sorted(deps), list(after), call, ns, token, ns if busy is None else busy))
+        if q in chain:
+            after, chain[q] = list(after) + chain[q], [me]
+        ops.append((q, sorted(deps), list(after), call, ns, token, ns if busy is None else busy,
+                    "%s%d" % (writes[0][1], writes[0][2][0]) if writes else None))
         return me
 
     def raw(x):
@@ -184,9 +262,9 @@ def rank_program(g, core, T, topo):
 
     def ns_of(o, xs, by=None, k=1.0):
         if by:
-            return 60 + 1.3 * len(o[2])
+            return 50 + 1.25 * len(o[2])
         two = all(SCRATCH[x[1]][2] in (B2, U2) for x in [o] + xs)
-        return 60 + 0.85 * k * len(o[2]) * (0.5 if two else 1)
+        return 50 + 0.83 * k * len(o[2]) * (0.5 if two else 1)
 
     def memset(o, c):
         op("v", [], [o], lambda: V.memset(o[0], c), ns_of(o, []))
@@ -202,10 +280,13 @@ def rank_program(g, core, T, topo):
         op("v", [i, by], [o], lambda: V.tensor_copy(o[0], ind(i, by)), ns_of(o, [i], by))
 
     def scatter(win, by, i):
-        op("v", [i, by], [win], lambda: V.tensor_copy(ind(win, by), i[0]), 60 + 3.0 * len(i[2]))
+        op("v", [i, by], [win], lambda: V.tensor_copy(ind(win, by), i[0]), 50 + 2.9 * len(i[2]))
 
     def scan(o, d0, d1, init, op0, op1):
         op("v", [d0, d1], [o], lambda: V.tensor_tensor_scan(o[0], d0[0], d1[0], init, op0, op1), ns_of(o, [d0, d1]))
+
+    def total_of(o, i):
+        op("v", [i], [o], lambda: V.tensor_reduce(o[0], i[0], AxisListType.X, OP.add), 90)
 
     def act(o, i, f=AF.Copy, bias=None, scale=1.0, acc=None, by=None):
         kw = {"scale": raw(scale)}
@@ -213,10 +294,11 @@ def rank_program(g, core, T, topo):
             kw["bias"] = raw(bias)
         if acc:
             kw["accum_out"] = acc[0]
-        op("s", [i, bias, scale, by], [o, acc], lambda: S.activation(o[0], ind(i, by), f, **kw), 75 + (1.3 if by else 0.85) * len(o[2]))
+        op("s", [i, bias, scale, by], [o, acc], lambda: S.activation(o[0], ind(i, by), f, **kw),
+           (85 if acc else 65) + (1.25 if by else 0.83) * len(o[2]))
 
     def quant2(p, i):
-        op("v", [i], p, lambda: V.quantize_mx(p[0][0], p[1][0], i[0]), 15 + 0.24 * len(i[2]))
+        op("v", [i], p, lambda: V.quantize_mx(p[0][0], p[1][0], i[0]), 12 + 0.22 * len(i[2]))
 
     def pair(n, a=0, b=None):
         return [A(n + "q", a, b), A(n + "p", a, b)]
@@ -225,18 +307,18 @@ def rank_program(g, core, T, topo):
         quant2(pair(n, a, b), i)
 
     def mm(o, l, r, start=True, stop=True):
-        op("p", l + r, [o], lambda: g.tensor.matmul_mx(o[0], l[0][0], l[1][0], r[0][0], r[1][0], start, stop), 60 + 0.6 * len(r[0][2]))
+        op("p", l + r, [o], lambda: g.tensor.matmul_mx(o[0], l[0][0], l[1][0], r[0][0], r[1][0], start, stop), 40 + 0.6 * len(r[0][2]))
 
     def iota(o, pattern, base=0, cm=0):
         kw = {} if SCRATCH[o[1]][2] == I4 else {"allow_small_or_imprecise_dtypes": True}
-        op("g", [], [o], lambda: g.iota(o[0], pattern, base, cm, **kw), 130 + 1.8 * len(o[2]))
+        op("g", [], [o], lambda: g.iota(o[0], pattern, base, cm, **kw), 130 + 1.66 * len(o[2]))
 
     def fill(o, c):
         iota(o, [[0, len(o[2])]], c)
 
     last_dma = {}
 
-    def dma(q, sem, total, out, in_, reads, writes, ns=2500):
+    def dma(q, sem, total, out, in_, reads, writes, ns=2200):
         last_dma[q] = op(q, reads, writes, lambda: Q[q].dma_start(out, in_).then_inc(T.sem[sem], 16), ns, (sem, total),
                          [last_dma[q]] if q in last_dma else [], 60)
 
@@ -245,7 +327,7 @@ def rank_program(g, core, T, topo):
             _PLAN["order"] = _plan(ops)
         count, known, token = {}, {}, {}
         for i in _PLAN["order"]:
-            q, deps, _, call, _, tok, _ = ops[i]
+            q, deps, _, call, _, tok = ops[i][:6]
             if q != "net":
                 w = {}
                 for d in deps:
@@ -264,28 +346,30 @@ def rank_program(g, core, T, topo):
         for sem, val in count.items():
             g.wait_ge(T.sem[sem], val)
 
-    CQ, CQ1, CQ4, CQ41, CG, CS16, CS4, CT4, CQ2, CP, CF16 = [A("pc", k, k + 1) for k in range(11)]
+    CQ, CQ1, CQ4, CQ41, CG, CS16, CS4, CT4, CQ2, CP, CPO, CH16, CH4, CU4, CQ16 = [A("pc", k, k + 1) for k in range(15)]
+    CZ = A("vec", 255, 256)
     HALVES = ((0, HALF), (HALF, C))
 
-    def W(k, n=NB):
-        return A("wf", 32 * k, 32 * k + n)
+    def W(k, a=0, b=NB):
+        return A("wf", 32 * k + a, 32 * k + b)
 
-    def keep16(row, a, b):
-        scan(A("ex", a, b), A("k16", a, b), row, 0.0, OP.mult, OP.add)
+    def vec(k, a=0, b=16):
+        return A("vec", 16 * k + a, 16 * k + b)
 
-    def read16(dst, a, b):
-        ts(dst, A("ex", a + 15, b, 16), CS16, OP.mult, -0.26, OP.add)
+    def keep(row, a, b, dst):
+        scan(A("exh", a, b), A("k16", a, b), row, 0.0, OP.mult, OP.add)
+        ts(dst, A("exh", a + 15, b, 16), CH16, OP.mult, float(HALF), OP.add)
 
     def wrap4(row, n, dst, a=0):
-        scan(A("ex", a, a + n), A("k4", 0, n), row, 0.0, OP.mult, OP.add)
-        ts(dst, A("ex", a + 3, a + n, 4), CS4, OP.mult, CT4, OP.add)
+        scan(A("exh", a, a + n), A("k4", 0, n), row, 0.0, OP.mult, OP.add)
+        ts(dst, A("exh", a + 3, a + n, 4), CH4, OP.mult, CU4, OP.add)
 
-    def hold(row, k, n):
-        scan(A("exb", k * n, k * n + n), row, A("kx", 0, n), -512.0, OP.max, OP.add)
+    def hold(dst, row):
+        scan(dst, row, A("kx"), -512.0, OP.max, OP.add)
 
     dma("y", "lu", 16, T.ut[:], T.u[:], [], [A("ut")])
-    dma("s", "lx", 32, T.x0[:, 0:2 * C], T.x[:, 0:2 * C], [], [A("x0", 0, 2 * C)], 3500)
-    dma("y", "lx", 32, T.x0[:, 2 * C:4 * C], T.x[:, 2 * C:4 * C], [], [A("x0", 2 * C, 4 * C)], 3500)
+    dma("s", "lx", 32, T.x0[:, 0:2 * C], T.x[:, 0:2 * C], [], [A("x0", 0, 2 * C)], 2500)
+    dma("y", "lx", 32, T.x0[:, 2 * C:4 * C], T.x[:, 2 * C:4 * C], [], [A("x0", 2 * C, 4 * C)], 2500)
     dma("y", "lw", 32, T.wq[:].bitcast(dt.uint8), T.wc[:], [], [A("wq")])
     dma("y", "lw", 32, T.wp[:], T.ws[:], [], [A("wp")])
     dma("y", "lv", 16, T.vt[:], T.v[:], [], [A("vt")])
@@ -296,41 +380,60 @@ def rank_program(g, core, T, topo):
     def tab(k):
         return A("tab", 16 * k, 16 * k + 16)
 
+    EYE = tab(8)
     iota(pi(0), [[0, 1]], 0, 1)
     iota(tab(0), [[1, 16]])
     iota(A("cw"), [[16, NB]])
     iota(A("pi", 8, 16), [[16, 8]])
     iota(tab(1), [[0, 4], [1, 4]])
     iota(A("jw", 14, 42), [[8, NB]])
-    iota(A("g64"), [[1, 8], [0, 64]])
-    iota(A("seg"), [[0, NB], [64, 16]])
-    for m in range(7):
-        fill(A("fl", 4 * (TO[m] + (400 if m == 6 else 64 * m + 16)), 4 * (TO[m] + TW[m])), 0)
-    fill(A("ones"), 1)
+    iota(A("g32"), [[1, 8], [0, 4]])
+    iota(A("tab", 160, 192), [[-1, 2], [0, 16]], 1)
+    iota(tab(12), [[1, 4], [-1, 4]])
+    memset(tab(13), 0.0)
+    memset(A("ones"), 1.0)
+    op("g", [A("ones")], [A("em")], lambda: g.affine_select(T.em[:], T.ones[:], [[-1, 528]], OP.is_equal, 0.0, 3, 4), 1100)
+    memset(A("zz"), 0.0)
+    runs = []
+    for kind, lanes, lo, hi, a, _ in TILES:
+        runs.append((a, a + 16 * lanes[-1] - lo) if kind == "d" else (a + 16 * lanes[-1], a + hi))
+    runs[1] = (LOW, runs[1][1])
+    for a, b in reversed(runs):
+        dma("y", "lf", 16 * len(runs), T.fl[:, 4 * a:4 * b], T.zz[:, 0:4 * (b - a)], [A("zz", 0, 4 * (b - a))], [A("fl", 4 * a, 4 * b)])
     fill(A("win", 0, 4 * C), 0)
     iota(A("cnt"), [[1, C + L]])
-    iota(A("k5"), [[0, 112], [256, 5]])
+    iota(A("cne"), [[2, C]], -C)
+    iota(A("k5"), [[0, 84], [256, 5]])
     fill(A("lh"), 0)
-    op("g", [A("ones")], [A("em")], lambda: g.affine_select(T.em[:], T.ones[:], [[-1, 528]], OP.is_equal, 0.0, 3, 4), 1100)
+    iota(A("k6"), [[0, NB], [1, LN]])
+    fill(A("el"), 1)
+    fill(A("tl"), 0)
+    fill(A("nl"), 0)
 
-    memset(A("eqr", 0, 2), 0.0)
-    memset(A("eqr", C, C + 2), 0.0)
-    memset(A("rs", 0, 1), 0.0)
+    memset(A("gt", C, C + 16), 0.0)
+    memset(A("rs"), 0.0)
+    memset(A("ev"), 0.0)
+    memset(A("ev", 0, 1), float(C))
+    memset(A("lr"), 0.0)
+    for t in range(R):
+        memset(A("sn%d" % t), 0.0)
     ts(pi(1), pi(0), 15, OP.bitwise_and)
     ts(pi(2), pi(0), 4, OP.arith_shift_right)
     cp(CQ, pi(1))
     ts(pi(3), pi(1), 2, OP.arith_shift_right)
     ts(pi(4), pi(1), 3, OP.bitwise_and)
     ts(A("qo"), A("cw"), 0.0, OP.mult, CQ, OP.add)
-    ts(tab(2), tab(0), CQ, OP.is_equal, 2 * BIG, OP.mult)
+    ts(EYE, tab(0), CQ, OP.is_equal)
     ts(tab(3), tab(0), CQ, OP.is_gt, 2 * BIG, OP.mult)
     ts(CQ1, pi(1), 1.0, OP.add)
-    ts(tab(2), tab(2), -BIG, OP.add)
+    ts(tab(2), EYE, 2 * BIG, OP.mult, -BIG, OP.add)
     ts(tab(3), tab(3), -BIG, OP.add)
     act(A("cm"), tab(2), by=A("qo"))
     act(A("ck"), tab(3), by=A("qo"))
+    iota(A("kr"), [[0, NB], [512, 16]])
+    ts(A("kb"), A("kr", 0, LOW), -256.0, OP.add, BIG / 256, OP.mult)
     ts(tab(4), tab(0), CQ, OP.is_lt, -512.0, OP.mult)
-    ts(tab(5), tab(0), CQ, OP.is_equal, 256.0, OP.mult)
+    ts(tab(5), EYE, 256.0, OP.mult)
     ts(tab(6), tab(0), 15.0, OP.is_equal, -512.0, OP.mult)
     ts(tab(7), tab(0), CQ1, OP.is_equal, F, OP.mult)
     tt(tab(4), tab(4), tab(5), OP.add)
@@ -338,251 +441,317 @@ def rank_program(g, core, T, topo):
     cp(A("ulu"), A("pi", 8, 16))
     tt(tab(4), tab(4), tab(6), OP.add)
     tt(tab(7), tab(7), tab(0), OP.max)
+    act(A("ky"), tab(4), scale=2.0, by=A("qo"))
     act(A("kx"), tab(4), by=A("qo"))
     act(A("k16"), tab(7), by=A("qo"))
-    memset(A("pf"), 0.0)
+    memset(A("pf", C, 512), 0.0)
+    ts(CQ16, pi(1), -16.0, OP.add)
     ts(pi(5), pi(1), 1, OP.arith_shift_right)
     cp(CG, pi(2))
     cp(CQ4, pi(3))
     ts(CQ41, pi(3), 1.0, OP.add)
     ts(CP, pi(1), 2.0, OP.subtract)
-    ts(CT4, pi(4), -0.2, OP.add)
+    cp(CT4, pi(4))
+    ts(CU4, pi(4), 2.0 * C, OP.add)
     cp(CQ2, pi(5))
     tt(CP, CP, CP, OP.mult)
     ts(CS16, pi(1), 15.0, OP.is_equal, 1.0 - 1.0 / F, OP.mult)
-    ts(CF16, pi(1), 15.0, OP.not_equal, F - 1.0, OP.mult)
     ts(CS4, pi(3), 3.0, OP.is_equal, 4.0 - 4.0 / F, OP.mult)
     ts(CP, CP, 1.0, OP.is_le)
     ts(CS16, CS16, 1.0 / F, OP.add)
-    ts(CF16, CF16, 1.0, OP.add)
     ts(CS4, CS4, 4.0 / F, OP.add)
+    ts(CH16, CS16, 0.5, OP.mult)
+    ts(CH4, CS4, 0.5, OP.mult)
     quant("u", A("ut"))
     op("v", [A("uq"), A("ulu")], [A("urq")], lambda: V.tensor_copy(
         T.urq[:, 0:128].bitcast(dt.uint32), T.uq[:, 0:128].bitcast(dt.uint32).indirect(T.ulu[:, 0:8])), 240)
-    op("v", [A("up"), A("ulu")], [A("urp")], lambda: V.tensor_copy(T.urp[:, 0:128], T.up[:, 0:128].indirect(T.ulu[:, 0:8])), 240)
-    ts(A("cpt"), A("g64"), CG, OP.is_equal, CP, OP.mult)
-    ts(A("cst"), A("g64"), CG, OP.is_equal)
+    op("s", [A("up"), A("ulu")], [A("urp")], lambda: S.activation(T.urp[:, 0:128], T.up[:, 0:128].indirect(T.ulu[:, 0:8]), AF.Copy), 225)
+    ts(A("g32"), A("g32"), CG, OP.is_equal, CQ16, OP.mult)
+    ts(A("go"), A("g32"), 16.0, OP.add)
+    ts(tab(12), tab(12), 0.0, OP.is_equal, CP, OP.mult)
+    act(A("cst"), A("tab", 160, 192), by=A("go"))
+    act(A("cpt"), A("tab", 192, 224), by=A("go"))
+    ts(CPO, CS4, -C / 4.0, OP.mult)
     ts(A("jw", 42, 70), A("cw"), CQ, OP.add)
     ts(tab(5), tab(1), CQ41, OP.is_equal, F, OP.mult)
     ts(tab(1), tab(1), CQ4, OP.not_equal)
     quant("cp", A("cpt"))
     quant("cs", A("cst"))
-    ts(A("cw"), A("cw"), CQ, OP.subtract, 15.0, OP.add)
+    ts(A("cw", NV, NB), A("cw", NV, NB), CQ, OP.subtract, 15.0 + 512.0 - 4096.0, OP.add)
+    ts(A("cw", 0, NV), A("jw", 42, 42 + NV), -1.0, OP.mult, LOW - 1.0 + 512.0 - 4096.0, OP.add)
+    ts(A("cw"), A("cw"), A("ky", 15, 16), OP.add)
     ts(A("jw", 14, 42), A("jw", 14, 42), CQ2, OP.add)
     cp(A("jw", 0, 14), A("jw", 42, 56))
     ts(A("jw", 70, 84), A("jw", 42, 56), float(HALF), OP.add)
-    ts(A("jw", 84, 112), A("jw", 42, 70), -1.0, OP.mult, C - 1.0, OP.add)
+    ts(A("jw", 84, 112), A("jw", 42, 70), -1.0, OP.mult, C - 1.0 + 512.0, OP.add)
     tt(tab(5), tab(5), tab(1), OP.max)
-    cp(W(8, B0), A("jw", 84, 84 + B0))
-    act(A("k4"), tab(5), by=A("qo"))
+    act(A("k4", 0, 128), tab(5), by=A("qo", 0, 8))
+    act(A("k4", 128, C), tab(5), by=A("qo", 8, NB))
+    ts(A("k6"), A("k6"), 1.0, OP.min)
+    ts(A("k6n"), A("k6"), -1.0, OP.mult, 1.0, OP.add)
     quant("v", A("vt"))
     for b in range(4):
         quant2([A("eq4", 128 * b, 128 * b + 128), A("ep4", 128 * b, 128 * b + 128)], A("em", 3 - b, 515 - b))
+    z0 = TILES[ND - 2][5] - PAD
+    quant("fl", A("zz"), z0, z0 + 256)
+    for m, (kind, lanes, lo, hi, a, q0) in reversed(list(enumerate(TILES))):
+        if lo and m != ND - 2:
+            dma("y", "lz", 32 * (ND - 2), T.flq[:, q0:q0 + lo].bitcast(dt.uint8), T.flq[:, z0:z0 + lo].bitcast(dt.uint8),
+                [A("flq", z0, z0 + lo)], [A("flq", q0, q0 + lo)])
+            dma("y", "lz", 32 * (ND - 2), T.flp[:, q0:q0 + lo], T.flp[:, z0:z0 + lo], [A("flp", z0, z0 + lo)], [A("flp", q0, q0 + lo)])
 
-    def slot(b):
-        m = (b - 1) // 4
-        return 4 * TO[m] + 4 * m + 4 - b
+    def E(b):
+        return [A("eq4", 128 * b, 128 * b + 128), A("ep4", 128 * b, 128 * b + 128)]
 
-    def qtile(m):
-        a, b = TO[m], TO[m] + TW[m]
-        quant("fl", A("fl", 4 * a, 4 * b), a, b)
-        mm(bank(2, TW[m]), pair("cs"), pair("fl", a, b), m == 6, m == 0)
+    JW = A("jw", 42, 70)
+    EH, EN, EU, EM, HH, HM, HN, ST, XV, NN, NH, AH = range(12)
 
-    for t in range(R):
-        K = 4 + t
-        NV = NVS[t]
-        xb = "x0" if t == 0 else "xs"
-        sq, sp, sn, pw = "sq%d" % t, "sp%d" % t, "sn%d" % t, "pw%d" % t
-        quant("x", A(xb))
-        mm(bank(0, C), pair("ur"), pair("x"))
-        mm(bank(1, C), pair("ur"), pair("x"))
-        if t == 0:
-            mm(bank(3, C), pair("u"), pair("x"))
-            act(A("sg", 3200, 3200 + C), bank(3, C), AF.Sign)
-            act(A("pf", 0, 4 * C, 4), A("sg", 3200, 3200 + C), AF.Relu)
-            quant("pf", A("pf"))
-            mm(bank(4, C), pair("cp"), pair("pf"))
-            hold(bank(4, C), 0, C)
-        else:
-            act(A("ptr"), A("pw%d" % (t - 1)), by=A("nx1"))
-            hold(A("ptr"), 0, C)
-        ts(A("poff"), A("exb", 15, C, 16), -float(C), OP.mult, float(C * (K - 1 - 256)), OP.add)
-        for a, b in HALVES:
-            tt(A("yy", a, b), bank(0, b, a), A("cm", a, b), OP.min)
-            scan(A("hd", a, b), A("ck", a, b), A("yy", a, b), 0.0, OP.min, OP.max)
-        for b in range(NV - 1, 0, -1):
-            h = A("sg", 8 * b * (b - 1), 8 * b * (b + 1))
-            act(h, bank(1, 16 * b), AF.Sign, bias=A("hd", 16 * b + 15, 16 * b + 16), scale=-1.0)
-            act(A("fl", slot(b), slot(b) + 64 * b, 4), h, AF.Relu, acc=A("rs", b, b + 1))
-        for a, b in HALVES:
-            act(A("xh", 4 * a, 4 * b), A(xb, 4 * a, 4 * b), scale=0.5)
-        for a, b in HALVES:
-            diag = A("fl", 4 * (TO[6] + a), 4 * (TO[6] + b), 4)
-            tt(diag, bank(0, b, a), A("hd", a, b), OP.is_le)
-            scan(A("dsc", a, b), A("seg", a, b), diag, 0.0, OP.min, OP.add)
-        for b in range(NB - 1, NV - 1, -1):
-            ts(A("fl", slot(b), slot(b) + 64 * b, 4), bank(0, 16 * b), A("hd", 16 * b + 15, 16 * b + 16), OP.is_lt)
-            e = RS * (b - NV + 1)
-            scan(A("rsc", e - 8 * b, e), A("fl", slot(b), slot(b) + 32 * b, 4), A("fl", slot(b) + 32 * b, slot(b) + 64 * b, 4),
-                 -float(HALF), OP.add, OP.add)
-        tt(A("base"), A("cw"), A("dsc", 15, C, 16), OP.subtract)
-        tt(A("base"), A("base"), A("poff"), OP.add)
-        ts(A("rs", NV, NB), A("rsc", RS - 1, RS * (NB - NV), RS), float(HALF), OP.add)
-        for m in (6, 3, 5, 4, 2, 1, 0):
-            qtile(m)
-        tt(A("base"), A("base"), A("rs"), OP.subtract)
-        ts(A("base"), A("base"), CF16, OP.mult)
-        for a, b in HALVES:
-            keep16(bank(2, b, a), a, b)
-            tt(A("wf", a // 16, b // 16), A("ex", a + 15, b, 16), A("base", a // 16, b // 16), OP.add)
-            ts(A("o1", a // 16, b // 16), A("wf", a // 16, b // 16), CS16, OP.mult, -0.26, OP.add)
-        n = K * C
-        scatter(A("win", 0, n), A("o1"), A("ones", 0, C))
-        scan(A("so", 0, n), A("win", 0, n), A("win", 0, n), -C - 2.0, OP.add, OP.add)
-        act(A("plr", HALF, C), A("so", 0, n), AF.Identity, bias=float(HALF), scale=0.5, by=A("o1", 14, NB))
-        ts(A("plr", 0, HALF), A("so", 0, n), 0.5, OP.mult, float(HALF), OP.add, A("o1", 0, 14))
-        if t + 1 < R:
-            fill(A("win", 0, n + C), 0)
-        ends = A("so", C - 1, C * (K - 1), C)
+    def brackets(K):
         k1 = K - 1
-        ts(A("ei", 0, k1), ends, 0.5, OP.mult, HALF + 1.0, OP.add)
-        ts(A("ef", 0, k1), ends, 0.5, OP.mult, HALF + 1.0, OP.add)
-        ts(A("ei", 8, 8 + k1), A("ei", 0, k1), 1, OP.arith_shift_right)
-        ts(A("ef", 24, 24 + k1), A("ei", 8, 8 + k1), -1.0, OP.mult, 0.5, OP.add)
-        cp(A("ef", 8, 8 + k1), A("ei", 8, 8 + k1))
-        ts(A("ef", 16, 16 + k1), A("ei", 8, 8 + k1), -float(HALF), OP.add)
-        for k in range(k1):
-            ts(A("lh", 420 + k, 560, 5), A("jw", 42, 70), A("ef", k, k + 1), OP.is_lt, float(k1 - k), OP.mult)
-            act(A("sgn", 42 * k, 42 * k + 42), A("jw", 0, 42), AF.Sign, bias=A("ef", 24 + k, 25 + k))
-            act(A("lh", k, 210, 5), A("sgn", 42 * k, 42 * k + 42), scale=A("ef", 8 + k, 9 + k))
-            act(A("lh", 210 + k, 420, 5), A("sgn", 42 * k, 42 * k + 42), scale=A("ef", 16 + k, 17 + k))
-        for a, b in HALVES:
-            keep16(A("plr", a, b), a, b)
-            read16(A("plw", a // 16, b // 16), a, b)
-        scan(A("lo", 420, 560), A("k5", 420, 560), A("lh", 420, 560), 0.0, OP.min, OP.max)
-        cp(A("clw"), A("lo", 424, 560, 5))
-        scatter(A("orow"), A("plw"), A("cnt", 0, C))
-        act(A("clr"), A("cnt", 0, 16), by=A("clw"))
+        ev = A("ev")
+        cp(A("ei"), ev)
+        ts(vec(EN), ev, -1.0, OP.mult)
+        ts(vec(EU), ev, -0.5, OP.add)
+        ts(A("ei"), A("ei"), 1, OP.arith_shift_right)
+        cp(vec(HH), A("ei"))
+        ts(vec(HN), A("ei"), -1.0, OP.mult, 0.5, OP.add)
+        ts(vec(HM), A("ei"), -float(HALF), OP.add)
+        for k in range(1, K):
+            s = A("sgn", 42 * (k - 1), 42 * k)
+            act(s, A("jw", 0, 42), AF.Sign, bias=vec(HN, k, k + 1))
+            act(A("lh", k - 1, 210, 5), s, scale=vec(HH, k, k + 1))
+            act(A("lh", 209 + k, 420, 5), s, scale=vec(HM, k, k + 1))
         scan(A("lo", 210, 420), A("k5", 210, 420), A("lh", 210, 420), 0.0, OP.min, OP.max)
         scan(A("lo", 0, 210), A("k5", 0, 210), A("lh", 0, 210), 0.0, OP.min, OP.max)
-        tt(A("wf", 46, 60), A("jw", 70, 84), A("lo", 214, 280, 5), OP.subtract)
-        tt(A("wf", 32, 46), A("jw", 0, 14), A("lo", 4, 70, 5), OP.add)
-        cp(A("fiw", 14, NB), A("wf", 46, 60))
-        cp(A("fiw", 0, 14), A("wf", 32, 46))
-        cp(A("abr", HALF, C), A("orow"), by=A("fiw", 14, NB))
-        act(A("abr", 0, HALF), A("orow"), by=A("fiw", 0, 14))
-        wrap4(A("abr", HALF, C), HALF, A("ab4", 2 * NB, 4 * NB), HALF)
-        wrap4(A("abr", 0, HALF), HALF, A("ab4", 0, 2 * NB))
+        tt(W(1, 14, NB), A("jw", 70, 84), A("lo", 214, 280, 5), OP.subtract)
+        tt(W(1, 0, 14), A("jw", 0, 14), A("lo", 4, 70, 5), OP.add)
+        cp(A("fiw"), W(1))
         lo_, hi_ = A("lo", 74, 210, 5), A("lo", 284, 420, 5)
-        tt(W(2), A("jw", 42, 70), lo_, OP.subtract)
+        tt(W(2), JW, lo_, OP.subtract)
         tt(W(3), lo_, hi_, OP.add)
         tt(W(4), W(2), hi_, OP.add)
         ts(W(4), W(4), float(HALF), OP.is_ge)
         tt(W(4), W(4), W(3), OP.mult)
         tt(W(7), W(4), W(2), OP.add)
         cp(A("fw"), W(7))
-        for k in range(4):
-            act(A("bh", HALF * k, HALF * k + HALF), A("xh"), by=A("ab4", 2 * NB + 14 * k, 2 * NB + 14 * k + 14))
-            tt(A("zt", HALF * k, HALF * k + HALF), A("xh"), A("bh", HALF * k, HALF * k + HALF), OP.add, by=A("ab4", 14 * k, 14 * k + 14))
+        act(A("fr", P0, C), A("cne"), by=A("fw", B0, NB))
+        for k in range(1, K):
+            act(A("el", k - 1, LN * NB, LN), JW, AF.Abs, bias=vec(EN, k, k + 1))
+            act(A("sge", 32 * k, 32 * k + NB), JW, AF.Sign, bias=vec(EU, k, k + 1), scale=-1.0)
+        scan(A("eo"), A("k6n"), A("el"), 1.0, OP.max, OP.min)
+        cp(A("eqw"), A("eo", LN - 1, LN * NB, LN))
+        act(A("eqr"), A("cnt", 0, 16), by=A("eqw"))
+        ts(vec(EH), vec(HH), -2.0, OP.mult)
+        ts(vec(EM), vec(HH), -float(C), OP.add)
+        tt(vec(EH), vec(EH), ev, OP.add)
+        tt(vec(EM), vec(EM), EYE, OP.mult)
+        tt(vec(EH), vec(EH), vec(EM), OP.mult)
+        total_of(CZ, vec(EH))
+        ts(A("xi", 0, 1), CZ, float(C), OP.add)
+        tt(vec(ST), vec(HH), ev, OP.subtract)
+        tt(vec(ST, 0, 8), vec(ST, 0, 8), vec(HH, 1, 9), OP.subtract)
+        ts(vec(ST, 0, 8), vec(ST, 0, 8), float(C), OP.add)
+
+    for t in range(R):
+        K = 4 + t
+        xb = "x0" if t == 0 else "xs"
+        sq, sp, sn, an = "sq%d" % t, "sp%d" % t, "sn%d" % t, "an%d" % t
+        if t == 0:
+            quant("x", A(xb))
+        mm(bank(0, C), pair("ur"), pair("x"))
+        mm(bank(1, C), pair("ur"), pair("x"))
+        if t == 0:
+            mm(bank(7, C), pair("u"), pair("x"))
+            act(A("sg", SG, SG + C), bank(7, C), AF.Sign)
+            act(A("pf", 0, C), A("sg", SG, SG + C), AF.Relu)
+            quant("pf", A("pf"))
+            mm(bank(5, 128), pair("cp"), pair("pf"))
+            scan(A("ex0"), A("k4", 0, C // 4), bank(5, C // 4), 0.0, OP.mult, OP.add)
+            ts(A("poff"), A("ex0", 3, C // 4, 4), CPO, OP.mult, float(C * (K - 1)), OP.add)
+            for k in range(1, K):
+                ts(A("pf", NB * k, NB * (k + 1)), A("ex0", 3, C // 4, 4), CS4, OP.mult, 4.0 * k - 2.0, OP.is_ge)
+            quant("pf", A("pf"))
+            mm(bank(6, 128), pair("cs"), pair("pf"))
+            for k in range(1, K):
+                total_of(A("ev", k, k + 1), bank(6, NB // 4 * (k + 1), NB // 4 * k))
+            brackets(K)
+        for a, b in ((LOW, C), (0, LOW)):
+            tt(A("yy", a, b), bank(0, b, a), A("cm", a, b), OP.min)
+        for a, b in ((LOW, C), (0, LOW)):
+            scan(A("hd", a, b), A("ck", a, b), A("yy", a, b), -BIG, OP.min, OP.max)
+        back = (T.hx[:, LOW - 1::-1], "hx", np.arange(LOW)), (T.hd[:, LOW - 1::-1], "hd", np.arange(LOW))
+        scan(back[0], A("kb"), back[1], -BIG, OP.min, OP.max)
+        o, late = 0, None
+        chain["s"] = []
+        for kind, lanes, lo, hi, a, q0 in TILES:
+            for k, d in enumerate(lanes if kind == "b" else ()):
+                h = A("sg", o, o + 16 * d)
+                o += 16 * d
+                act(h, bank(1, 16 * d), AF.Sign, bias=A("hd", 16 * d + 15, 16 * d + 16), scale=-1.0)
+                if late:
+                    act(*late)
+                late = (A("fl", 4 * a + k, 4 * (a + 16 * d), 4), h, AF.Relu, None, 1.0, A("rs", d, d + 1))
+        act(*late)
+        chain.pop("s")
+
+        def sums(m):
+            kind, lanes, lo, hi, a, q0 = TILES[m]
+            quant("fl", A("fl", 4 * a, 4 * (a + hi - lo)), q0 + lo, q0 + hi)
+            if kind == "d":
+                for k, d in enumerate(lanes):
+                    first = m == SUMS[0] and k == 0
+                    n = LOW if first else max(128, LOW - 16 * d)
+                    mm(bank(3, n), E(k), pair("fl", q0 + 16 * d, q0 + 16 * d + n), first, d == LAST_D)
+                if m == 0:
+                    mm(bank(4, C - LOW), E(0), pair("fl", q0 + LOW, q0 + C))
+            hi = C if m == SUMS[0] else hi
+            mm(bank(2, hi), pair("cs"), pair("fl", q0, q0 + hi), m == SUMS[0], m == SUMS[-1])
+
+        late = []
+        for m in SUMS:
+            kind, lanes, lo, hi, a, q0 = TILES[m]
+            for k, d in enumerate(lanes if kind == "d" else ()):
+                e = C if d == 0 else LOW
+                tt(A("fl", 4 * (a + 16 * d - lo) + k, 4 * (a + e - lo), 4), bank(0, e, 16 * d), A("hx" if d else "hd", 0, e - 16 * d), OP.is_le)
+                while late:
+                    sums(late.pop(0))
+            late.append(m)
+        for m in late:
+            sums(m)
+        for a, b in HALVES:
+            act(A("xh", 4 * a, 4 * b), A(xb, 4 * a, 4 * b), scale=0.5)
+        scan(A("xr", LOW, C), A("kr", LOW, C), bank(4, C - LOW), 0.0, OP.min, OP.add)
+        scan(A("xr", 0, LOW), A("kr", 0, LOW), bank(3, LOW), 0.0, OP.min, OP.add)
+        tt(A("base"), A("cw"), A("poff"), OP.add)
+        tt(A("base"), A("base"), A("rs"), OP.subtract)
+        tt(A("ky", 15, C, 16), A("base"), A("xr", 15, C, 16), OP.subtract)
+        for a, b in HALVES:
+            scan(A("ex", a, b), bank(2, b, a), A("ky", a, b), -1024.0, OP.max, OP.add)
+            ts(A("o1", a // 16, b // 16), A("ex", a + 15, b, 16), 4096.0, OP.add)
+        n = K * C
+        scatter(A("win", 0, n), A("o1"), A("ones", 0, C))
+        scan(A("so", 0, n), A("win", 0, n), A("win", 0, n), -C - 2.0, OP.add, OP.add)
+        act(A("plr", HALF, C), A("so", 0, n), by=A("o1", 14, NB))
+        cp(A("plr", 0, HALF), A("so", 0, n), A("o1", 0, 14))
+        if t + 1 < R:
+            fill(A("win", 0, n + C), 0)
+        for a, b in HALVES:
+            keep(A("plr", a, b), a, b, A("plw", a // 16, b // 16))
+        scatter(A("orow"), A("plw"), A("cne"))
+        cp(A("abr", HALF, C), A("orow"), by=A("fiw", 14, NB))
+        act(A("abr", 0, HALF), A("orow"), by=A("fiw", 0, 14))
+        wrap4(A("abr", HALF, C), HALF, A("ab4", 2 * NB, 4 * NB), HALF)
+        wrap4(A("abr", 0, HALF), HALF, A("ab4", 0, 2 * NB))
+        for a, b in ((0, 8), (8, 28), (28, 48), (48, 2 * NB)):
+            act(A("bh", 16 * a, 16 * b), A("xh"), by=A("ab4", 2 * NB + a, 2 * NB + b))
+            tt(A("zt", 16 * a, 16 * b), A("xh"), A("bh", 16 * a, 16 * b), OP.add, by=A("ab4", a, b))
         for k in range(2):
-            act(A("ab", C * k, C * k + C), A(xb), by=A("ab4", NB * k, NB * k + NB))
-            act(A("ab", 2 * C + C * k, 3 * C + C * k), A("bh", C * k, C * k + C), scale=2.0)
-        quant("z", A("zt"))
+            act(A("xn", C * k, C * k + C), A(xb), by=A("ab4", NB * k, NB * k + NB))
+            act(A("bb", C * k, C * k + C), A("bh", C * k, C * k + C), scale=2.0)
+        qz, qh = [A("zq"), A(sp, L, L + HALF)], [A("hq"), A(sp, L + HALF, L + C)]
+        quant2(qz, A("zt"))
         for b in range(4):
-            mm(bank(3 + b, HALF), pair("w", 128 * b, 128 * b + 128), pair("z"))
-        for a in range(1, C, 149):
-            tt(A("eqr", a, a + 149), A("clr", a, a + 149), A("clr", a - 1, a + 148), OP.is_equal)
+            mm(bank(3 + b, HALF), pair("w", 128 * b, 128 * b + 128), qz)
         for b in range(2):
             ts(A("ht", b, 2 * C, 4), bank(3 + b, HALF), 0.03125, OP.mult)
             act(A("ht", 2 + b, 2 * C, 4), bank(5 + b, HALF), scale=0.03125)
-        qh = [A("hq"), A(sp, L, L + HALF)]
         quant2(qh, A("ht"))
+        mm(bank(0, HALF), pair("ur"), qh)
         mm(bank(7, HALF), pair("ur"), qh)
-        ts(A("gr", 0, HALF), bank(7, HALF), 0.0, OP.is_gt)
-        ts(A("gr", HALF, C), bank(7, HALF), 0.0, OP.is_le)
+        ts(A("gt", 0, HALF), bank(0, HALF), 0.0, OP.is_le)
+        act(A("gt", HALF, C), bank(7, HALF), AF.Sign)
+        op("g", [A("ht"), A("xn", 0, 2 * C)], [A("xn", 0, 2 * C)],
+           lambda: g.dma_start(T.xn[:, 0:2 * C], T.ht[:], accum_op=OP.add).then_inc(T.sem.acc, 16), 3500, ("acc", 16 * t + 16), (), 1000)
         for a in range(0, 2 * C, L):
-            tt(A("xn", a, a + L), A("ab", a, a + L), A("ht", a, a + L), OP.add)
-            tt(A("xn", 2 * C + a, 2 * C + a + L), A("ab", 2 * C + a, 2 * C + a + L), A("ht", a, a + L), OP.subtract)
-        act(A("gb", HALF, C), A("gr"), AF.Identity, bias=1.0, scale=-1.0, by=A("fw", 14, NB))
-        ts(A("gb", 0, HALF), A("gr"), -1.0, OP.mult, 1.0, OP.add, A("fw", 0, 14))
-        act(A("lrg", 2 * C + P0, 3 * C), A("gb", P0, C), AF.Identity, bias=1.0, scale=-1.0)
-        act(A("fr", P0, C), A("cnt", 0, C), by=A("fw", B0, NB))
-        scan(A("lrg", 0, C), A("eqr", 0, C), A("gb"), 0.0, OP.mult, OP.add)
-        hold(A("lrg", P0, C), 0, C - P0)
-        scan(A("lrg", 2 * C - 1, C + P0 - 1, -1), A("eqr", C, P0, -1), A("lrg", 3 * C - 1, 2 * C + P0 - 1, -1), 0.0, OP.mult, OP.add)
-        hold(A("gb", P0, C), 2, C - P0)
-        hold(A("lrg", C + P0, 2 * C), 1, C - P0)
-        w = NB - B0
-        lg, rg, lost = [A("exb", 15 + (C - P0) * k, (C - P0) * (k + 1), 16) for k in range(3)]
-        jl = A("wf", 256 + B0, 256 + NB)
-        ts(W(9, w), lost, -1.0, OP.mult, -255.0, OP.add)
-        ts(W(11, w), lost, 256.0, OP.add)
-        ts(W(6, w), lost, 256.0, OP.add, -256.0, OP.mult)
-        ts(W(10, w), lg, 256.0, OP.add)
-        tt(W(6, w), W(6, w), A("jw", 84 + B0, 112), OP.add)
-        tt(W(10, w), W(10, w), W(9, w), OP.mult)
-        tt(W(5, w), rg, W(11, w), OP.mult)
-        tt(W(5, w), W(6, w), W(5, w), OP.subtract)
-        tt(jl, W(10, w), W(5, w), OP.add)
-        cp(A("jlw", 0, w), jl)
-        scatter(A("lr"), A("jlw", 0, w), A("fr", P0, C))
+            tt(A("xn", 2 * C + a, 2 * C + a + L), A("bb", a, a + L), A("ht", a, a + L), OP.subtract)
+        act(vec(XV), A("gt"), by=A("xi", 0, 1))
+        tt(vec(NN, 0, 8), vec(XV, 0, 8), vec(XV, 1, 9), OP.subtract)
+        tt(A(sn, 0, 8), vec(NN, 0, 8), vec(ST, 0, 8), OP.add)
+        rid, pid = topo.addr(relays[2], core)
+        s2 = op("g", [A(sn)], [], lambda a=(T["rn%d" % t][:, 0:8], T[sn][:, 0:8], T.sem["hop%d" % t], T.sem.sent, pid, rid,
+                                            topo.mask(core, relays[2])): g.remote_dma(*a), 300, ("sent", 32 * R))
+        act(A("gb", HALF, C), A("gt"), AF.Relu, by=A("fw", 14, NB))
+        ts(A("gb", 0, HALF), A("gt"), 0.5, OP.is_gt, by=A("fw", 0, 14))
+        for k in range(K):
+            act(A("nl", k, LN * NB, LN), A("ones", 0, NB) if k == 0 else A("sge", 32 * k, 32 * k + NB), scale=A(sn, k, k + 1))
+        scan(A("la"), A("eqr"), A("gb"), 0.0, OP.mult, OP.add)
+        hold(A("exb", C, 2 * C), A("gb"))
+        hold(A("exb", 0, C), A("la"))
+        scan(A("no"), A("k6"), A("nl"), 0.0, OP.mult, OP.max)
+        la, lost = A("exb", 15, C, 16), A("exb", C + 15, 2 * C, 16)
+        ts(W(9), lost, 256.0, OP.add, -1024.0, OP.mult)
+        tt(W(9), W(9), A("jw", 84, 112), OP.add)
+        tt(W(10), A("no", LN - 1, LN * NB, LN), la, OP.subtract)
+        tt(W(9), W(9), la, OP.add)
+        tt(W(8), W(9), W(10), OP.max)
+        ts(A("jlw"), W(8), -256.0, OP.add)
+        scatter(A("lr"), A("jlw", B0, NB), A("fr", P0, C))
         for k in range(2):
             wrap4(A("lr", 64 * k, 64 * k + 64), 64, A("l4", 16 * k, 16 * k + 16), 64 * k)
         act(A("st", 0, 2 * L), A("xn", 0, 4 * C), by=A("l4", 0, 16))
         cp(A("st", 2 * L, 4 * L), A("xn", 0, 4 * C), by=A("l4", 16, 32))
         quant2([A(sq), A(sp, 0, L)], A("st"))
         tr = []
-        for k in range(3):
+        for k in range(2):
             rid, pid = topo.addr(relays[k], core)
-            if k < 2:
-                src, dst = T[sq][:, 64 * k:64 * k + 64].bitcast(dt.uint8), T["rq%d" % t][:, 64 * k:64 * k + 64].bitcast(dt.uint8)
+            if k == 0:
+                src, dst = T[sq][:, 0:L].bitcast(dt.uint8), T["rq%d" % t][:, 0:L].bitcast(dt.uint8)
             else:
-                src, dst = T[sp][:, 0:2 * L], T["rp%d" % t][:, 0:2 * L]
-            tr.append(RemoteDMATransfer(dst_ids=[DstId(rid=rid, pnc=pid)], dma_engine_mask=_mask(topo.engines(core, relays[k])[4 * k:4 * k + 4]),
+                src, dst = T[sp][:, 0:4 * L], T["rp%d" % t][:, 0:4 * L]
+            tr.append(RemoteDMATransfer(dst_ids=[DstId(rid=rid, pnc=pid)], dma_engine_mask=_mask(topo.engines(core, relays[k])[8 * k:8 * k + 8]),
                                         remote_sem=T.sem["hop%d" % t], src=src, dst=dst))
-        s1 = op("g", [A(sq), A(sp)], [], lambda tr=tr: g.remote_dma_fused(tr, local_sem=T.sem.sent), 300, ("sent", 16 * R))
-        act(A("clp"), A("clr"), by=A("fiw"))
+        s1 = op("g", [A(sq), A(sp)], [], lambda tr=tr: g.remote_dma_fused(tr, local_sem=T.sem.sent), 300, ("sent", 32 * R), [s2])
         tt(W(5), W(8), W(7), OP.subtract)
-        ts(W(6), W(8), float(L), OP.is_lt)
-        keep16(A("lr", 0, L), L, 2 * L)
-        ts(W(5), W(5), float(C), OP.add)
-        read16(A("l1"), L, 2 * L)
+        ts(W(6), W(8), L + 256.0, OP.is_lt)
+        ts(W(5), W(5), C - 256.0, OP.add)
         tt(W(5), W(5), W(6), OP.mult)
         tt(W(5), W(5), W(7), OP.add)
         cp(A("m2w"), W(5))
-        act(A("abr"), A("cnt"), by=A("m2w"))
-        act(A("nxr"), A("abr"), by=A("plw"))
-        for a in range(0, C, 112):
-            tt(A(pw, a, a + 112), A("clp", a, a + 112), A("gr", a, a + 112), OP.add)
-        cp(A(sn), A(pw, 0, C), by=A("l1"))
-        rid, pid = topo.addr(relays[3], core)
-        s2 = op("g", [A(sn)], [], lambda a=(T["rn%d" % t][:, 0:L], T[sn][:, 0:L], T.sem["hop%d" % t], T.sem.sent, pid, rid,
-                                            _mask(topo.engines(core, relays[3])[12:16])): g.remote_dma(*a), 300, ("sent", 16 * R), [s1])
-        wrap4(A("nxr"), C, A("nx4"))
-        keep16(A("nxr"), 0, C)
-        read16(A("nx1"), 0, C)
+        cp(A("m2r"), A("cnt"), by=A("m2w"))
+        cp(A("nxr"), A("m2r"), by=A("plw"))
+        scan(A("ex"), A("k4"), A("nxr"), 0.0, OP.mult, OP.add)
+        ts(A("nx4"), A("ex", 3, C, 4), CS4, OP.mult, CT4, OP.add)
+        op("net", [A(sn)], [A(an)], None, 3500, ("arn%d" % t, n_in[2]), [s2], 0)
+        ts(vec(NH, 0, 8), A(sn), -1.0, OP.mult, 0.5, OP.add)
+        ts(vec(AH, 0, 8), A(an), -1.0, OP.mult, 0.5, OP.add)
+        for k in range(K):
+            act(A("tl", k, LN * 8, LN), A("jw", 42, 50), AF.Sign, bias=vec(AH, k, k + 1))
+            act(A("tl", LN * 8 + k, LN * NB, LN), A("jw", 50, 70), AF.Sign, bias=vec(NH, k, k + 1))
+        scan(A("to"), A("k6"), A("tl"), 0.0, OP.mult, OP.add)
+        ts(A("ttw"), A("to", LN - 1, LN * NB, LN), 0.5, OP.mult, K / 2.0, OP.add)
+        act(A("ttr"), A("cnt", 0, 16), by=A("ttw"))
+        act(A("ptp"), A("ttr"), by=A("jlw"))
+        if t + 1 < R:
+            act(A("ptr"), A("ptp"), by=A("plw"))
+            hold(A("exb", 0, C), A("ptr"))
+            ts(A("poff"), A("exb", 15, C, 16), -float(C), OP.mult, float(C * (K - 256)), OP.add)
+            ts(vec(NN, 0, 8), A(sn), float(L), OP.max, -1.0, OP.mult)
+            ts(vec(NN, 8, 16), A(an), float(L), OP.min, -float(C + L), OP.add)
+            tt(A("ev", 1, K + 1), vec(NN, 0, K), vec(NN, 8, 8 + K), OP.subtract)
+            brackets(K + 1)
+        else:
+            act(A("pout"), A("ptp"), by=A("plw"))
         came = [A("aq%d" % t), A("ap%d" % t)]
-        op("net", [A(sq)], came, None, 4500, ("arc%d" % t, n_in[0] + n_in[1] + n_in[2]), [s1], 0)
-        op("net", [A(sn)], [A(pw, C, C + L)], None, 4500, ("arp%d" % t, n_in[3]), [s2], 0)
+        op("net", [A(sq)], came, None, 3900, ("arc%d" % t, n_in[0] + n_in[1]), [s1], 0)
         for b in (0, 2, 1, 3):
-            mm(bank(3 + b, L), [A("eq4", 128 * b, 128 * b + 128), A("ep4", 128 * b, 128 * b + 128)], came)
+            mm(bank(3 + b, L), E(b), came)
         for b in range(2):
             cp(A("xn", 4 * C + b, 4 * (C + L), 4), bank(3 + b, L))
             act(A("xn", 4 * C + 2 + b, 4 * (C + L), 4), bank(5 + b, L))
-        act(A("xs", 2 * C, 4 * C), A("xn"), by=A("nx4", 2 * NB, 4 * NB))
-        cp(A("xs", 0, 2 * C), A("xn"), by=A("nx4", 0, 2 * NB))
+        act(A("xs", 4 * XV_, 4 * C), A("xn"), by=A("nx4", XV_ // 4, 4 * NB))
+        cp(A("xs", 0, 4 * XV_), A("xn"), by=A("nx4", 0, XV_ // 4))
+        quant("x", A("xs", 0, 4 * XV_), 0, XV_)
+        quant("x", A("xs", 4 * XV_, 4 * C), XV_, C)
 
     total = 16 * 8
-    quant("x", A("xs"))
-    for k in range(2):
-        mm(bank(k, HALF), pair("v"), pair("x", HALF * k, HALF * k + HALF))
+    mid = (XV_ + C) // 2
+    for k, (a, b) in enumerate(((0, XV_), (XV_, mid), (mid, C))):
+        mm(bank(k, b - a), pair("v"), pair("x", a, b))
+        (cp if k == 2 else act)(A("yo", a, b), bank(k, b - a))
+    dma("y", "out", total, T.pts[:], T.pout[0:128:16, :], [A("pout")], [])
     dma("y", "out", total, T.oc[:], T.xq[:].bitcast(dt.uint8), [A("xq")], [])
-    act(A("plr"), A("pw%d" % (R - 1)), by=A("nx1"))
-    cp(A("orow", 0, HALF), bank(0, HALF))
-    act(A("orow", HALF, C), bank(1, HALF))
-    dma("s", "out", total, T.pts[:], T.plr[0:128:16, :], [A("plr")], [])
     for k in range(4):
-        dma("s" if k == 3 else "y", "out", total, T.osc[4 * k:4 * k + 4, :], T.xp[32 * k:32 * k + 4, :], [A("xp")], [])
-    dma("y", "out", total, T.y[:, 0:HALF], T.orow[:, 0:HALF], [A("orow", 0, HALF)], [])
-    dma("s", "out", total, T.y[:, HALF:C], T.orow[:, HALF:C], [A("orow", HALF, C)], [])
+        dma("y", "out", total, T.osc[4 * k:4 * k + 4, :], T.xp[32 * k:32 * k + 4, :], [A("xp")], [])
+    dma("s", "out", total, T.y[:, 0:mid], T.yo[:, 0:mid], [A("yo", 0, mid)], [])
+    dma("y", "out", total, T.y[:, mid:C], T.yo[:, mid:C], [A("yo", mid, C)], [])
     emit()

@@ -5,25 +5,32 @@ from concourse.mybir import dt, AluOpType, ActivationFunctionType, AxisListType
 C, L, R = 448, 128, 3
 HALF = C // 2
 NB = C // 16
-NV = 20
+NV = 19
 LOW = 16 * NV
 B0 = (C - HALF - L) // 16
 P0 = 16 * B0
-XV_ = 192
+A0 = P0 // 2
+NA, NS = HALF - A0, C - A0
+SHARE = [("v", LOW, C), ("s", 0, 128), ("v", 240, LOW), ("s", 128, 240)]
+PIECE = [(LOW, C), (0, 128), (128, LOW)]
+CFG = dict(add="dma", bb="v", un="svsv", lin="s", mg="s", ky="s", gv=6, bh=(0, 320, 448, 576, 896))
 BIG = 2.0 ** 80
 F = 2.0 ** 21
 LN = 6
+LT = 2 * LN
 X4, B2, F4, I4, U2, U1 = "float8_e4m3fn_x4", "bfloat16", "float32", "int32", "uint16", "uint8"
 
 TILES = []
 _a = 0
-for _kind, _all in (("d", list(range(NV))), ("b", list(range(NB - 1, NV - 1, -1)))):
-    for _m in range(0, len(_all), 4):
-        _l = _all[_m:_m + 4]
-        _hi = (C if _m == 0 else LOW) if _kind == "d" else 16 * _l[0]
-        _lo = min(16 * _l[0], _hi - 128) if _kind == "d" else 0
-        TILES.append([_kind, _l, _lo, _hi, _a, 0])
-        _a += _hi - _lo
+_x = (NB - NV) % 4
+_lanes = list(range(4 - _x)) + list(range(NV, NV + _x)) + list(range(4 - _x, NV)) + list(range(NB - 1, NV + _x - 1, -1))
+for _m in range(0, NB, 4):
+    _l = _lanes[_m:_m + 4]
+    _kind = "d" if _l[0] < NV else "b"
+    _hi = (C if _m == 0 else LOW) if _kind == "d" else 16 * _l[0]
+    _lo = min(16 * _l[0], _hi - 128) if _kind == "d" else 0
+    TILES.append([_kind, _l, _lo, _hi, _a, 0])
+    _a += _hi - _lo
 FLW = _a
 ND = (NV + 3) // 4
 PAD = 64
@@ -32,29 +39,32 @@ for _m in list(range(ND - 1, -1, -1)) + list(range(ND, len(TILES))):
     TILES[_m][5] = FLQ
     FLQ += TILES[_m][3] + (PAD if _m == ND - 1 else 0)
 SUMS = (4, 3, 0, 1, 5, 2, 6)
-LAST_D = [TILES[_m][1][-1] for _m in SUMS if TILES[_m][0] == "d"][-1]
+LAST_D = [_d for _m in SUMS for _d in TILES[_m][1] if _d < NV][-1]
 SG = sum(16 * b for b in range(NV, NB))
+SPL = LOW - 128
 
 _S = {
-    B2: dict(x0=4 * C, xs=4 * C, xh=4 * C, ut=512, vt=512, em=528, ones=528, cst=512, cpt=512, pf=512, fl=4 * FLW, zz=4 * 256,
-             cm=C, ck=C, k16=C, k4=C, kx=C, kr=C, kb=LOW, k5=420, k6=LN * NB, k6n=LN * NB, sg=SG + C, sgn=256, sge=256, exb=2 * C, exh=C,
-             win=6 * C, so=6 * C, cne=C, eqr=C, lh=420, lo=420, bh=2 * C, bb=2 * C, zt=2 * C, ht=2 * C, xn=4 * (C + L), gt=C + 16,
-             gb=C, la=C, st=4 * L, ptr=C, plr=C, orow=C, abr=C, fr=C, lr=C, el=LN * NB, eo=LN * NB, tl=LN * NB, to=LN * NB,
-             ttr=C, ptp=C),
-    F4: dict(pc=16, tab=224, g32=32, ex0=C // 4, cnt=C + L, jw=112, cw=NB, ky=C, yy=C, hd=C, hx=LOW, rs=NB, poff=NB, base=NB, wf=512, ex=C, xr=C, ev=16, vec=256,
-             nl=LN * NB, no=LN * NB, m2r=C, nxr=C, pout=C, yo=C),
+    B2: dict(x0=4 * C, xs=4 * C, xh=4 * C, ut=512, vt=512, em=528, ones=C, cst=512, cpt=512, pf=512, fl=4 * FLW, zz=4 * 256,
+             cm=C, k16=C, k4=C, kx=C, kr=C, kb=C, k5=420, k6=LN * NB, k6n=LN * NB, sg=SG + C, sgn=256, sge=256, exb=C, exh=C,
+             h3=48 * NB + 48, lb=C, win=6 * C, so=6 * C, cne=C, eqr=C + 16, lh=420, lo=420, bh=2 * C, bb=2 * C, zt=2 * C, ht=2 * C, xn=4 * (C + L), gt=C + 16,
+             gb=C, la=C, dn=4 * NS, plr=C, orow=C, abr=C, fr=C, lr=C, el=LN * NB, eo=LN * NB, tl=LT * NB, to=LT * NB,
+             k13=LT * NB),
+    F4: dict(pc=16, tab=224, g32=32, ex0=C // 4, cnt=C, c16=16, slc=C, jw=112, cw=NB, ky=C, yy=C, hd=C, hx=LOW, rs=NB + 4, poff=NB, base=NB, wf=512, ex=C, xr=C, ev=16, vec=256,
+             nl=LN * NB, no=LN * NB, m2r=C, pcol=C, wd=3 * NB, wo=3 * NB, nxr=C, pout=C, yo=C),
     I4: dict(pi=16, ei=16),
-    U2: dict(ulu=8, go=32, qo=NB, o1=NB, plw=NB, fiw=NB, fw=NB, jlw=NB, m2w=NB, eqw=NB, ttw=NB, ab4=4 * NB, nx4=4 * NB, l4=32, xi=2),
+    U2: dict(ulu=8, go=32, qo=NB, o1=NB, plw=NB, fiw=NB, fw=NB, jlw=NB, eqw=NB, ttw=NB, ab4=4 * NB, nx4=4 * NB, xi=2),
     X4: dict(wq=512, uq=128, urq=128, vq=128, xq=C, eq4=512, csq=128, cpq=128, pfq=128, flq=FLQ, zq=HALF, hq=HALF),
     U1: dict(wp=512, up=128, urp=128, vp=128, xp=C, ep4=512, csp=128, cpp=128, pfp=128, flp=FLQ),
 }
-for _t in range(R):
-    _S[X4].update({"sq%d" % _t: L, "rq%d" % _t: L, "aq%d" % _t: L})
-    _S[U1].update({"sp%d" % _t: L + C, "rp%d" % _t: 4 * L, "ap%d" % _t: L})
-    _S[F4].update({"sn%d" % _t: 8, "rn%d" % _t: 8, "an%d" % _t: 8})
+SPW = NS + C
+_S[X4].update(sq=R * NS, rq=R * NS, aq=R * NS)
+_S[U1].update(sp=R * SPW, rp=R * 2 * NS, ap=R * NS)
+_S[F4].update(sn=R * 8, rn=R * 8, an=R * 8)
+_S[U2].update(sl=R * 32, rl=R * 32, al=R * 32)
+PIECES = {"b": (NA, NS), "a": (0, NA)}
 PART = {}
-for _d, _b, _names in ((B2, "lanes", "k6 k6n el eo tl to sgn sge k5 lh lo"), (B2, "rows", "ttr ptp ptr"), (F4, "lanef", "nl no"),
-                       (U2, "lists", "o1 plw fiw fw jlw m2w eqw ttw xi")):
+for _d, _b, _names in ((B2, "lanes", "k6 k6n el eo tl to sgn sge k5 lh lo"), (F4, "lanef", "nl no"),
+                       (U2, "lists", "o1 plw fiw fw jlw eqw ttw xi")):
     _o = 0
     for _n in _names.split():
         PART[_n] = (_b, _o, _S[_d].pop(_n))
@@ -62,142 +72,228 @@ for _d, _b, _names in ((B2, "lanes", "k6 k6n el eo tl to sgn sge k5 lh lo"), (B2
     _S[_d][_b] = _o
 SCRATCH = {n: ("sbuf", [128, w], d) for d in _S for n, w in _S[d].items()}
 SCRATCH["ps"] = ("psum", [128, 4096], F4)
-SEMAPHORES = (["qv", "qs", "qp", "qg", "sent", "lu", "lx", "lw", "lv", "lz", "lf", "out", "acc"]
-              + ["%s%d" % (n, t) for t in range(R) for n in ("hop", "arc", "arn")])
+SEMAPHORES = (["qv", "qs", "qp", "qg", "sent", "lu", "lx", "lh", "lw", "lv", "lz", "lf", "out", "acc"]
+              + ["%s%d" % (n, t) for t in range(R) for n in ("hn", "hl", "ha", "hb", "an", "al", "aa", "ab")])
 
 OP = AluOpType
 AF = ActivationFunctionType
 _PLAN = {}
-WAKE = 150
-SWEEPS, SPAN, TRIES, SOFT = 6, 100, 800, 30.0
-FIRST = "zz0 cm0 ck0 em0 urq0 xq0 go0 urp0 cst0 cpt0 k40 kb0 flq320 eq40 eq4128 eq4256 eq4384 pf0".split()
-STEPS = (-40.0, -12.0, -4.0, 4.0, 12.0, 40.0)
+SPEEDS = [dict(e=1.0, g=1.0, s=1.0, p=1.0, n=1.0, w=150.0), dict(e=1.3, g=1.5, s=1.5, p=1.8, n=1.0, w=120.0),
+          dict(e=1.1, g=0.9, s=0.8, p=1.3, n=1.25, w=220.0)]
+NET = dict(n=3100, l=3100, b=4000, a=3800, add=3300)
+SWEEPS, SPAN, TRIES, SOFT = 12, 100, 1200, 30.0
+FIRST = ("zz0 cm0 go0 kb0 cst0 urq0 xq%d xq0 urp0 cpt0 em0 k40 flq%d csq0 sg0 eq40 eq4128 eq4256 eq4384 cpq0" % (PIECE[0][0], LOW)).split()
+STEPS = (-12, -8, -5, -3, -2, -1, -1, 1, 1, 2, 3, 5, 8, 12)
+PASSES, HEAT = 6, 1.0
 
 
-def _place(ops, order, edges, start=None, free={}):
-    start, slots = list(start or [0.0] * len(ops)), {q: ([-1.0], [t]) for q, t in free.items()}
+def _edges(ops, m):
+    w = SPEEDS[m]["w"]
+    return [[(d, ops[d][4][m] + (0.0 if o[0] == ops[d][0] == "p" else w)) for d in o[1]] + [(d, ops[d][6][m]) for d in o[2]] for o in ops]
+
+
+def _fill(order, edges, queue, busy, shift):
+    start, slots = [0.0] * len(edges), {}
     for i in order:
-        t = 0.0
-        for d, lag in edges[i]:
-            if start[d] + lag > t:
-                t = start[d] + lag
-        busy = ops[i][6]
-        if busy:
-            a, b = slots.setdefault(ops[i][0], ([], []))
-            lo, k = 0, len(b)
-            while lo < k:
-                m = (lo + k) // 2
-                if b[m] > t:
-                    k = m
-                else:
-                    lo = m + 1
-            while k < len(a) and a[k] < t + busy:
+        t = max([0.0] + [start[d] + lag for d, lag in edges[i]])
+        if busy[i]:
+            t += shift[i]
+            a, b = slots.setdefault(queue[i], ([], []))
+            k = int(np.searchsorted(b, t, "right"))
+            while k < len(a) and a[k] < t + busy[i]:
                 t = max(t, b[k])
                 k += 1
             a.insert(k, t)
-            b.insert(k, t + busy)
+            b.insert(k, t + busy[i])
+            t -= shift[i]
         start[i] = t
     return start
 
 
-def _plan(ops):
-    n = len(ops)
-    fwd, bwd = [[] for _ in ops], [[] for _ in ops]
-    for i, o in enumerate(ops):
-        for d in o[1]:
-            w = 0 if o[0] == ops[d][0] == "p" else WAKE
-            fwd[i].append((d, ops[d][4] + w))
-            bwd[d].append((i, o[4] + w))
-        for d in o[2]:
-            fwd[i].append((d, ops[d][6]))
-            bwd[d].append((i, o[4] - ops[d][4] + ops[d][6]))
-    ns = np.array([o[4] for o in ops], float)
+def _run(order, edges, queue, busy, start, free):
+    for i in order:
+        q = queue[i]
+        t = free[q]
+        for d, lag in edges[i]:
+            if start[d] + lag > t:
+                t = start[d] + lag
+        start[i] = t
+        if busy[i]:
+            free[q] = t + busy[i]
 
-    lag = {(d, i): w for i in range(n) for d, w in sorted(fwd[i])}
+
+def _plan(ops):
+    n, M = len(ops), range(len(SPEEDS))
+    names = sorted({o[0] for o in ops})
+    queue = [names.index(o[0]) for o in ops]
+    edges = [_edges(ops, m) for m in M]
+    busy = [[o[6][m] for o in ops] for m in M]
+    pre = [[d for d, _ in e] for e in edges[0]]
+    post = [[] for _ in ops]
+    for i in range(n):
+        for d in pre[i]:
+            post[d].append(i)
 
     def moved(key, i, by, inside):
         key, todo = key.copy(), [i]
         key[i] += by
         while todo:
             j = todo.pop()
-            for d, _ in (fwd if by < 0 else bwd)[j]:
+            for d in (pre if by < 0 else post)[j]:
                 if (inside is None or d in inside) and (key[d] - key[j]) * by <= 0:
                     key[d] = key[j] + (1e-3 if by > 0 else -1e-3)
                     todo.append(d)
         return key
 
-    rng = np.random.default_rng(1)
-    key = -(np.array(_place([o[:6] + (0,) for o in ops], range(n - 1, -1, -1), bwd)) + ns)
-    key = (key + 1e-4 * np.arange(n)).tolist()
+    def times(order):
+        out = []
+        for m in M:
+            s = [0.0] * n
+            _run(order, edges[m], queue, busy[m], s, [0.0] * len(names))
+            out.append((s, max(s[i] + ops[i][4][m] for i in order)))
+        return out
+
+    tail = [o[4][0] for o in ops]
+    for i in range(n - 1, -1, -1):
+        for d, lag in edges[0][i]:
+            tail[d] = max(tail[d], lag + tail[i])
+    key = [1e-4 * i - tail[i] for i in range(n)]
     for k, name in enumerate(FIRST):
         i = [o[7] for o in ops].index(name)
         key = moved(key, i, min(0.0, k - 1e7 - key[i]), None)
     order = np.argsort(key, kind="stable").tolist()
-    start = _place(ops, order, fwd)
+    now = None
+    for m in M:
+        ns = [o[4][m] for o in ops]
+        rev = [[] for _ in ops]
+        for i in range(n):
+            for d, lag in edges[m][i]:
+                rev[d].append((i, lag + ns[i] - ns[d]))
+        seq = order
+        for _ in range(PASSES):
+            start = _fill(seq, edges[m], queue, busy[m], [0.0] * n)
+            rank = {i: k for k, i in enumerate(seq)}
+            seq = sorted(seq, key=lambda i: (start[i], rank[i]))
+            new = times(seq)
+            if now is None or sum(e for _, e in new) < sum(e for _, e in now):
+                best_order, now = seq, new
+            end = _fill(seq[::-1], rev, queue, busy[m], [ns[i] - busy[m][i] for i in range(n)])
+            rank = {i: k for k, i in enumerate(seq)}
+            key = [0.0] * n
+            for i in seq:
+                key[i] = max([-end[i] - ns[i]] + [key[d] + 1e-6 for d in pre[i]])
+            seq = sorted(seq, key=lambda i: (key[i], rank[i]))
+    order = best_order
+    rng = np.random.default_rng(1)
     for sweep in range(SWEEPS):
         for p0 in range((sweep % 2) * SPAN // 4, n, SPAN // 2):
             rank = {i: k for k, i in enumerate(order)}
-            order.sort(key=lambda i: (start[i], rank[i]))
-            end = max(start[i] + ops[i][4] for i in order)
-            win, latest, nxt = order[p0:p0 + SPAN], {}, {}
+            order.sort(key=lambda i: (now[0][0][i], rank[i]))
+            win = order[p0:p0 + SPAN]
             inside = set(win)
-            for i in reversed(order[p0:]):
-                t = end - ops[i][4]
-                for u, _ in bwd[i]:
-                    if u not in inside:
-                        t = min(t, latest[u] - lag[i, u])
-                if ops[i][6]:
-                    t = min(t, nxt.get(ops[i][0], 1e18) - ops[i][6])
+            last, free = [], []
+            for m in M:
+                latest, nxt = [now[m][1] - o[4][m] for o in ops], [1e18] * len(names)
+                for i in reversed(order[p0:]):
+                    if busy[m][i]:
+                        latest[i] = min(latest[i], nxt[queue[i]] - busy[m][i])
                     if i not in inside:
-                        nxt[ops[i][0]] = t
-                latest[i] = t
-            free = {}
-            for i in order[:p0]:
-                free[ops[i][0]] = max(free.get(ops[i][0], 0.0), start[i] + ops[i][6])
-            last = np.array([latest[i] for i in win])
+                        if busy[m][i]:
+                            nxt[queue[i]] = latest[i]
+                        for d, lag in edges[m][i]:
+                            latest[d] = min(latest[d], latest[i] - lag)
+                last.append(np.array([latest[i] for i in win]))
+                f = [0.0] * len(names)
+                for i in order[:p0]:
+                    if busy[m][i]:
+                        f[queue[i]] = now[m][0][i] + busy[m][i]
+                free.append(f)
+            work = [list(now[m][0]) for m in M]
 
-            def run(key):
-                new = _place(ops, sorted(win, key=key.get), fwd, start, free)
-                return float(np.exp((np.array([new[i] for i in win]) - last) / SOFT).sum())
+            def late(key):
+                seq, r = sorted(win, key=key.get), 0.0
+                for m in M:
+                    _run(seq, edges[m], queue, busy[m], work[m], list(free[m]))
+                    r += float(np.log(np.exp((np.array([work[m][i] for i in win]) - last[m]) / SOFT).sum()))
+                return r
 
             key = {i: float(k) for k, i in enumerate(win)}
-            best = run(key)
-            for _ in range(TRIES):
-                new = moved(key, win[int(rng.integers(len(win)))], float(rng.choice(STEPS)) * (0.1 + rng.random()), inside)
-                r = run(new)
-                if r <= best:
+            best = late(key)
+            held, top, draw = key, best, rng.random((TRIES, 5)).tolist()
+            for it, (u0, u1, u2, u3, u4) in enumerate(draw):
+                if it % 40 == 0:
+                    m = it // 40 % len(M)
+                    late(key)
+                    seq = sorted(win, key=key.get)
+                    lt, nxt = dict(zip(win, last[m].tolist())), [1e18] * len(names)
+                    for i in reversed(seq):
+                        if busy[m][i]:
+                            lt[i] = nxt[queue[i]] = min(lt[i], nxt[queue[i]] - busy[m][i])
+                        for d, lag in edges[m][i]:
+                            if d in inside and lt[i] - lag < lt[d]:
+                                lt[d] = lt[i] - lag
+                    least = min(lt[i] - work[m][i] for i in win)
+                    tight = [i for i in win if lt[i] - work[m][i] < least + SOFT and busy[m][i]] or win
+                i = tight[int(u0 * len(tight))] if u1 < 0.6 else win[int(u0 * len(win))]
+                same = sorted((j for j in win if queue[j] == queue[i]), key=key.get)
+                k, step = same.index(i), STEPS[int(u2 * len(STEPS))]
+                if u1 < 0.3 and k:
+                    k = max(0, k - 1 - int(u3 * 3))
+                    i, step = same[k], abs(step)
+                elif u1 < 0.6:
+                    step = -abs(step)
+                if not busy[0][i] or not 0 <= k + step < len(same):
+                    continue
+                j = same[k + step]
+                new = moved(key, i, key[j] - key[i] + (1e-2 if step > 0 else -1e-2) * (0.1 + u3), inside)
+                r = late(new)
+                if r <= best - HEAT * (1.0 - it / TRIES) * float(np.log(u4 + 1e-12)):
                     best, key = r, new
-            trial = order[:p0] + sorted(win, key=key.get) + order[p0 + SPAN:]
-            new = _place(ops, trial, fwd)
-            if max(new[i] + ops[i][4] for i in order) <= end:
-                order, start = trial, new
-    _PLAN["ns"] = max(start[i] + ops[i][4] for i in order)
-    rank = {i: k for k, i in enumerate(order)}
-    return sorted(order, key=lambda i: (start[i], rank[i]))
+                    if r <= top:
+                        top, held = r, new
+            trial = order[:p0] + sorted(win, key=held.get) + order[p0 + SPAN:]
+            new = times(trial)
+            if sum(e for _, e in new) <= sum(e for _, e in now):
+                order, now = trial, new
+    _PLAN["ns"] = [e for _, e in now]
+    _PLAN["start"] = now[0][0]
+    return order
 
 
 def _relays(rank_core, nxt, topo):
     c = [k for k in topo.cores_of(rank_core) if k != rank_core and topo.may_write(k, nxt)]
-    return sorted(c, key=lambda k: topo.die(k) != topo.die(rank_core))[:3]
+    return sorted(c, key=lambda k: topo.die(k) != topo.die(rank_core))[:4]
 
 
 def _mask(engs):
     return sum(1 << e for e in engs)
 
 
+def _share(k, piece, t):
+    a, b = PIECES[piece]
+    h = (a + b) // 2
+    a, b = ((a, h), (h, b), (a, b))[k - 1]
+    return t * NS + a, t * NS + b
+
+
 def hand_on(g, core, T, topo, nxt, k):
     rid, pid = topo.addr(nxt, core)
     m = topo.mask(core, nxt)
     for t in range(R):
-        g.wait_ge(T.sem["hop%d" % t], 8 if k < 2 else 16)
-        if k == 0:
-            dst, src, sem = T["aq%d" % t][:, 0:L].bitcast(dt.uint8), T["rq%d" % t][:, 0:L].bitcast(dt.uint8), "arc%d" % t
-        elif k == 1:
-            dst, src, sem = T["ap%d" % t][:, 0:L], T["rp%d" % t][:, 0:L], "arc%d" % t
-        else:
-            dst, src, sem = T["an%d" % t][:, 0:8], T["rn%d" % t][:, 0:8], "arn%d" % t
-        g.remote_dma(dst, src, T.sem[sem], T.sem.sent, pid, rid, m)
-    g.wait_ge(T.sem.sent, len(topo.engines(core, nxt)) * R)
+        for x in ("n", "l") if k == 0 else PIECES:
+            g.wait_ge(T.sem["h%s%d" % (x, t)], 16 if k == 0 else 4)
+            if k == 0:
+                w = 8 if x == "n" else 32
+                dst, src = T["a" + x][:, w * t:w * t + w], T["r" + x][:, w * t:w * t + w]
+            elif k < 3:
+                a, b = _share(k, x, t)
+                dst, src = T.aq[:, a:b].bitcast(dt.uint8), T.rq[:, a:b].bitcast(dt.uint8)
+            else:
+                a, b = _share(k, x, t)
+                o = 2 * (t * NS + PIECES[x][0])
+                dst, src = T.ap[:, a:b], T.rp[:, o:o + b - a]
+            g.remote_dma(dst, src, T.sem["a%s%d" % (x, t)], T.sem.sent, pid, rid, m)
+    g.wait_ge(T.sem.sent, len(topo.engines(core, nxt)) * 2 * R)
 
 
 def rank_program(g, core, T, topo):
@@ -212,6 +308,7 @@ def rank_program(g, core, T, topo):
         return
     relays = _relays(core, cores[(rank + 1) % len(cores)], topo)
     n_in = [len(topo.engines(k, core)) for k in _relays(cores[rank - 1], core, topo)]
+    SENT = ("sent", (2 * len(topo.engines(core, relays[0])) + 24) * R)
 
     Q = {"v": g.vector, "s": g.scalar, "p": g.tensor, "g": g, "y": g.sync}
     QS = {"v": "qv", "s": "qs", "p": "qp", "g": "qg"}
@@ -225,6 +322,9 @@ def rank_program(g, core, T, topo):
 
     def bank(k, n, a=0):
         return (T.ps[:, 512 * k + a:512 * k + n], "ps", np.array([k]), n - a)
+
+    def cost(**parts):
+        return tuple(sum(x * sp[k] for k, x in parts.items()) for sp in SPEEDS)
 
     def op(q, reads, writes, call, ns, token=None, after=(), busy=None):
         reads = [x for x in reads if isinstance(x, tuple)]
@@ -250,7 +350,7 @@ def rank_program(g, core, T, topo):
         deps.discard(me)
         if q in chain:
             after, chain[q] = list(after) + chain[q], [me]
-        ops.append((q, sorted(deps), list(after), call, ns, token, ns if busy is None else busy,
+        ops.append((q, sorted(deps), list(after), call, ns, token, ns if busy is None else (busy,) * len(SPEEDS),
                     "%s%d" % (writes[0][1], writes[0][2][0]) if writes else None))
         return me
 
@@ -262,9 +362,9 @@ def rank_program(g, core, T, topo):
 
     def ns_of(o, xs, by=None, k=1.0):
         if by:
-            return 50 + 1.25 * len(o[2])
+            return cost(e=50, g=1.25 * len(o[2]))
         two = all(SCRATCH[x[1]][2] in (B2, U2) for x in [o] + xs)
-        return 50 + 0.83 * k * len(o[2]) * (0.5 if two else 1)
+        return cost(e=50 + 0.83 * k * len(o[2]) * (0.5 if two else 1))
 
     def memset(o, c):
         op("v", [], [o], lambda: V.memset(o[0], c), ns_of(o, []))
@@ -280,13 +380,13 @@ def rank_program(g, core, T, topo):
         op("v", [i, by], [o], lambda: V.tensor_copy(o[0], ind(i, by)), ns_of(o, [i], by))
 
     def scatter(win, by, i):
-        op("v", [i, by], [win], lambda: V.tensor_copy(ind(win, by), i[0]), 50 + 2.9 * len(i[2]))
+        op("v", [i, by], [win], lambda: V.tensor_copy(ind(win, by), i[0]), cost(e=50, s=2.9 * len(i[2])))
 
     def scan(o, d0, d1, init, op0, op1):
         op("v", [d0, d1], [o], lambda: V.tensor_tensor_scan(o[0], d0[0], d1[0], init, op0, op1), ns_of(o, [d0, d1]))
 
     def total_of(o, i):
-        op("v", [i], [o], lambda: V.tensor_reduce(o[0], i[0], AxisListType.X, OP.add), 90)
+        op("v", [i], [o], lambda: V.tensor_reduce(o[0], i[0], AxisListType.X, OP.add), cost(e=90))
 
     def act(o, i, f=AF.Copy, bias=None, scale=1.0, acc=None, by=None):
         kw = {"scale": raw(scale)}
@@ -295,10 +395,22 @@ def rank_program(g, core, T, topo):
         if acc:
             kw["accum_out"] = acc[0]
         op("s", [i, bias, scale, by], [o, acc], lambda: S.activation(o[0], ind(i, by), f, **kw),
-           (85 if acc else 65) + (1.25 if by else 0.83) * len(o[2]))
+           cost(e=65, g=1.25 * len(o[2])) if by else cost(e=(85 if acc else 65) + 0.83 * len(o[2])))
+
+    def lin(o, i, scale, bias, q=None):
+        if (q or CFG["lin"]) == "s":
+            act(o, i, AF.Identity, bias, scale)
+        else:
+            ts(o, i, scale, OP.mult, bias, OP.add)
+
+    def pick(q, o, i, by):
+        if q == "s":
+            act(o, i, by=by)
+        else:
+            cp(o, i, by)
 
     def quant2(p, i):
-        op("v", [i], p, lambda: V.quantize_mx(p[0][0], p[1][0], i[0]), 12 + 0.22 * len(i[2]))
+        op("v", [i], p, lambda: V.quantize_mx(p[0][0], p[1][0], i[0]), cost(e=12 + 0.22 * len(i[2])))
 
     def pair(n, a=0, b=None):
         return [A(n + "q", a, b), A(n + "p", a, b)]
@@ -307,11 +419,11 @@ def rank_program(g, core, T, topo):
         quant2(pair(n, a, b), i)
 
     def mm(o, l, r, start=True, stop=True):
-        op("p", l + r, [o], lambda: g.tensor.matmul_mx(o[0], l[0][0], l[1][0], r[0][0], r[1][0], start, stop), 40 + 0.6 * len(r[0][2]))
+        op("p", l + r, [o], lambda: g.tensor.matmul_mx(o[0], l[0][0], l[1][0], r[0][0], r[1][0], start, stop), cost(p=40 + 0.6 * len(r[0][2])))
 
     def iota(o, pattern, base=0, cm=0):
         kw = {} if SCRATCH[o[1]][2] == I4 else {"allow_small_or_imprecise_dtypes": True}
-        op("g", [], [o], lambda: g.iota(o[0], pattern, base, cm, **kw), 130 + 1.66 * len(o[2]))
+        op("g", [], [o], lambda: g.iota(o[0], pattern, base, cm, **kw), cost(e=130 + 1.66 * len(o[2])))
 
     def fill(o, c):
         iota(o, [[0, len(o[2])]], c)
@@ -319,7 +431,7 @@ def rank_program(g, core, T, topo):
     last_dma = {}
 
     def dma(q, sem, total, out, in_, reads, writes, ns=2200):
-        last_dma[q] = op(q, reads, writes, lambda: Q[q].dma_start(out, in_).then_inc(T.sem[sem], 16), ns, (sem, total),
+        last_dma[q] = op(q, reads, writes, lambda: Q[q].dma_start(out, in_).then_inc(T.sem[sem], 16), cost(n=ns), (sem, total),
                          [last_dma[q]] if q in last_dma else [], 60)
 
     def emit():
@@ -346,8 +458,8 @@ def rank_program(g, core, T, topo):
         for sem, val in count.items():
             g.wait_ge(T.sem[sem], val)
 
-    CQ, CQ1, CQ4, CQ41, CG, CS16, CS4, CT4, CQ2, CP, CPO, CH16, CH4, CU4, CQ16 = [A("pc", k, k + 1) for k in range(15)]
-    CZ = A("vec", 255, 256)
+    CQ, CQ1, CQ4, CQ41, CG, CS16, CS4, CT4, CQ2, CP, CPO, CH16, CH4, CU4, CQ16, CL4 = [A("pc", k, k + 1) for k in range(16)]
+    CZ, CB, CY = A("vec", 255, 256), A("tab", 32, 33), A("tab", 33, 34)
     HALVES = ((0, HALF), (HALF, C))
 
     def W(k, a=0, b=NB):
@@ -356,20 +468,25 @@ def rank_program(g, core, T, topo):
     def vec(k, a=0, b=16):
         return A("vec", 16 * k + a, 16 * k + b)
 
+    def back(x):
+        a, b = int(x[2][0]), int(x[2][-1])
+        return (T[x[1]][:, b::-1] if a == 0 else T[x[1]][:, b:a - 1:-1], x[1], x[2])
+
     def keep(row, a, b, dst):
         scan(A("exh", a, b), A("k16", a, b), row, 0.0, OP.mult, OP.add)
         ts(dst, A("exh", a + 15, b, 16), CH16, OP.mult, float(HALF), OP.add)
 
-    def wrap4(row, n, dst, a=0):
+    def wrap4(row, n, dst, a=0, add=CU4):
         scan(A("exh", a, a + n), A("k4", 0, n), row, 0.0, OP.mult, OP.add)
-        ts(dst, A("exh", a + 3, a + n, 4), CH4, OP.mult, CU4, OP.add)
+        ts(dst, A("exh", a + 3, a + n, 4), CH4, OP.mult, add, OP.add)
 
     def hold(dst, row):
         scan(dst, row, A("kx"), -512.0, OP.max, OP.add)
 
     dma("y", "lu", 16, T.ut[:], T.u[:], [], [A("ut")])
-    dma("s", "lx", 32, T.x0[:, 0:2 * C], T.x[:, 0:2 * C], [], [A("x0", 0, 2 * C)], 2500)
-    dma("y", "lx", 32, T.x0[:, 2 * C:4 * C], T.x[:, 2 * C:4 * C], [], [A("x0", 2 * C, 4 * C)], 2500)
+    cut = 4 * PIECE[0][0]
+    dma("s", "lh", 16, T.x0[:, cut:4 * C], T.x[:, cut:4 * C], [], [A("x0", cut, 4 * C)], 2400)
+    dma("y", "lx", 16, T.x0[:, 0:cut], T.x[:, 0:cut], [], [A("x0", 0, cut)], 2500)
     dma("y", "lw", 32, T.wq[:].bitcast(dt.uint8), T.wc[:], [], [A("wq")])
     dma("y", "lw", 32, T.wp[:], T.ws[:], [], [A("wp")])
     dma("y", "lv", 16, T.vt[:], T.v[:], [], [A("vt")])
@@ -382,26 +499,29 @@ def rank_program(g, core, T, topo):
 
     EYE = tab(8)
     iota(pi(0), [[0, 1]], 0, 1)
-    iota(tab(0), [[1, 16]])
+    J16 = A("c16")
+    iota(J16, [[1, 16]])
     iota(A("cw"), [[16, NB]])
-    iota(A("pi", 8, 16), [[16, 8]])
     iota(tab(1), [[0, 4], [1, 4]])
-    iota(A("jw", 14, 42), [[8, NB]])
     iota(A("g32"), [[1, 8], [0, 4]])
     iota(A("tab", 160, 192), [[-1, 2], [0, 16]], 1)
     iota(tab(12), [[1, 4], [-1, 4]])
-    memset(tab(13), 0.0)
-    memset(A("ones"), 1.0)
-    op("g", [A("ones")], [A("em")], lambda: g.affine_select(T.em[:], T.ones[:], [[-1, 528]], OP.is_equal, 0.0, 3, 4), 1100)
+    fill(tab(13), 0)
+    fill(A("ones"), 1)
     memset(A("zz"), 0.0)
+    op("g", [A("zz", 0, 528)], [A("em")], lambda: g.affine_select(T.em[:], T.zz[:, 0:528], [[-1, 528]], OP.not_equal, 1.0, 3, 4), cost(e=1100))
     runs = []
     for kind, lanes, lo, hi, a, _ in TILES:
-        runs.append((a, a + 16 * lanes[-1] - lo) if kind == "d" else (a + 16 * lanes[-1], a + hi))
+        runs.append((a, a + 16 * max(d for d in lanes if d < NV) - lo) if kind == "d" else (a + 16 * lanes[-1], a + hi))
     runs[1] = (LOW, runs[1][1])
     for a, b in reversed(runs):
         dma("y", "lf", 16 * len(runs), T.fl[:, 4 * a:4 * b], T.zz[:, 0:4 * (b - a)], [A("zz", 0, 4 * (b - a))], [A("fl", 4 * a, 4 * b)])
     fill(A("win", 0, 4 * C), 0)
-    iota(A("cnt"), [[1, C + L]])
+    iota(A("cnt", 0, L), [[1, L]], C)
+    iota(A("cnt", L, C), [[-1, C - L]], -L)
+    fill(A("eqr", C, C + 16), 0)
+    fill(A("h3", 1, 48 * NB + 48, 3), -1024)
+    iota(A("k13"), [[0, NB], [1, LT]])
     iota(A("cne"), [[2, C]], -C)
     iota(A("k5"), [[0, 84], [256, 5]])
     fill(A("lh"), 0)
@@ -409,86 +529,80 @@ def rank_program(g, core, T, topo):
     fill(A("el"), 1)
     fill(A("tl"), 0)
     fill(A("nl"), 0)
+    fill(A("gt", C, C + 16), 0)
+    fill(A("lr"), 0)
+    fill(A("sn"), 0)
+    iota(A("ev"), [[0, 16]], 0)
+    iota(A("ev", 0, 1), [[0, 1]], C)
 
-    memset(A("gt", C, C + 16), 0.0)
-    memset(A("rs"), 0.0)
-    memset(A("ev"), 0.0)
-    memset(A("ev", 0, 1), float(C))
-    memset(A("lr"), 0.0)
-    for t in range(R):
-        memset(A("sn%d" % t), 0.0)
     ts(pi(1), pi(0), 15, OP.bitwise_and)
     ts(pi(2), pi(0), 4, OP.arith_shift_right)
     cp(CQ, pi(1))
     ts(pi(3), pi(1), 2, OP.arith_shift_right)
     ts(pi(4), pi(1), 3, OP.bitwise_and)
     ts(A("qo"), A("cw"), 0.0, OP.mult, CQ, OP.add)
-    ts(EYE, tab(0), CQ, OP.is_equal)
-    ts(tab(3), tab(0), CQ, OP.is_gt, 2 * BIG, OP.mult)
-    ts(CQ1, pi(1), 1.0, OP.add)
-    ts(tab(2), EYE, 2 * BIG, OP.mult, -BIG, OP.add)
-    ts(tab(3), tab(3), -BIG, OP.add)
-    act(A("cm"), tab(2), by=A("qo"))
-    act(A("ck"), tab(3), by=A("qo"))
+    ts(EYE, J16, CQ, OP.is_equal)
+    lin(CQ1, CQ, 1.0, 1.0)
+    ts(CB, pi(1), -BIG, OP.mult)
     iota(A("kr"), [[0, NB], [512, 16]])
-    ts(A("kb"), A("kr", 0, LOW), -256.0, OP.add, BIG / 256, OP.mult)
-    ts(tab(4), tab(0), CQ, OP.is_lt, -512.0, OP.mult)
-    ts(tab(5), EYE, 256.0, OP.mult)
-    ts(tab(6), tab(0), 15.0, OP.is_equal, -512.0, OP.mult)
-    ts(tab(7), tab(0), CQ1, OP.is_equal, F, OP.mult)
-    tt(tab(4), tab(4), tab(5), OP.add)
-    ts(tab(0), tab(0), CQ, OP.not_equal)
-    cp(A("ulu"), A("pi", 8, 16))
-    tt(tab(4), tab(4), tab(6), OP.add)
+    act(A("cm"), A("kr"), AF.Abs, CB, BIG / 512)
+    lin(A("kb"), A("kr"), BIG / 256, -BIG)
+    ts(tab(4), J16, CQ, OP.is_lt, -512.0, OP.mult)
+    lin(tab(3), EYE, 256.0, 0.0)
+    ts(tab(7), J16, CQ1, OP.is_equal, F, OP.mult)
+    tt(tab(4), tab(4), tab(3), OP.add)
+    lin(tab(0), EYE, -1.0, 1.0)
+    cp(A("ulu"), A("cw", 0, 8))
+    lin(A("tab", 79, 80), A("tab", 79, 80), 1.0, -512.0)
     tt(tab(7), tab(7), tab(0), OP.max)
     act(A("ky"), tab(4), scale=2.0, by=A("qo"))
     act(A("kx"), tab(4), by=A("qo"))
     act(A("k16"), tab(7), by=A("qo"))
-    memset(A("pf", C, 512), 0.0)
+    fill(A("pf", C, 512), 0)
     ts(CQ16, pi(1), -16.0, OP.add)
     ts(pi(5), pi(1), 1, OP.arith_shift_right)
     cp(CG, pi(2))
     cp(CQ4, pi(3))
-    ts(CQ41, pi(3), 1.0, OP.add)
-    ts(CP, pi(1), 2.0, OP.subtract)
+    lin(CQ41, CQ4, 1.0, 1.0)
+    act(CP, CQ, AF.Abs, -2.0)
     cp(CT4, pi(4))
-    ts(CU4, pi(4), 2.0 * C, OP.add)
+    lin(CU4, CT4, 1.0, 2.0 * C)
+    lin(CL4, CT4, 1.0, 2.0 * C - 4.0 * A0)
     cp(CQ2, pi(5))
-    tt(CP, CP, CP, OP.mult)
-    ts(CS16, pi(1), 15.0, OP.is_equal, 1.0 - 1.0 / F, OP.mult)
     ts(CS4, pi(3), 3.0, OP.is_equal, 4.0 - 4.0 / F, OP.mult)
     ts(CP, CP, 1.0, OP.is_le)
-    ts(CS16, CS16, 1.0 / F, OP.add)
-    ts(CS4, CS4, 4.0 / F, OP.add)
-    ts(CH16, CS16, 0.5, OP.mult)
-    ts(CH4, CS4, 0.5, OP.mult)
+    lin(CH16, A("tab", 143, 144), 0.5 - 0.5 / F, 0.5 / F)
+    lin(CS4, CS4, 1.0, 4.0 / F)
+    lin(CH4, CS4, 0.5, 0.0)
     quant("u", A("ut"))
     op("v", [A("uq"), A("ulu")], [A("urq")], lambda: V.tensor_copy(
-        T.urq[:, 0:128].bitcast(dt.uint32), T.uq[:, 0:128].bitcast(dt.uint32).indirect(T.ulu[:, 0:8])), 240)
-    op("s", [A("up"), A("ulu")], [A("urp")], lambda: S.activation(T.urp[:, 0:128], T.up[:, 0:128].indirect(T.ulu[:, 0:8]), AF.Copy), 225)
+        T.urq[:, 0:128].bitcast(dt.uint32), T.uq[:, 0:128].bitcast(dt.uint32).indirect(T.ulu[:, 0:8])), cost(e=50, g=190))
+    op("s", [A("up"), A("ulu")], [A("urp")], lambda: S.activation(T.urp[:, 0:128], T.up[:, 0:128].indirect(T.ulu[:, 0:8]), AF.Copy), cost(e=65, g=160))
     ts(A("g32"), A("g32"), CG, OP.is_equal, CQ16, OP.mult)
     ts(A("go"), A("g32"), 16.0, OP.add)
     ts(tab(12), tab(12), 0.0, OP.is_equal, CP, OP.mult)
     act(A("cst"), A("tab", 160, 192), by=A("go"))
     act(A("cpt"), A("tab", 192, 224), by=A("go"))
-    ts(CPO, CS4, -C / 4.0, OP.mult)
-    ts(A("jw", 42, 70), A("cw"), CQ, OP.add)
+    lin(CPO, CS4, -C / 4.0, 0.0)
+    lin(A("jw", 42, 70), A("cw"), 1.0, CQ)
     ts(tab(5), tab(1), CQ41, OP.is_equal, F, OP.mult)
     ts(tab(1), tab(1), CQ4, OP.not_equal)
     quant("cp", A("cpt"))
     quant("cs", A("cst"))
+    lin(A("jw", 14, 42), A("cw"), 0.5, CQ2)
     ts(A("cw", NV, NB), A("cw", NV, NB), CQ, OP.subtract, 15.0 + 512.0 - 4096.0, OP.add)
-    ts(A("cw", 0, NV), A("jw", 42, 42 + NV), -1.0, OP.mult, LOW - 1.0 + 512.0 - 4096.0, OP.add)
-    ts(A("cw"), A("cw"), A("ky", 15, 16), OP.add)
-    ts(A("jw", 14, 42), A("jw", 14, 42), CQ2, OP.add)
-    cp(A("jw", 0, 14), A("jw", 42, 56))
-    ts(A("jw", 70, 84), A("jw", 42, 56), float(HALF), OP.add)
-    ts(A("jw", 84, 112), A("jw", 42, 70), -1.0, OP.mult, C - 1.0 + 512.0, OP.add)
+    lin(A("cw", 0, NV), A("jw", 42, 42 + NV), -1.0, LOW - 1.0 + 512.0 - 4096.0)
+    lin(CY, A("tab", 79, 80), 2.0, 0.0)
+    lin(A("cw"), A("cw"), 1.0, CY)
+    lin(A("jw", 0, 14), A("jw", 42, 56), 1.0, 0.0)
+    lin(A("jw", 70, 84), A("jw", 42, 56), 1.0, float(HALF))
+    lin(A("jw", 84, 112), A("jw", 42, 70), -1.0, float(C))
     tt(tab(5), tab(5), tab(1), OP.max)
     act(A("k4", 0, 128), tab(5), by=A("qo", 0, 8))
     act(A("k4", 128, C), tab(5), by=A("qo", 8, NB))
-    ts(A("k6"), A("k6"), 1.0, OP.min)
-    ts(A("k6n"), A("k6"), -1.0, OP.mult, 1.0, OP.add)
+    act(A("k6"), A("k6"), AF.Sign)
+    act(A("k13"), A("k13"), AF.Sign)
+    lin(A("k6n"), A("k6"), -1.0, 1.0)
     quant("v", A("vt"))
     for b in range(4):
         quant2([A("eq4", 128 * b, 128 * b + 128), A("ep4", 128 * b, 128 * b + 128)], A("em", 3 - b, 515 - b))
@@ -504,18 +618,16 @@ def rank_program(g, core, T, topo):
         return [A("eq4", 128 * b, 128 * b + 128), A("ep4", 128 * b, 128 * b + 128)]
 
     JW = A("jw", 42, 70)
-    EH, EN, EU, EM, HH, HM, HN, ST, XV, NN, NH, AH = range(12)
+    EH, EN, EU, EM, HH, HM, HN, ST, XV, NN, NH, AH, SU, EC = range(14)
 
     def brackets(K):
-        k1 = K - 1
         ev = A("ev")
-        cp(A("ei"), ev)
-        ts(vec(EN), ev, -1.0, OP.mult)
-        ts(vec(EU), ev, -0.5, OP.add)
-        ts(A("ei"), A("ei"), 1, OP.arith_shift_right)
+        ts(A("ei"), ev, 0.5, OP.mult, -0.25, OP.add)
+        lin(vec(EN), ev, -1.0, 0.0)
+        lin(vec(EU), ev, 1.0, -0.5)
         cp(vec(HH), A("ei"))
-        ts(vec(HN), A("ei"), -1.0, OP.mult, 0.5, OP.add)
-        ts(vec(HM), A("ei"), -float(HALF), OP.add)
+        lin(vec(HN), vec(HH), -1.0, 0.5)
+        lin(vec(HM), vec(HH), 1.0, -float(HALF))
         for k in range(1, K):
             s = A("sgn", 42 * (k - 1), 42 * k)
             act(s, A("jw", 0, 42), AF.Sign, bias=vec(HN, k, k + 1))
@@ -534,15 +646,21 @@ def rank_program(g, core, T, topo):
         tt(W(4), W(4), W(3), OP.mult)
         tt(W(7), W(4), W(2), OP.add)
         cp(A("fw"), W(7))
-        act(A("fr", P0, C), A("cne"), by=A("fw", B0, NB))
+        act(A("fr"), A("cne"), by=A("fw"))
         for k in range(1, K):
             act(A("el", k - 1, LN * NB, LN), JW, AF.Abs, bias=vec(EN, k, k + 1))
             act(A("sge", 32 * k, 32 * k + NB), JW, AF.Sign, bias=vec(EU, k, k + 1), scale=-1.0)
         scan(A("eo"), A("k6n"), A("el"), 1.0, OP.max, OP.min)
         cp(A("eqw"), A("eo", LN - 1, LN * NB, LN))
-        act(A("eqr"), A("cnt", 0, 16), by=A("eqw"))
-        ts(vec(EH), vec(HH), -2.0, OP.mult)
-        ts(vec(EM), vec(HH), -float(C), OP.add)
+        act(A("eqr", 0, C), A("c16"), by=A("eqw"))
+        lin(vec(EC), ev, -1.0, float(C))
+        for k in range(1, K):
+            act(A("nl", k, LN * NB, LN), A("sge", 32 * k, 32 * k + NB), scale=vec(EC, k, k + 1))
+        scan(A("no"), A("k6"), A("nl"), 0.0, OP.mult, OP.max)
+        tt(A("wd", 1, 3 * NB, 3), A("jw", 84, 112), A("no", LN - 1, LN * NB, LN), OP.subtract)
+        lin(A("wd", 2, 3 * NB, 3), A("no", LN - 1, LN * NB, LN), 1.0, 255.0 - 2048.0)
+        lin(vec(EH), vec(HH), -2.0, 0.0)
+        lin(vec(EM), vec(HH), 1.0, -float(C))
         tt(vec(EH), vec(EH), ev, OP.add)
         tt(vec(EM), vec(EM), EYE, OP.mult)
         tt(vec(EH), vec(EH), vec(EM), OP.mult)
@@ -550,67 +668,87 @@ def rank_program(g, core, T, topo):
         ts(A("xi", 0, 1), CZ, float(C), OP.add)
         tt(vec(ST), vec(HH), ev, OP.subtract)
         tt(vec(ST, 0, 8), vec(ST, 0, 8), vec(HH, 1, 9), OP.subtract)
-        ts(vec(ST, 0, 8), vec(ST, 0, 8), float(C), OP.add)
+        scan(back(vec(SU)), back(vec(ST)), A("cwc"), 0.0, OP.add, OP.add)
 
+    PART["cwc"] = ("tab", 144, 16)
+    fill(A("cwc"), C)
+
+    def quant_x(xb):
+        for a, b in PIECE:
+            quant("x", A(xb, 4 * a, 4 * b), a, b)
+
+    quant_x("x0")
+    sends, sent = [], {}
     for t in range(R):
         K = 4 + t
         xb = "x0" if t == 0 else "xs"
-        sq, sp, sn, an = "sq%d" % t, "sp%d" % t, "sn%d" % t, "an%d" % t
-        if t == 0:
-            quant("x", A(xb))
+        sn, an = (lambda a=0, b=8, t=t: A("sn", 8 * t + a, 8 * t + b)), (lambda a=0, b=8, t=t: A("an", 8 * t + a, 8 * t + b))
+        for k, (a, b) in enumerate(PIECE[:-1]):
+            mm(bank(5 + k, b - a), pair("ur"), pair("x", a, b))
+        mm(bank(1, C - 16), pair("ur"), pair("x", 0, C - 16))
         mm(bank(0, C), pair("ur"), pair("x"))
-        mm(bank(1, C), pair("ur"), pair("x"))
+        for k, (a, b) in enumerate(PIECE):
+            tt(A("yy", a, b), bank(5 + k, b - a) if k + 1 < len(PIECE) else bank(0, b, a), A("cm", a, b), OP.subtract)
+            scan(A("hd", a, b), A("kb", a, b), A("yy", a, b), -BIG, OP.min, OP.max)
+            if a < LOW:
+                b = min(b, LOW)
+                scan(back(A("hx", a, b)), A("kb", 0, b - a), back(A("hd", a, b)), -BIG, OP.min, OP.max)
         if t == 0:
             mm(bank(7, C), pair("u"), pair("x"))
-            act(A("sg", SG, SG + C), bank(7, C), AF.Sign)
-            act(A("pf", 0, C), A("sg", SG, SG + C), AF.Relu)
+            ts(A("pf", 0, C), bank(7, C), 0.0, OP.is_gt)
             quant("pf", A("pf"))
             mm(bank(5, 128), pair("cp"), pair("pf"))
             scan(A("ex0"), A("k4", 0, C // 4), bank(5, C // 4), 0.0, OP.mult, OP.add)
-            ts(A("poff"), A("ex0", 3, C // 4, 4), CPO, OP.mult, float(C * (K - 1)), OP.add)
+            lin(A("poff"), A("ex0", 3, C // 4, 4), CPO, float(C * (K - 1)))
             for k in range(1, K):
-                ts(A("pf", NB * k, NB * (k + 1)), A("ex0", 3, C // 4, 4), CS4, OP.mult, 4.0 * k - 2.0, OP.is_ge)
+                act(A("pf", NB * k, NB * (k + 1)), A("ex0", 3, C // 4, 4), AF.Sign, 2.0 - 4.0 * k, CS4)
             quant("pf", A("pf"))
-            mm(bank(6, 128), pair("cs"), pair("pf"))
+            mm(bank(7, 128), pair("cs"), pair("pf"))
             for k in range(1, K):
-                total_of(A("ev", k, k + 1), bank(6, NB // 4 * (k + 1), NB // 4 * k))
+                act(W(11, 0, NB // 4), bank(7, NB // 4 * (k + 1), NB // 4 * k), AF.Identity, 2.0 * C / NB, 0.5, A("ev", k, k + 1))
             brackets(K)
-        for a, b in ((LOW, C), (0, LOW)):
-            tt(A("yy", a, b), bank(0, b, a), A("cm", a, b), OP.min)
-        for a, b in ((LOW, C), (0, LOW)):
-            scan(A("hd", a, b), A("ck", a, b), A("yy", a, b), -BIG, OP.min, OP.max)
-        back = (T.hx[:, LOW - 1::-1], "hx", np.arange(LOW)), (T.hd[:, LOW - 1::-1], "hd", np.arange(LOW))
-        scan(back[0], A("kb"), back[1], -BIG, OP.min, OP.max)
         o, late = 0, None
         chain["s"] = []
         for kind, lanes, lo, hi, a, q0 in TILES:
-            for k, d in enumerate(lanes if kind == "b" else ()):
+            for k, d in enumerate(lanes):
+                if d < NV:
+                    continue
                 h = A("sg", o, o + 16 * d)
                 o += 16 * d
                 act(h, bank(1, 16 * d), AF.Sign, bias=A("hd", 16 * d + 15, 16 * d + 16), scale=-1.0)
                 if late:
                     act(*late)
                 late = (A("fl", 4 * a + k, 4 * (a + 16 * d), 4), h, AF.Relu, None, 1.0, A("rs", d, d + 1))
-        act(*late)
+        o -= 16 * d
+        act(A("fl", 4 * a + k, 4 * (a + SPL), 4), A("sg", o, o + SPL), AF.Relu, acc=A("rs", d, d + 1))
+        act(A("fl", 4 * (a + SPL) + k, 4 * (a + 16 * d), 4), A("sg", o + SPL, o + 16 * d), AF.Relu, acc=A("rs", NB, NB + 1))
         chain.pop("s")
+        last_row = d
 
         def sums(m):
             kind, lanes, lo, hi, a, q0 = TILES[m]
-            quant("fl", A("fl", 4 * a, 4 * (a + hi - lo)), q0 + lo, q0 + hi)
+            for c, e in ((lo, SPL), (SPL, hi)) if m == SUMS[-1] else ((lo, hi),):
+                quant("fl", A("fl", 4 * (a + c - lo), 4 * (a + e - lo)), q0 + c, q0 + e)
             if kind == "d":
                 for k, d in enumerate(lanes):
+                    if d >= NV:
+                        continue
                     first = m == SUMS[0] and k == 0
                     n = LOW if first else max(128, LOW - 16 * d)
                     mm(bank(3, n), E(k), pair("fl", q0 + 16 * d, q0 + 16 * d + n), first, d == LAST_D)
                 if m == 0:
                     mm(bank(4, C - LOW), E(0), pair("fl", q0 + LOW, q0 + C))
             hi = C if m == SUMS[0] else hi
-            mm(bank(2, hi), pair("cs"), pair("fl", q0, q0 + hi), m == SUMS[0], m == SUMS[-1])
+            if lo < SPL:
+                mm(bank(2, SPL), pair("cs"), pair("fl", q0, q0 + SPL), m == [x for x in SUMS if TILES[x][2] < SPL][0], m == SUMS[-1])
+            mm(bank(6, hi - SPL), pair("cs"), pair("fl", q0 + SPL, q0 + hi), m == SUMS[0], m == SUMS[-1])
 
         late = []
         for m in SUMS:
             kind, lanes, lo, hi, a, q0 = TILES[m]
-            for k, d in enumerate(lanes if kind == "d" else ()):
+            for k, d in enumerate(lanes):
+                if d >= NV:
+                    continue
                 e = C if d == 0 else LOW
                 tt(A("fl", 4 * (a + 16 * d - lo) + k, 4 * (a + e - lo), 4), bank(0, e, 16 * d), A("hx" if d else "hd", 0, e - 16 * d), OP.is_le)
                 while late:
@@ -623,10 +761,12 @@ def rank_program(g, core, T, topo):
         scan(A("xr", LOW, C), A("kr", LOW, C), bank(4, C - LOW), 0.0, OP.min, OP.add)
         scan(A("xr", 0, LOW), A("kr", 0, LOW), bank(3, LOW), 0.0, OP.min, OP.add)
         tt(A("base"), A("cw"), A("poff"), OP.add)
-        tt(A("base"), A("base"), A("rs"), OP.subtract)
+        tt(A("base", NV, NB), A("base", NV, NB), A("rs", NV, NB), OP.subtract)
         tt(A("ky", 15, C, 16), A("base"), A("xr", 15, C, 16), OP.subtract)
-        for a, b in HALVES:
-            scan(A("ex", a, b), bank(2, b, a), A("ky", a, b), -1024.0, OP.max, OP.add)
+        y = A("ky", 16 * last_row + 15, 16 * last_row + 16)
+        ts(y, y, A("rs", NB, NB + 1), OP.subtract)
+        for k, a, b in ((2, 0, SPL), (6, SPL, C)):
+            scan(A("ex", a, b), bank(k, b - a), A("ky", a, b), -1024.0, OP.max, OP.add)
             ts(A("o1", a // 16, b // 16), A("ex", a + 15, b, 16), 4096.0, OP.add)
         n = K * C
         scatter(A("win", 0, n), A("o1"), A("ones", 0, C))
@@ -647,8 +787,9 @@ def rank_program(g, core, T, topo):
             tt(A("zt", 16 * a, 16 * b), A("xh"), A("bh", 16 * a, 16 * b), OP.add, by=A("ab4", a, b))
         for k in range(2):
             act(A("xn", C * k, C * k + C), A(xb), by=A("ab4", NB * k, NB * k + NB))
-            act(A("bb", C * k, C * k + C), A("bh", C * k, C * k + C), scale=2.0)
-        qz, qh = [A("zq"), A(sp, L, L + HALF)], [A("hq"), A(sp, L + HALF, L + C)]
+            lin(A("bb", C * k, C * k + C), A("bh", C * k, C * k + C), 2.0, 0.0, CFG["bb"])
+        p0 = t * SPW
+        qz, qh = [A("zq"), A("sp", p0 + NS, p0 + NS + HALF)], [A("hq"), A("sp", p0 + NS + HALF, p0 + SPW)]
         quant2(qz, A("zt"))
         for b in range(4):
             mm(bank(3 + b, HALF), pair("w", 128 * b, 128 * b + 128), qz)
@@ -660,98 +801,102 @@ def rank_program(g, core, T, topo):
         mm(bank(7, HALF), pair("ur"), qh)
         ts(A("gt", 0, HALF), bank(0, HALF), 0.0, OP.is_le)
         act(A("gt", HALF, C), bank(7, HALF), AF.Sign)
-        op("g", [A("ht"), A("xn", 0, 2 * C)], [A("xn", 0, 2 * C)],
-           lambda: g.dma_start(T.xn[:, 0:2 * C], T.ht[:], accum_op=OP.add).then_inc(T.sem.acc, 16), 3500, ("acc", 16 * t + 16), (), 1000)
-        for a in range(0, 2 * C, L):
-            tt(A("xn", 2 * C + a, 2 * C + a + L), A("bb", a, a + L), A("ht", a, a + L), OP.subtract)
-        act(vec(XV), A("gt"), by=A("xi", 0, 1))
-        tt(vec(NN, 0, 8), vec(XV, 0, 8), vec(XV, 1, 9), OP.subtract)
-        tt(A(sn, 0, 8), vec(NN, 0, 8), vec(ST, 0, 8), OP.add)
-        rid, pid = topo.addr(relays[2], core)
-        s2 = op("g", [A(sn)], [], lambda a=(T["rn%d" % t][:, 0:8], T[sn][:, 0:8], T.sem["hop%d" % t], T.sem.sent, pid, rid,
-                                            topo.mask(core, relays[2])): g.remote_dma(*a), 300, ("sent", 32 * R))
-        act(A("gb", HALF, C), A("gt"), AF.Relu, by=A("fw", 14, NB))
-        ts(A("gb", 0, HALF), A("gt"), 0.5, OP.is_gt, by=A("fw", 0, 14))
-        for k in range(K):
-            act(A("nl", k, LN * NB, LN), A("ones", 0, NB) if k == 0 else A("sge", 32 * k, 32 * k + NB), scale=A(sn, k, k + 1))
-        scan(A("la"), A("eqr"), A("gb"), 0.0, OP.mult, OP.add)
-        hold(A("exb", C, 2 * C), A("gb"))
-        hold(A("exb", 0, C), A("la"))
-        scan(A("no"), A("k6"), A("nl"), 0.0, OP.mult, OP.max)
-        la, lost = A("exb", 15, C, 16), A("exb", C + 15, 2 * C, 16)
-        ts(W(9), lost, 256.0, OP.add, -1024.0, OP.mult)
-        tt(W(9), W(9), A("jw", 84, 112), OP.add)
-        tt(W(10), A("no", LN - 1, LN * NB, LN), la, OP.subtract)
-        tt(W(9), W(9), la, OP.add)
-        tt(W(8), W(9), W(10), OP.max)
-        ts(A("jlw"), W(8), -256.0, OP.add)
+        if CFG["add"] == "dma":
+            sends.append(op("g", [A("ht"), A("xn", 0, 2 * C)], [A("xn", 0, 2 * C)],
+                            lambda: g.dma_start(T.xn[:, 0:2 * C], T.ht[:], accum_op=OP.add).then_inc(T.sem.acc, 16), cost(n=NET["add"]),
+                            ("acc", 16 * t + 16), sends[-1:], 1000))
+        else:
+            for a in range(0, 2 * C, L):
+                tt(A("xn", a, a + L), A("xn", a, a + L), A("ht", a, a + L), OP.add)
+        for a, b in zip(CFG["bh"], CFG["bh"][1:]):
+            tt(A("xn", 2 * C + a, 2 * C + b), A("bb", a, b), A("ht", a, b), OP.subtract)
+
+        def send(x, reads, call, arrives, n):
+            s = op("g", reads, [], call, cost(n=300), SENT, [sent[dict(a="b", l="n")[x]]] if x in "al" else [])
+            sends.append(s)
+            sent[x] = s
+            op("net", [], arrives, None, cost(n=NET[x]), ("a%s%d" % (x, t), n), [s], 0)
+
+        def small(x, w):
+            rid, pid = topo.addr(relays[0], core)
+            a = (T["r" + x][:, w * t:w * t + w], T["s" + x][:, w * t:w * t + w], T.sem["h%s%d" % (x, t)], T.sem.sent, pid, rid, topo.mask(core, relays[0]))
+            send(x, [A("s" + x, w * t, w * t + w)], lambda: g.remote_dma(*a), [A("a" + x, w * t, w * t + w)], n_in[0])
+
+        for x, banks in (("b", (3, 4, 5, 6)), ("a", (0, 1, 2, 7))):
+            a, b = PIECES[x]
+            quant2([A("sq", t * NS + a, t * NS + b), A("sp", p0 + a, p0 + b)], A("xn", 4 * (A0 + a), 4 * (A0 + b)))
+            tr, w = [], 2 * (b - a)
+            for k in (1, 2, 3):
+                rid, pid = topo.addr(relays[k], core)
+                c, d = _share(k, x, t)
+                if k < 3:
+                    src, dst = T.sq[:, c:d].bitcast(dt.uint8), T.rq[:, c:d].bitcast(dt.uint8)
+                else:
+                    src, dst = T.sp[:, p0 + a:p0 + a + w], T.rp[:, 2 * (t * NS + a):2 * (t * NS + a) + w]
+                engs = topo.engines(core, relays[k])
+                tr.append(RemoteDMATransfer(dst_ids=[DstId(rid=rid, pnc=pid)], dma_engine_mask=_mask((engs[1::4], engs[0::4], engs[2::4])[k - 1]),
+                                            remote_sem=T.sem["h%s%d" % (x, t)], src=src, dst=dst))
+            came = [A("aq", t * NS + a, t * NS + b), A("ap", t * NS + a, t * NS + b)]
+            send(x, [A("sq", t * NS + a, t * NS + b), A("sp", p0 + a, p0 + a + w)],
+                 lambda tr=tr: g.remote_dma_fused(tr, local_sem=T.sem.sent), came, sum(n_in[1:]))
+            for k in range(4):
+                mm(bank(banks[k], b - a), E(k), came)
+                (act if CFG.get("un", "ssss")[k] == "s" else cp)(A("dn", 4 * a + k, 4 * b, 4), bank(banks[k], b - a))
+        tt(vec(XV), A("gt"), vec(SU), OP.add, by=A("xi", 0, 1))
+        tt(sn(), vec(XV, 0, 8), vec(XV, 1, 9), OP.subtract)
+        small("n", 8)
+        gv = CFG["gv"]
+        act(A("gb", 16 * gv, C), A("gt"), AF.Relu, by=A("fw", gv, NB))
+        if gv:
+            ts(A("gb", 0, 16 * gv), A("gt"), 0.5, OP.is_gt, by=A("fw", 0, gv))
+        scan(A("la"), A("eqr", 0, C), A("gb"), 0.0, OP.mult, OP.add)
+        scan(back(A("lb")), back(A("eqr", 1, C + 1)), back(A("gb")), 0.0, OP.mult, OP.add)
+        hold(A("exb"), A("gb"))
+        hold(A("h3", 0, 3 * C, 3), A("la"))
+        hold(A("h3", 32, 3 * C + 32, 3), A("lb"))
+        lin(A("wd", 0, 3 * NB, 3), A("exb", 15, C, 16), -1024.0, -1024.0 * 256.0, CFG["mg"])
+        scan(A("wo"), A("h3", 45, 45 + 48 * NB, 16), A("wd"), -4096.0, OP.max, OP.add)
+        ts(A("jlw"), A("wo", 2, 3 * NB, 3), 2048.0, OP.add)
         scatter(A("lr"), A("jlw", B0, NB), A("fr", P0, C))
         for k in range(2):
-            wrap4(A("lr", 64 * k, 64 * k + 64), 64, A("l4", 16 * k, 16 * k + 16), 64 * k)
-        act(A("st", 0, 2 * L), A("xn", 0, 4 * C), by=A("l4", 0, 16))
-        cp(A("st", 2 * L, 4 * L), A("xn", 0, 4 * C), by=A("l4", 16, 32))
-        quant2([A(sq), A(sp, 0, L)], A("st"))
-        tr = []
-        for k in range(2):
-            rid, pid = topo.addr(relays[k], core)
-            if k == 0:
-                src, dst = T[sq][:, 0:L].bitcast(dt.uint8), T["rq%d" % t][:, 0:L].bitcast(dt.uint8)
-            else:
-                src, dst = T[sp][:, 0:4 * L], T["rp%d" % t][:, 0:4 * L]
-            tr.append(RemoteDMATransfer(dst_ids=[DstId(rid=rid, pnc=pid)], dma_engine_mask=_mask(topo.engines(core, relays[k])[8 * k:8 * k + 8]),
-                                        remote_sem=T.sem["hop%d" % t], src=src, dst=dst))
-        s1 = op("g", [A(sq), A(sp)], [], lambda tr=tr: g.remote_dma_fused(tr, local_sem=T.sem.sent), 300, ("sent", 32 * R), [s2])
-        tt(W(5), W(8), W(7), OP.subtract)
-        ts(W(6), W(8), L + 256.0, OP.is_lt)
-        ts(W(5), W(5), C - 256.0, OP.add)
-        tt(W(5), W(5), W(6), OP.mult)
-        tt(W(5), W(5), W(7), OP.add)
-        cp(A("m2w"), W(5))
-        cp(A("m2r"), A("cnt"), by=A("m2w"))
-        cp(A("nxr"), A("m2r"), by=A("plw"))
+            wrap4(A("lr", 64 * k, 64 * k + 64), 64, A("sl", 32 * t + 16 * k, 32 * t + 16 * k + 16), 64 * k, CL4)
+        small("l", 32)
+        act(A("m2r"), A("cnt"), by=A("jlw"))
+        act(A("slc"), A("fr"), AF.Identity, float(HALF), 0.5, by=A("plw"))
+        tt(A("nxr"), A("m2r"), A("slc"), OP.max, by=A("plw"))
         scan(A("ex"), A("k4"), A("nxr"), 0.0, OP.mult, OP.add)
         ts(A("nx4"), A("ex", 3, C, 4), CS4, OP.mult, CT4, OP.add)
-        op("net", [A(sn)], [A(an)], None, 3500, ("arn%d" % t, n_in[2]), [s2], 0)
-        ts(vec(NH, 0, 8), A(sn), -1.0, OP.mult, 0.5, OP.add)
-        ts(vec(AH, 0, 8), A(an), -1.0, OP.mult, 0.5, OP.add)
+        act(A("pcol"), A("m2r"), by=A("plw"))
+        scan(A("xr"), A("k16"), A("pcol"), 0.0, OP.mult, OP.add)
+        lin(W(8), A("xr", 15, C, 16), CH16, 0.0)
+        lin(vec(NH, 0, 8), sn(), -1.0, 0.5)
+        lin(vec(AH, 0, 8), an(), -1.0, 0.5 - C)
         for k in range(K):
-            act(A("tl", k, LN * 8, LN), A("jw", 42, 50), AF.Sign, bias=vec(AH, k, k + 1))
-            act(A("tl", LN * 8 + k, LN * NB, LN), A("jw", 50, 70), AF.Sign, bias=vec(NH, k, k + 1))
-        scan(A("to"), A("k6"), A("tl"), 0.0, OP.mult, OP.add)
-        ts(A("ttw"), A("to", LN - 1, LN * NB, LN), 0.5, OP.mult, K / 2.0, OP.add)
-        act(A("ttr"), A("cnt", 0, 16), by=A("ttw"))
-        act(A("ptp"), A("ttr"), by=A("jlw"))
+            act(A("tl", k, LT * NB, LT), W(8), AF.Sign, vec(AH, k, k + 1), 2.0)
+            act(A("tl", LN + k, LT * NB, LT), W(8), AF.Sign, vec(NH, k, k + 1), -2.0)
+        scan(A("to"), A("k13"), A("tl"), 0.0, OP.mult, OP.add)
         if t + 1 < R:
-            act(A("ptr"), A("ptp"), by=A("plw"))
-            hold(A("exb", 0, C), A("ptr"))
-            ts(A("poff"), A("exb", 15, C, 16), -float(C), OP.mult, float(C * (K - 256)), OP.add)
-            ts(vec(NN, 0, 8), A(sn), float(L), OP.max, -1.0, OP.mult)
-            ts(vec(NN, 8, 16), A(an), float(L), OP.min, -float(C + L), OP.add)
+            lin(A("poff"), A("to", LT - 1, LT * NB, LT), -C / 2.0, 0.0)
+            ts(vec(NN, 0, 8), sn(), float(L), OP.max, -1.0, OP.mult)
+            ts(vec(NN, 8, 16), an(), float(L), OP.min, -float(C + L), OP.add)
             tt(A("ev", 1, K + 1), vec(NN, 0, K), vec(NN, 8, 8 + K), OP.subtract)
             brackets(K + 1)
         else:
-            act(A("pout"), A("ptp"), by=A("plw"))
-        came = [A("aq%d" % t), A("ap%d" % t)]
-        op("net", [A(sq)], came, None, 3900, ("arc%d" % t, n_in[0] + n_in[1]), [s1], 0)
-        for b in (0, 2, 1, 3):
-            mm(bank(3 + b, L), E(b), came)
-        for b in range(2):
-            cp(A("xn", 4 * C + b, 4 * (C + L), 4), bank(3 + b, L))
-            act(A("xn", 4 * C + 2 + b, 4 * (C + L), 4), bank(5 + b, L))
-        act(A("xs", 4 * XV_, 4 * C), A("xn"), by=A("nx4", XV_ // 4, 4 * NB))
-        cp(A("xs", 0, 4 * XV_), A("xn"), by=A("nx4", 0, XV_ // 4))
-        quant("x", A("xs", 0, 4 * XV_), 0, XV_)
-        quant("x", A("xs", 4 * XV_, 4 * C), XV_, C)
+            ts(A("ttw"), A("to", LT - 1, LT * NB, LT), 0.5, OP.mult, float(K), OP.add)
+            act(A("pout"), A("c16"), by=A("ttw"))
+        for k, q in enumerate("sv"):
+            pick(q, A("xn", 4 * C + 2 * L * k, 4 * C + 2 * L * (k + 1)), A("dn"), A("al", 32 * t + 16 * k, 32 * t + 16 * k + 16))
+        for q, a, b in SHARE:
+            pick(q, A("xs", 4 * a, 4 * b), A("xn"), A("nx4", a // 4, b // 4))
+        quant_x("xs")
 
-    total = 16 * 8
-    mid = (XV_ + C) // 2
-    for k, (a, b) in enumerate(((0, XV_), (XV_, mid), (mid, C))):
-        mm(bank(k, b - a), pair("v"), pair("x", a, b))
-        (cp if k == 2 else act)(A("yo", a, b), bank(k, b - a))
-    dma("y", "out", total, T.pts[:], T.pout[0:128:16, :], [A("pout")], [])
+    total = 16 * (6 + len(PIECE))
     dma("y", "out", total, T.oc[:], T.xq[:].bitcast(dt.uint8), [A("xq")], [])
-    for k in range(4):
-        dma("y", "out", total, T.osc[4 * k:4 * k + 4, :], T.xp[32 * k:32 * k + 4, :], [A("xp")], [])
-    dma("s", "out", total, T.y[:, 0:mid], T.yo[:, 0:mid], [A("yo", 0, mid)], [])
-    dma("y", "out", total, T.y[:, mid:C], T.yo[:, mid:C], [A("yo", mid, C)], [])
+    for m in range(4):
+        dma("y", "out", total, T.osc[4 * m:4 * m + 4, :], T.xp[32 * m:32 * m + 4, :], [A("xp")], [])
+    dma("y", "out", total, T.pts[:], T.pout[0:128:16, :], [A("pout")], [])
+    for k, (a, b) in enumerate(PIECE):
+        mm(bank(k, b - a), pair("v"), pair("x", a, b))
+        (act if k < 2 else cp)(A("yo", a, b), bank(k, b - a))
+        dma("sy"[k // 2], "out", total, T.y[:, a:b], T.yo[:, a:b], [A("yo", a, b)], [])
     emit()

@@ -1,3 +1,4 @@
+import math
 import numpy as np
 from concourse.bass import DstId, RemoteDMATransfer
 from concourse.mybir import dt, AluOpType, ActivationFunctionType, AxisListType
@@ -9,61 +10,74 @@ NV = 19
 LOW = 16 * NV
 B0 = (C - HALF - L) // 16
 P0 = 16 * B0
-A0 = P0 // 2
+A0 = P0
 NA, NS = HALF - A0, C - A0
-SHARE = [("v", LOW, C), ("s", 0, 128), ("v", 240, LOW), ("s", 128, 240)]
-PIECE = [(LOW, C), (0, 128), (128, LOW)]
-CFG = dict(add="dma", bb="v", un="svsv", lin="s", mg="s", ky="s", gv=6, bh=(0, 320, 448, 576, 896))
+SHARE = [("s", 0, 0, C), ("v", 2, 0, C), ("s", 1, 0, C), ("v", 3, 0, C)]
+PIECE = [(LOW, C), (0, LOW)]
+RUNS = [(A0, HALF, A0), (0, A0, 0)]
+ZP = ((24, 32), (32, 44), (44, 56), (0, 16), (16, 24))
+CFG = dict(bb="s", un="svsv", lin="s", mg="s", gv=14, ht=("vsvs", "vsvs"), bh=(0, 384, 640, 896), zb="vssss")
+BEHIND = dict(a="b", l="n", b="n"), dict(a="b", l="n")
 BIG = 2.0 ** 80
 F = 2.0 ** 21
 LN = 6
 LT = 2 * LN
 X4, B2, F4, I4, U2, U1 = "float8_e4m3fn_x4", "bfloat16", "float32", "int32", "uint16", "uint8"
 
-TILES = []
-_a = 0
-_x = (NB - NV) % 4
-_lanes = list(range(4 - _x)) + list(range(NV, NV + _x)) + list(range(4 - _x, NV)) + list(range(NB - 1, NV + _x - 1, -1))
-for _m in range(0, NB, 4):
-    _l = _lanes[_m:_m + 4]
-    _kind = "d" if _l[0] < NV else "b"
-    _hi = (C if _m == 0 else LOW) if _kind == "d" else 16 * _l[0]
-    _lo = min(16 * _l[0], _hi - 128) if _kind == "d" else 0
-    TILES.append([_kind, _l, _lo, _hi, _a, 0])
-    _a += _hi - _lo
-FLW = _a
-ND = (NV + 3) // 4
-PAD = 64
-FLQ = 0
-for _m in list(range(ND - 1, -1, -1)) + list(range(ND, len(TILES))):
-    TILES[_m][5] = FLQ
-    FLQ += TILES[_m][3] + (PAD if _m == ND - 1 else 0)
-SUMS = (4, 3, 0, 1, 5, 2, 6)
-LAST_D = [_d for _m in SUMS for _d in TILES[_m][1] if _d < NV][-1]
+W4, ND = C // 4, NV // 2
+WR = 4 * ND
+GAP = max(W4 - 4 * NV, WR)
+DIAG = [(5, 0), (9, 1), (8, 2), (7, 3), (6, 4)]
+ROWS = [(27, 19), (26, 25), (24, 23), (22, 21), (20,)]
+VROWS = ((), (19,), (19,))
+VORD = "yh hh yl 0b hl 19a p1 hx 0a p2 5a 5b 9a s0 p3 9b 1a 1b s5 8a s1 8b 2a 2b p4 7a s2 7b s6 3a 3b 6a s3 6b 4a 4b s7 s4 s8 s9".split()
+
+
+def _long(x):
+    return 4 * x if x >= NV else 4 * NV if x else W4
+
+
+GROUPS, ZERO, FLQ = [], [], 0
+_at, _room = max(WR - 4 * _g[0] for _g in DIAG), []
+ZERO.append((0, _at))
+for _k in range(3):
+    _b = _at + 4 * NV + GAP
+    _room.append((_at, _b))
+    ZERO += [(_at + 4 * NV, _b), (_b + (W4 if _k == 2 else 4 * NV), _b + 128)]
+    _at = _b + 128
+for _k, _g in enumerate(DIAG + ROWS):
+    if _g[0] < NV:
+        _a, _pre = _room[2 if _g[-1] == 0 else _k % 2], WR - 4 * _g[0]
+    else:
+        _a, _pre = tuple(_at + W4 * _i for _i in range(len(_g))), 0
+        ZERO += [(_x + 4 * _b, _x + (128 if _b == _g[-1] else W4)) for _x, _b in zip(_a, _g)]
+        _at = _a[-1] + 128
+    GROUPS.append((_g, _a, tuple(FLQ + _pre + _x - _a[0] for _x in _a), _pre, 128 - _long(_g[-1])))
+    FLQ += _pre + _a[-1] - _a[0] + 128
+FLW = _at
 SG = sum(16 * b for b in range(NV, NB))
-SPL = LOW - 128
 
 _S = {
-    B2: dict(x0=4 * C, xs=4 * C, xh=4 * C, ut=512, vt=512, em=528, ones=C, cst=512, cpt=512, pf=512, fl=4 * FLW, zz=4 * 256,
-             cm=C, k16=C, k4=C, kx=C, kr=C, kb=C, k5=420, k6=LN * NB, k6n=LN * NB, sg=SG + C, sgn=256, sge=256, exb=C, exh=C,
-             h3=48 * NB + 48, lb=C, win=6 * C, so=6 * C, cne=C, eqr=C + 16, lh=420, lo=420, bh=2 * C, bb=2 * C, zt=2 * C, ht=2 * C, xn=4 * (C + L), gt=C + 16,
-             gb=C, la=C, dn=4 * NS, plr=C, orow=C, abr=C, fr=C, lr=C, el=LN * NB, eo=LN * NB, tl=LT * NB, to=LT * NB,
-             k13=LT * NB),
-    F4: dict(pc=16, tab=224, g32=32, ex0=C // 4, cnt=C, c16=16, slc=C, jw=112, cw=NB, ky=C, yy=C, hd=C, hx=LOW, rs=NB + 4, poff=NB, base=NB, wf=512, ex=C, xr=C, ev=16, vec=256,
-             nl=LN * NB, no=LN * NB, m2r=C, pcol=C, wd=3 * NB, wo=3 * NB, nxr=C, pout=C, yo=C),
+    B2: dict(x0=4 * C, xs=4 * C, xh=4 * C, ut=512, vt=512, em=528, eye=512, ones=C, cst=512, cpt=512, pf=512, fl=4 * FLW, zz=528,
+             cm=C, k16=C, k4=HALF, kx=C, kr=C, kr4=W4, kb4=W4 - 4 * NV, kb=C, k5=420, k6=LN * NB, sg=SG, sgn=256, sge=256, exb=C, exh=C, exs=C,
+             h3=48 * NB + 48, lb=C, win=6 * C, so=6 * C, cne=C, eqr=C + 32, lh=420, lo=420, bh=2 * C, bb=2 * C, zt=2 * C, ht=2 * C,
+             xn=4 * (C + L), gt=C + 16, gb=C, la=C, dn=4 * NS, plr=C, orow=C, abr=C, fr=C, lr=C, slc=C, tl=LT * NB, to=LT * NB, k13=LT * NB),
+    F4: dict(pc=24, tab=256, g32=32, ex0=W4, cnt=C, c16=16, jw=112, cw=NB, ky=W4, yy=C, hd=C, hx=LOW, rs=NB + 4, base=NB, wf=512,
+             ex=C, xr=W4, xb=W4, ev=40, eq=48, vec=256, wi=112, wm=56, wn=56,
+             nl=LN * NB, no=LN * NB, m2r=C, pcol=C, wd=3 * NB, wo=3 * NB, pout=C, yo=C),
     I4: dict(pi=16, ei=16),
-    U2: dict(ulu=8, go=32, qo=NB, o1=NB, plw=NB, fiw=NB, fw=NB, jlw=NB, eqw=NB, ttw=NB, ab4=4 * NB, nx4=4 * NB, xi=2),
-    X4: dict(wq=512, uq=128, urq=128, vq=128, xq=C, eq4=512, csq=128, cpq=128, pfq=128, flq=FLQ, zq=HALF, hq=HALF),
-    U1: dict(wp=512, up=128, urp=128, vp=128, xp=C, ep4=512, csp=128, cpp=128, pfp=128, flp=FLQ),
+    U2: dict(ulu=8, go=32, qo=NB, o1=NB, plw=NB, fiw=NB, fw=NB, jlw=NB, eqw=2, ttw=NB, ab4=4 * NB, nx=4 * NB, xi=2),
+    X4: dict(wq=512, uq=128, urq=128, vq=128, xq=C, eq4=512, eyq=128, csq=128, cpq=128, pfq=128, flq=FLQ, zq=256, hq=256),
+    U1: dict(wp=512, up=128, urp=128, vp=128, xp=C, ep4=512, eyp=128, csp=128, cpp=128, pfp=128, flp=FLQ),
 }
-SPW = NS + C
+SPW = NS + 512
 _S[X4].update(sq=R * NS, rq=R * NS, aq=R * NS)
 _S[U1].update(sp=R * SPW, rp=R * 2 * NS, ap=R * NS)
 _S[F4].update(sn=R * 8, rn=R * 8, an=R * 8)
 _S[U2].update(sl=R * 32, rl=R * 32, al=R * 32)
 PIECES = {"b": (NA, NS), "a": (0, NA)}
 PART = {}
-for _d, _b, _names in ((B2, "lanes", "k6 k6n el eo tl to sgn sge k5 lh lo"), (F4, "lanef", "nl no"),
+for _d, _b, _names in ((B2, "lanes", "k6 tl to sgn sge k5 lh lo kb4"), (F4, "lanef", "nl no wi wm wn eq"),
                        (U2, "lists", "o1 plw fiw fw jlw eqw ttw xi")):
     _o = 0
     for _n in _names.split():
@@ -72,7 +86,7 @@ for _d, _b, _names in ((B2, "lanes", "k6 k6n el eo tl to sgn sge k5 lh lo"), (F4
     _S[_d][_b] = _o
 SCRATCH = {n: ("sbuf", [128, w], d) for d in _S for n, w in _S[d].items()}
 SCRATCH["ps"] = ("psum", [128, 4096], F4)
-SEMAPHORES = (["qv", "qs", "qp", "qg", "sent", "lu", "lx", "lh", "lw", "lv", "lz", "lf", "out", "acc"]
+SEMAPHORES = (["qv", "qs", "qp", "qg", "sent", "lu", "lx", "lh", "lw", "lv", "lf", "out", "acc0", "acc1"]
               + ["%s%d" % (n, t) for t in range(R) for n in ("hn", "hl", "ha", "hb", "an", "al", "aa", "ab")])
 
 OP = AluOpType
@@ -81,10 +95,10 @@ _PLAN = {}
 SPEEDS = [dict(e=1.0, g=1.0, s=1.0, p=1.0, n=1.0, w=150.0), dict(e=1.3, g=1.5, s=1.5, p=1.8, n=1.0, w=120.0),
           dict(e=1.1, g=0.9, s=0.8, p=1.3, n=1.25, w=220.0)]
 NET = dict(n=3100, l=3100, b=4000, a=3800, add=3300)
-SWEEPS, SPAN, TRIES, SOFT = 12, 100, 1200, 30.0
-FIRST = ("zz0 cm0 go0 kb0 cst0 urq0 xq%d xq0 urp0 cpt0 em0 k40 flq%d csq0 sg0 eq40 eq4128 eq4256 eq4384 cpq0" % (PIECE[0][0], LOW)).split()
+SWEEPS, SPAN, TRIES, SOFT = 30, 70, 800, 30.0
+FIRST = ("go0 zz0 cpt0 cst0 cm0 urq0 xq%d xq0 urp0 kb0 eye0 cpq0 eyq0 k40 sg0" % PIECE[0][0]).split()
 STEPS = (-12, -8, -5, -3, -2, -1, -1, 1, 1, 2, 3, 5, 8, 12)
-PASSES, HEAT = 6, 1.0
+PASSES, HEAT, WIDE = 6, 0.5, 30.0
 
 
 def _edges(ops, m):
@@ -134,13 +148,13 @@ def _plan(ops):
         for d in pre[i]:
             post[d].append(i)
 
-    def moved(key, i, by, inside):
-        key, todo = key.copy(), [i]
+    def moved(key, i, by, pre, post):
+        key, todo = key[:], [i]
         key[i] += by
         while todo:
             j = todo.pop()
             for d in (pre if by < 0 else post)[j]:
-                if (inside is None or d in inside) and (key[d] - key[j]) * by <= 0:
+                if (key[d] - key[j]) * by <= 0:
                     key[d] = key[j] + (1e-3 if by > 0 else -1e-3)
                     todo.append(d)
         return key
@@ -160,7 +174,7 @@ def _plan(ops):
     key = [1e-4 * i - tail[i] for i in range(n)]
     for k, name in enumerate(FIRST):
         i = [o[7] for o in ops].index(name)
-        key = moved(key, i, min(0.0, k - 1e7 - key[i]), None)
+        key = moved(key, i, min(0.0, k - 1e7 - key[i]), pre, post)
     order = np.argsort(key, kind="stable").tolist()
     now = None
     for m in M:
@@ -186,74 +200,93 @@ def _plan(ops):
     order = best_order
     rng = np.random.default_rng(1)
     for sweep in range(SWEEPS):
+        soft = SOFT * max(1.0, WIDE ** (1.0 - sweep / (0.6 * SWEEPS)))
         for p0 in range((sweep % 2) * SPAN // 4, n, SPAN // 2):
             rank = {i: k for k, i in enumerate(order)}
             order.sort(key=lambda i: (now[0][0][i], rank[i]))
             win = order[p0:p0 + SPAN]
-            inside = set(win)
-            last, free = [], []
+            at = {i: k for k, i in enumerate(win)}
+            ww = range(len(win))
+            wq = [queue[i] for i in win]
+            wpre = [[at[d] for d in pre[i] if d in at] for i in win]
+            wpost = [[at[d] for d in post[i] if d in at] for i in win]
+            view = []
             for m in M:
                 latest, nxt = [now[m][1] - o[4][m] for o in ops], [1e18] * len(names)
                 for i in reversed(order[p0:]):
                     if busy[m][i]:
                         latest[i] = min(latest[i], nxt[queue[i]] - busy[m][i])
-                    if i not in inside:
+                    if i not in at:
                         if busy[m][i]:
                             nxt[queue[i]] = latest[i]
                         for d, lag in edges[m][i]:
                             latest[d] = min(latest[d], latest[i] - lag)
-                last.append(np.array([latest[i] for i in win]))
                 f = [0.0] * len(names)
                 for i in order[:p0]:
                     if busy[m][i]:
                         f[queue[i]] = now[m][0][i] + busy[m][i]
-                free.append(f)
-            work = [list(now[m][0]) for m in M]
+                view.append(([latest[i] for i in win], f, [busy[m][i] for i in win],
+                             [max([0.0] + [now[m][0][d] + lag for d, lag in edges[m][i] if d not in at]) for i in win],
+                             [[(at[d], lag) for d, lag in edges[m][i] if d in at] for i in win], [0.0] * len(win)))
 
             def late(key):
-                seq, r = sorted(win, key=key.get), 0.0
-                for m in M:
-                    _run(seq, edges[m], queue, busy[m], work[m], list(free[m]))
-                    r += float(np.log(np.exp((np.array([work[m][i] for i in win]) - last[m]) / SOFT).sum()))
+                seq, r = sorted(ww, key=lambda i: key[i]), 0.0
+                for last, f, b, low, e, s in view:
+                    f, x = f[:], 1e-300
+                    for i in seq:
+                        q = wq[i]
+                        t = f[q]
+                        if low[i] > t:
+                            t = low[i]
+                        for d, lag in e[i]:
+                            if s[d] + lag > t:
+                                t = s[d] + lag
+                        s[i] = t
+                        if b[i]:
+                            f[q] = t + b[i]
+                        t -= last[i]
+                        if t > -10.0 * soft:
+                            x += math.exp(min(t / soft, 500.0))
+                    r += math.log(x) * soft / SOFT
                 return r
 
-            key = {i: float(k) for k, i in enumerate(win)}
+            key = [float(k) for k in ww]
             best = late(key)
+            mates = [[j for j in ww if wq[j] == q] for q in range(len(names))]
             held, top, draw = key, best, rng.random((TRIES, 5)).tolist()
             for it, (u0, u1, u2, u3, u4) in enumerate(draw):
                 if it % 40 == 0:
-                    m = it // 40 % len(M)
                     late(key)
-                    seq = sorted(win, key=key.get)
-                    lt, nxt = dict(zip(win, last[m].tolist())), [1e18] * len(names)
-                    for i in reversed(seq):
-                        if busy[m][i]:
-                            lt[i] = nxt[queue[i]] = min(lt[i], nxt[queue[i]] - busy[m][i])
-                        for d, lag in edges[m][i]:
-                            if d in inside and lt[i] - lag < lt[d]:
+                    last, _, b, _, e, s = view[it // 40 % len(M)]
+                    lt, nxt = last[:], [1e18] * len(names)
+                    for i in sorted(ww, key=lambda i: -key[i]):
+                        if b[i]:
+                            lt[i] = nxt[wq[i]] = min(lt[i], nxt[wq[i]] - b[i])
+                        for d, lag in e[i]:
+                            if lt[i] - lag < lt[d]:
                                 lt[d] = lt[i] - lag
-                    least = min(lt[i] - work[m][i] for i in win)
-                    tight = [i for i in win if lt[i] - work[m][i] < least + SOFT and busy[m][i]] or win
-                i = tight[int(u0 * len(tight))] if u1 < 0.6 else win[int(u0 * len(win))]
-                same = sorted((j for j in win if queue[j] == queue[i]), key=key.get)
+                    least = min(lt[i] - s[i] for i in ww)
+                    tight = [i for i in ww if lt[i] - s[i] < least + SOFT and b[i]] or list(ww)
+                i = tight[int(u0 * len(tight))] if u1 < 0.6 else int(u0 * len(win))
+                same = sorted(mates[wq[i]], key=lambda j: key[j])
                 k, step = same.index(i), STEPS[int(u2 * len(STEPS))]
                 if u1 < 0.3 and k:
                     k = max(0, k - 1 - int(u3 * 3))
                     i, step = same[k], abs(step)
                 elif u1 < 0.6:
                     step = -abs(step)
-                if not busy[0][i] or not 0 <= k + step < len(same):
+                if not view[0][2][i] or not 0 <= k + step < len(same):
                     continue
                 j = same[k + step]
-                new = moved(key, i, key[j] - key[i] + (1e-2 if step > 0 else -1e-2) * (0.1 + u3), inside)
+                new = moved(key, i, key[j] - key[i] + (1e-2 if step > 0 else -1e-2) * (0.1 + u3), wpre, wpost)
                 r = late(new)
-                if r <= best - HEAT * (1.0 - it / TRIES) * float(np.log(u4 + 1e-12)):
+                if r <= best - HEAT * (1.0 - it / TRIES) * math.log(u4 + 1e-12):
                     best, key = r, new
                     if r <= top:
                         top, held = r, new
-            trial = order[:p0] + sorted(win, key=held.get) + order[p0 + SPAN:]
+            trial = order[:p0] + [win[i] for i in sorted(ww, key=lambda i: held[i])] + order[p0 + SPAN:]
             new = times(trial)
-            if sum(e for _, e in new) <= sum(e for _, e in now):
+            if sum(e for _, e in new) <= sum(e for _, e in now) + 3 * (soft - SOFT):
                 order, now = trial, new
     _PLAN["ns"] = [e for _, e in now]
     _PLAN["start"] = now[0][0]
@@ -313,7 +346,7 @@ def rank_program(g, core, T, topo):
     Q = {"v": g.vector, "s": g.scalar, "p": g.tensor, "g": g, "y": g.sync}
     QS = {"v": "qv", "s": "qs", "p": "qp", "g": "qg"}
     V, S = g.vector, g.scalar
-    ops, lastw, readers, chain = [], {}, {}, {}
+    ops, lastw, readers, mark, ORDER = [], {}, {}, {}, []
 
     def A(name, a=0, b=None, s=1):
         name, o, n = PART.get(name) or (name, 0, SCRATCH[name][1][1])
@@ -348,8 +381,6 @@ def rank_program(g, core, T, topo):
             m[x[2]] = True
             readers.setdefault(x[1], []).append((me, m))
         deps.discard(me)
-        if q in chain:
-            after, chain[q] = list(after) + chain[q], [me]
         ops.append((q, sorted(deps), list(after), call, ns, token, ns if busy is None else (busy,) * len(SPEEDS),
                     "%s%d" % (writes[0][1], writes[0][2][0]) if writes else None))
         return me
@@ -360,6 +391,9 @@ def rank_program(g, core, T, topo):
     def ind(win, by):
         return win[0].indirect(by[0]) if by else win[0]
 
+    def wide(x):
+        return x[3] if x[1] == "ps" else len(x[2])
+
     def ns_of(o, xs, by=None, k=1.0):
         if by:
             return cost(e=50, g=1.25 * len(o[2]))
@@ -367,26 +401,26 @@ def rank_program(g, core, T, topo):
         return cost(e=50 + 0.83 * k * len(o[2]) * (0.5 if two else 1))
 
     def memset(o, c):
-        op("v", [], [o], lambda: V.memset(o[0], c), ns_of(o, []))
+        return op("v", [], [o], lambda: V.memset(o[0], c), ns_of(o, []))
 
     def ts(o, i, s1, op0, s2=None, op1=None, by=None):
         more = () if op1 is None else (op1,)
-        op("v", [i, s1, s2, by], [o], lambda: V.tensor_scalar(o[0], ind(i, by), raw(s1), raw(s2), op0, *more), ns_of(o, [i], by))
+        return op("v", [i, s1, s2, by], [o], lambda: V.tensor_scalar(o[0], ind(i, by), raw(s1), raw(s2), op0, *more), ns_of(o, [i], by))
 
     def tt(o, a, b, o_, by=None):
-        op("v", [a, b, by], [o], lambda: V.tensor_tensor(o[0], ind(a, by), b[0], o_), ns_of(o, [a, b], by, 1 if a[1] == "ps" else 2))
+        return op("v", [a, b, by], [o], lambda: V.tensor_tensor(o[0], ind(a, by), b[0], o_), ns_of(o, [a, b], by, 1 if a[1] == "ps" else 2))
 
     def cp(o, i, by=None):
-        op("v", [i, by], [o], lambda: V.tensor_copy(o[0], ind(i, by)), ns_of(o, [i], by))
+        return op("v", [i, by], [o], lambda: V.tensor_copy(o[0], ind(i, by)), ns_of(o, [i], by))
 
     def scatter(win, by, i):
-        op("v", [i, by], [win], lambda: V.tensor_copy(ind(win, by), i[0]), cost(e=50, s=2.9 * len(i[2])))
+        return op("v", [i, by], [win], lambda: V.tensor_copy(ind(win, by), i[0]), cost(e=50, s=2.9 * len(i[2])))
 
     def scan(o, d0, d1, init, op0, op1):
-        op("v", [d0, d1], [o], lambda: V.tensor_tensor_scan(o[0], d0[0], d1[0], init, op0, op1), ns_of(o, [d0, d1]))
+        return op("v", [d0, d1], [o], lambda: V.tensor_tensor_scan(o[0], d0[0], d1[0], init, op0, op1), ns_of(o, [d0, d1]))
 
     def total_of(o, i):
-        op("v", [i], [o], lambda: V.tensor_reduce(o[0], i[0], AxisListType.X, OP.add), cost(e=90))
+        return op("v", [i], [o], lambda: V.tensor_reduce(o[0], i[0], AxisListType.X, OP.add), cost(e=50 + 0.83 * wide(i)))
 
     def act(o, i, f=AF.Copy, bias=None, scale=1.0, acc=None, by=None):
         kw = {"scale": raw(scale)}
@@ -394,39 +428,39 @@ def rank_program(g, core, T, topo):
             kw["bias"] = raw(bias)
         if acc:
             kw["accum_out"] = acc[0]
-        op("s", [i, bias, scale, by], [o, acc], lambda: S.activation(o[0], ind(i, by), f, **kw),
-           cost(e=65, g=1.25 * len(o[2])) if by else cost(e=(85 if acc else 65) + 0.83 * len(o[2])))
+        return op("s", [i, bias, scale, by], [o, acc], lambda: S.activation(o[0], ind(i, by), f, **kw),
+                  cost(e=65, g=1.25 * len(o[2])) if by else cost(e=(85 if acc else 65) + 0.83 * len(o[2])))
 
     def lin(o, i, scale, bias, q=None):
         if (q or CFG["lin"]) == "s":
-            act(o, i, AF.Identity, bias, scale)
-        else:
-            ts(o, i, scale, OP.mult, bias, OP.add)
+            return act(o, i, AF.Copy if bias is None else AF.Identity, bias, scale)
+        return ts(o, i, scale, OP.mult) if bias is None else ts(o, i, scale, OP.mult, bias, OP.add)
 
-    def pick(q, o, i, by):
-        if q == "s":
-            act(o, i, by=by)
-        else:
-            cp(o, i, by)
+    def pick(q, o, i, by=None):
+        return act(o, i, by=by) if q == "s" else cp(o, i, by)
 
     def quant2(p, i):
-        op("v", [i], p, lambda: V.quantize_mx(p[0][0], p[1][0], i[0]), cost(e=12 + 0.22 * len(i[2])))
+        return op("v", [i], p, lambda: V.quantize_mx(p[0][0], p[1][0], i[0]), cost(e=12 + 0.22 * len(i[2])))
 
     def pair(n, a=0, b=None):
         return [A(n + "q", a, b), A(n + "p", a, b)]
 
     def quant(n, i, a=0, b=None):
-        quant2(pair(n, a, b), i)
+        return quant2(pair(n, a, b), i)
 
     def mm(o, l, r, start=True, stop=True):
-        op("p", l + r, [o], lambda: g.tensor.matmul_mx(o[0], l[0][0], l[1][0], r[0][0], r[1][0], start, stop), cost(p=40 + 0.6 * len(r[0][2])))
+        return op("p", l + r, [o], lambda: g.tensor.matmul_mx(o[0], l[0][0], l[1][0], r[0][0], r[1][0], start, stop), cost(p=40 + 0.6 * len(r[0][2])))
 
     def iota(o, pattern, base=0, cm=0):
         kw = {} if SCRATCH[o[1]][2] == I4 else {"allow_small_or_imprecise_dtypes": True}
-        op("g", [], [o], lambda: g.iota(o[0], pattern, base, cm, **kw), cost(e=130 + 1.66 * len(o[2])))
+        return op("g", [], [o], lambda: g.iota(o[0], pattern, base, cm, **kw), cost(e=130 + 1.66 * len(o[2])))
 
     def fill(o, c):
-        iota(o, [[0, len(o[2])]], c)
+        return iota(o, [[0, len(o[2])]], c)
+
+    def ones_at(o, pattern, base, cm):
+        z = A("zz", 0, len(o[2]))
+        op("g", [z], [o], lambda: g.affine_select(o[0], z[0], pattern, OP.not_equal, 1.0, base, cm), cost(e=170 + 1.66 * len(o[2])))
 
     last_dma = {}
 
@@ -434,7 +468,27 @@ def rank_program(g, core, T, topo):
         last_dma[q] = op(q, reads, writes, lambda: Q[q].dma_start(out, in_).then_inc(T.sem[sem], 16), cost(n=ns), (sem, total),
                          [last_dma[q]] if q in last_dma else [], 60)
 
+    def renumber():
+        for seq in ORDER:
+            for x, y in zip(seq, seq[1:]):
+                ops[y][2].append(x)
+        done, new = {}, []
+        for i in range(len(ops)):
+            todo = [i]
+            while todo:
+                j = todo[-1]
+                left = [d for d in ops[j][1] + ops[j][2] if d not in done]
+                if left:
+                    todo.extend(left)
+                    continue
+                todo.pop()
+                if j not in done:
+                    done[j] = len(new)
+                    new.append(j)
+        ops[:] = [(o[0], [done[d] for d in o[1]], [done[d] for d in o[2]]) + tuple(o[3:]) for o in (ops[j] for j in new)]
+
     def emit():
+        renumber()
         if "order" not in _PLAN:
             _PLAN["order"] = _plan(ops)
         count, known, token = {}, {}, {}
@@ -458,8 +512,9 @@ def rank_program(g, core, T, topo):
         for sem, val in count.items():
             g.wait_ge(T.sem[sem], val)
 
-    CQ, CQ1, CQ4, CQ41, CG, CS16, CS4, CT4, CQ2, CP, CPO, CH16, CH4, CU4, CQ16, CL4 = [A("pc", k, k + 1) for k in range(16)]
-    CZ, CB, CY = A("vec", 255, 256), A("tab", 32, 33), A("tab", 33, 34)
+    (CQ, CQ1, CQ4, CQ41, CG, CS16, CS4, CT4, CQ2, CP, CPO, CH16, CH4, CU4, CQ16, CL4,
+     CF16, CD, CDN) = [A("pc", k, k + 1) for k in range(19)]
+    CB, CY, CZ = A("tab", 32, 33), A("tab", 33, 34), A("tab", 34, 35)
     HALVES = ((0, HALF), (HALF, C))
 
     def W(k, a=0, b=NB):
@@ -503,40 +558,39 @@ def rank_program(g, core, T, topo):
     iota(J16, [[1, 16]])
     iota(A("cw"), [[16, NB]])
     iota(tab(1), [[0, 4], [1, 4]])
-    iota(A("g32"), [[1, 8], [0, 4]])
-    iota(A("tab", 160, 192), [[-1, 2], [0, 16]], 1)
-    iota(tab(12), [[1, 4], [-1, 4]])
-    fill(tab(13), 0)
+    iota(A("g32"), [[-16, 8], [0, 4]], 16, 1)
+    iota(tab(15), [[1, 4], [-1, 4]])
+    memset(A("tab", 160, 240), 0.0)
+    memset(tab(11), 1.0)
     fill(A("ones"), 1)
     memset(A("zz"), 0.0)
-    op("g", [A("zz", 0, 528)], [A("em")], lambda: g.affine_select(T.em[:], T.zz[:, 0:528], [[-1, 528]], OP.not_equal, 1.0, 3, 4), cost(e=1100))
-    runs = []
-    for kind, lanes, lo, hi, a, _ in TILES:
-        runs.append((a, a + 16 * max(d for d in lanes if d < NV) - lo) if kind == "d" else (a + 16 * lanes[-1], a + hi))
-    runs[1] = (LOW, runs[1][1])
-    for a, b in reversed(runs):
-        dma("y", "lf", 16 * len(runs), T.fl[:, 4 * a:4 * b], T.zz[:, 0:4 * (b - a)], [A("zz", 0, 4 * (b - a))], [A("fl", 4 * a, 4 * b)])
+    ones_at(A("em"), [[-1, 528]], 3, 4)
+    ones_at(A("eye"), [[1, 128], [0, 4]], 0, -1)
+    for a, b in ZERO:
+        dma("y", "lf", 16 * len(ZERO), T.fl[:, 4 * a:4 * b], T.zz[:, 0:4 * (b - a)], [A("zz", 0, 4 * (b - a))], [A("fl", 4 * a, 4 * b)])
     fill(A("win", 0, 4 * C), 0)
-    iota(A("cnt", 0, L), [[1, L]], C)
-    iota(A("cnt", L, C), [[-1, C - L]], -L)
-    fill(A("eqr", C, C + 16), 0)
+    iota(A("cnt", 0, L), [[2, L]], C)
+    iota(A("cnt", L, C), [[-2, C - L]], -C - 2 * L)
+    fill(A("eqr"), 1)
+    iota(A("kr4"), [[0, NB], [512, 4]])
+    fill(A("wm", 0, 56, 2), -4096)
     fill(A("h3", 1, 48 * NB + 48, 3), -1024)
-    iota(A("k13"), [[0, NB], [1, LT]])
+    fill(A("k13"), 1)
+    fill(A("k13", 0, LT * NB, LT), 0)
     iota(A("cne"), [[2, C]], -C)
     iota(A("k5"), [[0, 84], [256, 5]])
     fill(A("lh"), 0)
-    iota(A("k6"), [[0, NB], [1, LN]])
-    fill(A("el"), 1)
+    fill(A("k6"), 1)
+    fill(A("k6", 0, LN * NB, LN), 0)
     fill(A("tl"), 0)
     fill(A("nl"), 0)
     fill(A("gt", C, C + 16), 0)
     fill(A("lr"), 0)
     fill(A("sn"), 0)
-    iota(A("ev"), [[0, 16]], 0)
-    iota(A("ev", 0, 1), [[0, 1]], C)
+    fill(A("ev"), 0)
+    iota(A("ev", 7, 9), [[-1, 2]], C + 1)
 
     ts(pi(1), pi(0), 15, OP.bitwise_and)
-    ts(pi(2), pi(0), 4, OP.arith_shift_right)
     cp(CQ, pi(1))
     ts(pi(3), pi(1), 2, OP.arith_shift_right)
     ts(pi(4), pi(1), 3, OP.bitwise_and)
@@ -555,13 +609,10 @@ def rank_program(g, core, T, topo):
     cp(A("ulu"), A("cw", 0, 8))
     lin(A("tab", 79, 80), A("tab", 79, 80), 1.0, -512.0)
     tt(tab(7), tab(7), tab(0), OP.max)
-    act(A("ky"), tab(4), scale=2.0, by=A("qo"))
     act(A("kx"), tab(4), by=A("qo"))
     act(A("k16"), tab(7), by=A("qo"))
     fill(A("pf", C, 512), 0)
-    ts(CQ16, pi(1), -16.0, OP.add)
     ts(pi(5), pi(1), 1, OP.arith_shift_right)
-    cp(CG, pi(2))
     cp(CQ4, pi(3))
     lin(CQ41, CQ4, 1.0, 1.0)
     act(CP, CQ, AF.Abs, -2.0)
@@ -578,100 +629,93 @@ def rank_program(g, core, T, topo):
     op("v", [A("uq"), A("ulu")], [A("urq")], lambda: V.tensor_copy(
         T.urq[:, 0:128].bitcast(dt.uint32), T.uq[:, 0:128].bitcast(dt.uint32).indirect(T.ulu[:, 0:8])), cost(e=50, g=190))
     op("s", [A("up"), A("ulu")], [A("urp")], lambda: S.activation(T.urp[:, 0:128], T.up[:, 0:128].indirect(T.ulu[:, 0:8]), AF.Copy), cost(e=65, g=160))
-    ts(A("g32"), A("g32"), CG, OP.is_equal, CQ16, OP.mult)
-    ts(A("go"), A("g32"), 16.0, OP.add)
-    ts(tab(12), tab(12), 0.0, OP.is_equal, CP, OP.mult)
-    act(A("cst"), A("tab", 160, 192), by=A("go"))
-    act(A("cpt"), A("tab", 192, 224), by=A("go"))
+    ts(A("go"), A("g32"), 0.0, OP.max, 47.0, OP.min)
+    ts(tab(13), tab(15), 0.0, OP.is_equal)
+    act(A("cst"), A("tab", 160, 208), by=A("go"))
+    act(A("cpt"), A("tab", 192, 240), by=A("go"))
     lin(CPO, CS4, -C / 4.0, 0.0)
     lin(A("jw", 42, 70), A("cw"), 1.0, CQ)
+    ts(tab(6), tab(1), CQ4, OP.is_lt, -1024.0, OP.mult)
+    ts(tab(9), tab(1), CQ4, OP.is_equal, 512.0, OP.mult)
+    tt(tab(6), tab(6), tab(9), OP.add)
+    act(A("ky"), tab(6), by=A("qo", 0, W4 // 16))
+    lin(CF16, CH16, 2.0, 0.0)
+    lin(CD, CQ, 1.0, C + 1.0)
+    lin(CDN, CQ, -1.0, -C - 1.0)
+    quant("ey", A("eye"))
     ts(tab(5), tab(1), CQ41, OP.is_equal, F, OP.mult)
     ts(tab(1), tab(1), CQ4, OP.not_equal)
     quant("cp", A("cpt"))
     quant("cs", A("cst"))
     lin(A("jw", 14, 42), A("cw"), 0.5, CQ2)
-    ts(A("cw", NV, NB), A("cw", NV, NB), CQ, OP.subtract, 15.0 + 512.0 - 4096.0, OP.add)
-    lin(A("cw", 0, NV), A("jw", 42, 42 + NV), -1.0, LOW - 1.0 + 512.0 - 4096.0)
-    lin(CY, A("tab", 79, 80), 2.0, 0.0)
-    lin(A("cw"), A("cw"), 1.0, CY)
+    lin(CY, A("tab", 99, 100), 1.0, 16.0 * ND + 15.0 - 512.0 - 4096.0)
+    lin(CY, CQ, -1.0, CY)
+    lin(CZ, CY, 1.0, float(C * 3))
+    fill(A("kb4"), 512)
+    iota(A("kb4", 0, W4 - 4 * NV, 4), [[-16, NB - NV]], 16 * (ND - NV))
     lin(A("jw", 0, 14), A("jw", 42, 56), 1.0, 0.0)
     lin(A("jw", 70, 84), A("jw", 42, 56), 1.0, float(HALF))
     lin(A("jw", 84, 112), A("jw", 42, 70), -1.0, float(C))
     tt(tab(5), tab(5), tab(1), OP.max)
-    act(A("k4", 0, 128), tab(5), by=A("qo", 0, 8))
-    act(A("k4", 128, C), tab(5), by=A("qo", 8, NB))
-    act(A("k6"), A("k6"), AF.Sign)
-    act(A("k13"), A("k13"), AF.Sign)
-    lin(A("k6n"), A("k6"), -1.0, 1.0)
+    act(A("k4"), tab(5), by=A("qo", 0, HALF // 16))
     quant("v", A("vt"))
     for b in range(4):
         quant2([A("eq4", 128 * b, 128 * b + 128), A("ep4", 128 * b, 128 * b + 128)], A("em", 3 - b, 515 - b))
-    z0 = TILES[ND - 2][5] - PAD
-    quant("fl", A("zz"), z0, z0 + 256)
-    for m, (kind, lanes, lo, hi, a, q0) in reversed(list(enumerate(TILES))):
-        if lo and m != ND - 2:
-            dma("y", "lz", 32 * (ND - 2), T.flq[:, q0:q0 + lo].bitcast(dt.uint8), T.flq[:, z0:z0 + lo].bitcast(dt.uint8),
-                [A("flq", z0, z0 + lo)], [A("flq", q0, q0 + lo)])
-            dma("y", "lz", 32 * (ND - 2), T.flp[:, q0:q0 + lo], T.flp[:, z0:z0 + lo], [A("flp", z0, z0 + lo)], [A("flp", q0, q0 + lo)])
+    PART["cwc"] = ("tab", 144, 16)
+    fill(A("cwc"), C)
 
     def E(b):
         return [A("eq4", 128 * b, 128 * b + 128), A("ep4", 128 * b, 128 * b + 128)]
 
     JW = A("jw", 42, 70)
-    EH, EN, EU, EM, HH, HM, HN, ST, XV, NN, NH, AH, SU, EC = range(14)
+    EU, HN, HM, ST, XV, NN, NH, AH, SU, EC, EQ = range(11)
+    EV, HH = (lambda a=0, b=16: A("ev", 8 + a, 8 + b)), (lambda a=0, b=16: A("ev", 24 + a, 24 + b))
 
     def brackets(K):
-        ev = A("ev")
+        ev = EV()
         ts(A("ei"), ev, 0.5, OP.mult, -0.25, OP.add)
-        lin(vec(EN), ev, -1.0, 0.0)
         lin(vec(EU), ev, 1.0, -0.5)
-        cp(vec(HH), A("ei"))
-        lin(vec(HN), vec(HH), -1.0, 0.5)
-        lin(vec(HM), vec(HH), 1.0, -float(HALF))
+        cp(HH(), A("ei"))
+        lin(vec(HN), HH(), -1.0, 0.5)
+        lin(vec(HM), HH(), 1.0, -float(HALF))
         for k in range(1, K):
             s = A("sgn", 42 * (k - 1), 42 * k)
             act(s, A("jw", 0, 42), AF.Sign, bias=vec(HN, k, k + 1))
-            act(A("lh", k - 1, 210, 5), s, scale=vec(HH, k, k + 1))
+            act(A("lh", k - 1, 210, 5), s, scale=HH(k, k + 1))
             act(A("lh", 209 + k, 420, 5), s, scale=vec(HM, k, k + 1))
-        scan(A("lo", 210, 420), A("k5", 210, 420), A("lh", 210, 420), 0.0, OP.min, OP.max)
-        scan(A("lo", 0, 210), A("k5", 0, 210), A("lh", 0, 210), 0.0, OP.min, OP.max)
-        tt(W(1, 14, NB), A("jw", 70, 84), A("lo", 214, 280, 5), OP.subtract)
-        tt(W(1, 0, 14), A("jw", 0, 14), A("lo", 4, 70, 5), OP.add)
-        cp(A("fiw"), W(1))
-        lo_, hi_ = A("lo", 74, 210, 5), A("lo", 284, 420, 5)
-        tt(W(2), JW, lo_, OP.subtract)
-        tt(W(3), lo_, hi_, OP.add)
-        tt(W(4), W(2), hi_, OP.add)
-        ts(W(4), W(4), float(HALF), OP.is_ge)
-        tt(W(4), W(4), W(3), OP.mult)
-        tt(W(7), W(4), W(2), OP.add)
-        cp(A("fw"), W(7))
+        scan(A("lo"), A("k5"), A("lh"), 0.0, OP.min, OP.max)
+        tt(A("wi", 1, 84, 2), A("jw", 42, 84), A("lo", 74, 280, 5), OP.subtract)
+        tt(A("wi", 85, 112, 2), A("jw", 0, 14), A("lo", 4, 70, 5), OP.add)
+        cp(A("fiw"), A("wi", 57, 112, 2))
+        tt(A("wi", 0, 56, 2), JW, A("lo", 284, 420, 5), OP.add)
+        tt(W(2), A("wi", 0, 56, 2), A("lo", 74, 210, 5), OP.subtract)
+        lin(A("wm", 1, 56, 2), W(2), 4096.0, -4096.0 * (HALF - 0.5))
+        scan(A("wn"), A("wm"), A("wi", 0, 56), 0.0, OP.min, OP.max)
+        cp(A("fw"), A("wn", 1, 56, 2))
         act(A("fr"), A("cne"), by=A("fw"))
-        for k in range(1, K):
-            act(A("el", k - 1, LN * NB, LN), JW, AF.Abs, bias=vec(EN, k, k + 1))
-            act(A("sge", 32 * k, 32 * k + NB), JW, AF.Sign, bias=vec(EU, k, k + 1), scale=-1.0)
-        scan(A("eo"), A("k6n"), A("el"), 1.0, OP.max, OP.min)
-        cp(A("eqw"), A("eo", LN - 1, LN * NB, LN))
-        act(A("eqr", 0, C), A("c16"), by=A("eqw"))
+        scan(A("eq", 0, 32), A("ev", 8, 40), A("kx", 0, 32), -512.0, OP.max, OP.add)
+        scan(A("eq", 32, 48), A("ev", 7, 23), A("kx", 0, 16), -512.0, OP.max, OP.add)
+        e, h, d = A("eq", 15, 16), A("eq", 31, 32), A("eq", 47, 48)
+        x = [vec(EQ, k, k + 1) for k in range(4)]
+        act(x[0], e, AF.Sign, d, -1.0)
+        lin(x[0], x[0], CDN, CD)
+        lin(x[1], e, 1.0, 256.0)
+        ts(A("eqw", 0, 1), x[1], x[0], OP.max)
+        scatter(A("eqr"), A("eqw", 0, 1), A("zz", 0, 16))
         lin(vec(EC), ev, -1.0, float(C))
         for k in range(1, K):
+            act(A("sge", 32 * k, 32 * k + NB), JW, AF.Sign, bias=vec(EU, k, k + 1), scale=-1.0)
             act(A("nl", k, LN * NB, LN), A("sge", 32 * k, 32 * k + NB), scale=vec(EC, k, k + 1))
         scan(A("no"), A("k6"), A("nl"), 0.0, OP.mult, OP.max)
         tt(A("wd", 1, 3 * NB, 3), A("jw", 84, 112), A("no", LN - 1, LN * NB, LN), OP.subtract)
         lin(A("wd", 2, 3 * NB, 3), A("no", LN - 1, LN * NB, LN), 1.0, 255.0 - 2048.0)
-        lin(vec(EH), vec(HH), -2.0, 0.0)
-        lin(vec(EM), vec(HH), 1.0, -float(C))
-        tt(vec(EH), vec(EH), ev, OP.add)
-        tt(vec(EM), vec(EM), EYE, OP.mult)
-        tt(vec(EH), vec(EH), vec(EM), OP.mult)
-        total_of(CZ, vec(EH))
-        ts(A("xi", 0, 1), CZ, float(C), OP.add)
-        tt(vec(ST), vec(HH), ev, OP.subtract)
-        tt(vec(ST, 0, 8), vec(ST, 0, 8), vec(HH, 1, 9), OP.subtract)
+        lin(x[2], h, -2.0, x[1])
+        lin(x[3], h, 1.0, 256.0 - C)
+        lin(x[2], x[2], 1.0, -512.0)
+        ts(A("xi", 0, 1), x[3], x[2], OP.mult, float(C), OP.add)
+        tt(vec(ST), HH(), ev, OP.subtract)
+        tt(vec(ST, 0, 8), vec(ST, 0, 8), HH(1, 9), OP.subtract)
         scan(back(vec(SU)), back(vec(ST)), A("cwc"), 0.0, OP.add, OP.add)
-
-    PART["cwc"] = ("tab", 144, 16)
-    fill(A("cwc"), C)
 
     def quant_x(xb):
         for a, b in PIECE:
@@ -683,91 +727,85 @@ def rank_program(g, core, T, topo):
         K = 4 + t
         xb = "x0" if t == 0 else "xs"
         sn, an = (lambda a=0, b=8, t=t: A("sn", 8 * t + a, 8 * t + b)), (lambda a=0, b=8, t=t: A("an", 8 * t + a, 8 * t + b))
-        for k, (a, b) in enumerate(PIECE[:-1]):
-            mm(bank(5 + k, b - a), pair("ur"), pair("x", a, b))
+        mm(bank(5, C - LOW), pair("ur"), pair("x", LOW, C))
+        mm(bank(0, LOW), pair("ur"), pair("x", 0, LOW))
         mm(bank(1, C - 16), pair("ur"), pair("x", 0, C - 16))
-        mm(bank(0, C), pair("ur"), pair("x"))
-        for k, (a, b) in enumerate(PIECE):
-            tt(A("yy", a, b), bank(5 + k, b - a) if k + 1 < len(PIECE) else bank(0, b, a), A("cm", a, b), OP.subtract)
-            scan(A("hd", a, b), A("kb", a, b), A("yy", a, b), -BIG, OP.min, OP.max)
-            if a < LOW:
-                b = min(b, LOW)
-                scan(back(A("hx", a, b)), A("kb", 0, b - a), back(A("hd", a, b)), -BIG, OP.min, OP.max)
+        for n, k, a, b in (("h", 5, LOW, C), ("l", 0, 0, LOW)):
+            mark["y" + n] = tt(A("yy", a, b), bank(k, b - a), A("cm", a, b), OP.subtract)
+            mark["h" + n] = scan(A("hd", a, b), A("kb", a, b), A("yy", a, b), -BIG, OP.min, OP.max)
+        mark["hx"] = scan(back(A("hx")), A("kb", 0, LOW), back(A("hd", 0, LOW)), -BIG, OP.min, OP.max)
+        between = {}
         if t == 0:
             mm(bank(7, C), pair("u"), pair("x"))
-            ts(A("pf", 0, C), bank(7, C), 0.0, OP.is_gt)
-            quant("pf", A("pf"))
-            mm(bank(5, 128), pair("cp"), pair("pf"))
-            scan(A("ex0"), A("k4", 0, C // 4), bank(5, C // 4), 0.0, OP.mult, OP.add)
-            lin(A("poff"), A("ex0", 3, C // 4, 4), CPO, float(C * (K - 1)))
-            for k in range(1, K):
-                act(A("pf", NB * k, NB * (k + 1)), A("ex0", 3, C // 4, 4), AF.Sign, 2.0 - 4.0 * k, CS4)
-            quant("pf", A("pf"))
+            mark["p1"] = ts(A("pf", 0, C), bank(7, C), 0.0, OP.is_gt, CP, OP.mult)
+            mark["p2"] = quant("pf", A("pf"))
+            mm(bank(6, 128), pair("cp"), pair("pf"))
+            mark["p3"] = scan(A("ex", 0, W4), A("k4", 0, W4), bank(6, W4), 0.0, OP.mult, OP.add)
+            lin(A("base"), A("ex", 3, W4, 4), CPO, CZ)
+            between[3] = [act(A("pf", NB * k, NB * (k + 1)), A("ex", 3, W4, 4), AF.Sign, 2.0 - 4.0 * k, CS4) for k in range(1, K)]
+            mark["p4"] = quant("pf", A("pf"))
             mm(bank(7, 128), pair("cs"), pair("pf"))
-            for k in range(1, K):
-                act(W(11, 0, NB // 4), bank(7, NB // 4 * (k + 1), NB // 4 * k), AF.Identity, 2.0 * C / NB, 0.5, A("ev", k, k + 1))
+            between[6] = [act(W(11 + k, 0, NB // 4), bank(7, NB // 4 * (k + 1), NB // 4 * k), AF.Identity, 2.0 * C / NB, 0.5, EV(k, k + 1))
+                          for k in range(1, K)]
             brackets(K)
-        o, late = 0, None
-        chain["s"] = []
-        for kind, lanes, lo, hi, a, q0 in TILES:
-            for k, d in enumerate(lanes):
-                if d < NV:
-                    continue
-                h = A("sg", o, o + 16 * d)
-                o += 16 * d
-                act(h, bank(1, 16 * d), AF.Sign, bias=A("hd", 16 * d + 15, 16 * d + 16), scale=-1.0)
-                if late:
-                    act(*late)
-                late = (A("fl", 4 * a + k, 4 * (a + 16 * d), 4), h, AF.Relu, None, 1.0, A("rs", d, d + 1))
-        o -= 16 * d
-        act(A("fl", 4 * a + k, 4 * (a + SPL), 4), A("sg", o, o + SPL), AF.Relu, acc=A("rs", d, d + 1))
-        act(A("fl", 4 * (a + SPL) + k, 4 * (a + 16 * d), 4), A("sg", o + SPL, o + 16 * d), AF.Relu, acc=A("rs", NB, NB + 1))
-        chain.pop("s")
-        last_row = d
+        where = {d: 4 * a for tiles, at, _, _, _ in GROUPS for d, a in zip(tiles, at)}
+        rows = [d for tiles in ROWS for d in tiles if d not in VROWS[t]]
+        o, first, second = 0, [], []
+        for d in rows:
+            h = A("sg", o, o + 16 * d)
+            o += 16 * d
+            first.append(act(h, bank(1, 16 * d), AF.Sign, bias=A("hd", 16 * d + 15, 16 * d + 16), scale=-1.0))
+            second.append(act(A("fl", where[d], where[d] + 16 * d), h, AF.Relu, acc=A("rs", d, d + 1)))
+        ORDER.append(first[:1] + [x for k, y in enumerate(zip(first[1:], second)) for x in list(y) + between.get(k, [])] + second[-1:])
 
         def sums(m):
-            kind, lanes, lo, hi, a, q0 = TILES[m]
-            for c, e in ((lo, SPL), (SPL, hi)) if m == SUMS[-1] else ((lo, hi),):
-                quant("fl", A("fl", 4 * (a + c - lo), 4 * (a + e - lo)), q0 + c, q0 + e)
-            if kind == "d":
-                for k, d in enumerate(lanes):
-                    if d >= NV:
-                        continue
-                    first = m == SUMS[0] and k == 0
-                    n = LOW if first else max(128, LOW - 16 * d)
-                    mm(bank(3, n), E(k), pair("fl", q0 + 16 * d, q0 + 16 * d + n), first, d == LAST_D)
-                if m == 0:
-                    mm(bank(4, C - LOW), E(0), pair("fl", q0 + LOW, q0 + C))
-            hi = C if m == SUMS[0] else hi
-            if lo < SPL:
-                mm(bank(2, SPL), pair("cs"), pair("fl", q0, q0 + SPL), m == [x for x in SUMS if TILES[x][2] < SPL][0], m == SUMS[-1])
-            mm(bank(6, hi - SPL), pair("cs"), pair("fl", q0 + SPL, q0 + hi), m == SUMS[0], m == SUMS[-1])
+            tiles, at, aq, pre, post = GROUPS[m]
+            pre, post = (pre, post) if t == 0 or len(tiles) == 1 else (0, 0)
+            n = at[-1] - at[0] + _long(tiles[-1])
+            mark["s%d" % m] = quant("fl", A("fl", 4 * (at[0] - pre), 4 * (at[0] + n + post)), aq[0] - pre, aq[0] + n + post)
+            for d, q0 in zip(tiles, aq):
+                if d < NV:
+                    c = q0 + 4 * d - WR
+                    mm(bank(3, 128), pair("ey"), pair("fl", c, c + 128), d == DIAG[0][0], d == DIAG[-1][-1])
+                if d == 0:
+                    mm(bank(4, 128), pair("ey"), pair("fl", q0, q0 + 128))
+                if d in VROWS[t]:
+                    mm(bank(6, 128), pair("ey"), pair("fl", q0, q0 + 128))
+                    act(W(11, 0, 4 * d), bank(6, 4 * d), acc=A("rs", d, d + 1))
+            for d, q0 in zip(tiles, aq):
+                mm(bank(2, 128), pair("cp"), pair("fl", q0, q0 + 128), d == DIAG[0][0], d == ROWS[-1][-1])
 
-        late = []
-        for m in SUMS:
-            kind, lanes, lo, hi, a, q0 = TILES[m]
-            for k, d in enumerate(lanes):
+        vord = [x for x in VORD if (t == 0 if x[0] == "p" else x[0] in "yhs" or int(x[:-1]) < NV or int(x[:-1]) in VROWS[t])]
+        for x in vord:
+            if x[0] == "s":
+                sums(int(x[1:]))
+            elif x[0] not in "yhp":
+                d = int(x[:-1])
+                a = where[d]
                 if d >= NV:
-                    continue
-                e = C if d == 0 else LOW
-                tt(A("fl", 4 * (a + 16 * d - lo) + k, 4 * (a + e - lo), 4), bank(0, e, 16 * d), A("hx" if d else "hd", 0, e - 16 * d), OP.is_le)
-                while late:
-                    sums(late.pop(0))
-            late.append(m)
-        for m in late:
-            sums(m)
+                    mark[x] = ts(A("fl", a, a + 16 * d), bank(0, 16 * d), A("hd", 16 * d + 15, 16 * d + 16), OP.is_lt)
+                elif x == "0b":
+                    mark[x] = tt(A("fl", a + LOW, a + C), bank(5, C - LOW), A("hd", LOW, C), OP.is_le)
+                elif x[-1] == "a":
+                    mark[x] = tt(A("fl", a + 16 * d, a + LOW), bank(0, LOW, 16 * d), A("hx" if d else "hd", 0, LOW - 16 * d), OP.is_le)
+                else:
+                    mark[x] = tt(A("fl", a, a + 16 * d), bank(0, 16 * d), A("hx", LOW - 16 * d, LOW), OP.is_lt)
+        ORDER.append([mark[x] for x in vord])
         for a, b in HALVES:
             act(A("xh", 4 * a, 4 * b), A(xb, 4 * a, 4 * b), scale=0.5)
-        scan(A("xr", LOW, C), A("kr", LOW, C), bank(4, C - LOW), 0.0, OP.min, OP.add)
-        scan(A("xr", 0, LOW), A("kr", 0, LOW), bank(3, LOW), 0.0, OP.min, OP.add)
-        tt(A("base"), A("cw"), A("poff"), OP.add)
-        tt(A("base", NV, NB), A("base", NV, NB), A("rs", NV, NB), OP.subtract)
-        tt(A("ky", 15, C, 16), A("base"), A("xr", 15, C, 16), OP.subtract)
-        y = A("ky", 16 * last_row + 15, 16 * last_row + 16)
-        ts(y, y, A("rs", NB, NB + 1), OP.subtract)
-        for k, a, b in ((2, 0, SPL), (6, SPL, C)):
-            scan(A("ex", a, b), bank(k, b - a), A("ky", a, b), -1024.0, OP.max, OP.add)
-            ts(A("o1", a // 16, b // 16), A("ex", a + 15, b, 16), 4096.0, OP.add)
+        n = 4 * NV + WR
+        scan(A("xb", 4 * NV, W4), A("kb4"), bank(4, W4, 4 * NV), 0.0, OP.min, OP.add)
+        scan(A("xr", 0, n), A("kr4", 0, n), bank(3, n), 0.0, OP.min, OP.add)
+        tt(A("base", NV, NB), A("base", NV, NB), A("xb", 4 * NV + 3, W4, 4), OP.subtract)
+        tt(A("base", NV - ND, NV), A("base", NV - ND, NV), A("xr", 3, WR, 4), OP.subtract)
+        tt(A("ky", 3, 4 * NV, 4), A("base", 0, NV), A("xr", WR + 3, n, 4), OP.subtract)
+        for a, b in ((NV, rows[-1]), (rows[-1], rows[-1] + 1), (rows[-1] + 1, NB)):
+            if b == a + 1:
+                lin(A("ky", 4 * a + 3, 4 * a + 4), A("rs", a, b), -1.0, A("base", a, b))
+            elif b > a:
+                tt(A("ky", 4 * a + 3, 4 * b, 4), A("base", a, b), A("rs", a, b), OP.subtract)
+        scan(A("ex0"), bank(2, W4), A("ky"), -1024.0, OP.max, OP.add)
+        ts(A("o1"), A("ex0", 3, W4, 4), 4096.0, OP.add)
         n = K * C
         scatter(A("win", 0, n), A("o1"), A("ones", 0, C))
         scan(A("so", 0, n), A("win", 0, n), A("win", 0, n), -C - 2.0, OP.add, OP.add)
@@ -775,44 +813,39 @@ def rank_program(g, core, T, topo):
         cp(A("plr", 0, HALF), A("so", 0, n), A("o1", 0, 14))
         if t + 1 < R:
             fill(A("win", 0, n + C), 0)
-        for a, b in HALVES:
-            keep(A("plr", a, b), a, b, A("plw", a // 16, b // 16))
+        keep(A("plr"), 0, C, A("plw"))
         scatter(A("orow"), A("plw"), A("cne"))
-        cp(A("abr", HALF, C), A("orow"), by=A("fiw", 14, NB))
-        act(A("abr", 0, HALF), A("orow"), by=A("fiw", 0, 14))
+        cp(A("abr", HALF, C), A("orow"), by=A("fiw", 0, 14))
+        act(A("abr", 0, HALF), A("orow"), by=A("fiw", 14, NB))
         wrap4(A("abr", HALF, C), HALF, A("ab4", 2 * NB, 4 * NB), HALF)
         wrap4(A("abr", 0, HALF), HALF, A("ab4", 0, 2 * NB))
-        for a, b in ((0, 8), (8, 28), (28, 48), (48, 2 * NB)):
-            act(A("bh", 16 * a, 16 * b), A("xh"), by=A("ab4", 2 * NB + a, 2 * NB + b))
-            tt(A("zt", 16 * a, 16 * b), A("xh"), A("bh", 16 * a, 16 * b), OP.add, by=A("ab4", a, b))
-        for k in range(2):
-            act(A("xn", C * k, C * k + C), A(xb), by=A("ab4", NB * k, NB * k + NB))
-            lin(A("bb", C * k, C * k + C), A("bh", C * k, C * k + C), 2.0, 0.0, CFG["bb"])
+        ORDER.append([pick(q, A("bh", 16 * a, 16 * b), A("xh"), A("ab4", 2 * NB + a, 2 * NB + b)) for q, (a, b) in zip(CFG["zb"], ZP)][CFG["zb"].count("v"):])
+        ORDER.append([tt(A("zt", 16 * a, 16 * b), A("xh"), A("bh", 16 * a, 16 * b), OP.add, by=A("ab4", a, b)) for a, b in ZP])
         p0 = t * SPW
-        qz, qh = [A("zq"), A("sp", p0 + NS, p0 + NS + HALF)], [A("hq"), A("sp", p0 + NS + HALF, p0 + SPW)]
-        quant2(qz, A("zt"))
-        for b in range(4):
-            mm(bank(3 + b, HALF), pair("w", 128 * b, 128 * b + 128), qz)
-        for b in range(2):
-            ts(A("ht", b, 2 * C, 4), bank(3 + b, HALF), 0.03125, OP.mult)
-            act(A("ht", 2 + b, 2 * C, 4), bank(5 + b, HALF), scale=0.03125)
-        quant2(qh, A("ht"))
-        mm(bank(0, HALF), pair("ur"), qh)
-        mm(bank(7, HALF), pair("ur"), qh)
-        ts(A("gt", 0, HALF), bank(0, HALF), 0.0, OP.is_le)
-        act(A("gt", HALF, C), bank(7, HALF), AF.Sign)
-        if CFG["add"] == "dma":
-            sends.append(op("g", [A("ht"), A("xn", 0, 2 * C)], [A("xn", 0, 2 * C)],
-                            lambda: g.dma_start(T.xn[:, 0:2 * C], T.ht[:], accum_op=OP.add).then_inc(T.sem.acc, 16), cost(n=NET["add"]),
-                            ("acc", 16 * t + 16), sends[-1:], 1000))
-        else:
-            for a in range(0, 2 * C, L):
-                tt(A("xn", a, a + L), A("xn", a, a + L), A("ht", a, a + L), OP.add)
+        for r, (a, b, c) in enumerate(RUNS):
+            act(A("xn", 4 * a, 4 * b), A(xb), by=A("ab4", a // 4, b // 4))
+            lin(A("bb", 4 * a, 4 * b), A("bh", 4 * a, 4 * b), 2.0, None, CFG["bb"])
+            o = p0 + NS + 128 * r
+            qz, qh = [A("zq", 128 * r, 128 * r + 128), A("sp", o, o + 128)], [A("hq", 128 * r, 128 * r + 128), A("sp", o + 256, o + 384)]
+            banks = ((3, 4, 5, 6), (0, 1, 2, 7))[r]
+            quant2(qz, A("zt", 4 * c, 4 * c + 512))
+            for k in range(4):
+                mm(bank(banks[k], 128), pair("w", 128 * k, 128 * k + 128), qz)
+            for k in range(4):
+                lin(A("ht", 4 * a + k, 4 * b, 4), bank(banks[k], b - c, a - c), 0.03125, None, CFG["ht"][r][k])
+            quant2(qh, A("ht", 4 * c, 4 * c + 512))
+            mm(bank(3 + 2 * r, 128), pair("ur"), qh)
+            mm(bank(4 + 2 * r, 128), pair("ur"), qh)
+            ts(A("gt", a, b), bank(3 + 2 * r, b - c, a - c), 0.0, OP.is_le)
+            act(A("gt", HALF + a, HALF + b), bank(4 + 2 * r, b - c, a - c), AF.Sign)
+            sends.append(op("g", [A("ht", 4 * a, 4 * b), A("xn", 4 * a, 4 * b)], [A("xn", 4 * a, 4 * b)],
+                            lambda a=4 * a, b=4 * b, s=T.sem["acc%d" % r]: g.dma_start(T.xn[:, a:b], T.ht[:, a:b], accum_op=OP.add).then_inc(s, 16),
+                            cost(n=NET["add"]), ("acc%d" % r, 16 * t + 16), sends[-1:], 1000))
         for a, b in zip(CFG["bh"], CFG["bh"][1:]):
             tt(A("xn", 2 * C + a, 2 * C + b), A("bb", a, b), A("ht", a, b), OP.subtract)
 
         def send(x, reads, call, arrives, n):
-            s = op("g", reads, [], call, cost(n=300), SENT, [sent[dict(a="b", l="n")[x]]] if x in "al" else [])
+            s = op("g", reads, [], call, cost(n=300), SENT, [sent[y] for y in BEHIND[min(t, 1)].get(x, "")])
             sends.append(s)
             sent[x] = s
             op("net", [], arrives, None, cost(n=NET[x]), ("a%s%d" % (x, t), n), [s], 0)
@@ -822,6 +855,9 @@ def rank_program(g, core, T, topo):
             a = (T["r" + x][:, w * t:w * t + w], T["s" + x][:, w * t:w * t + w], T.sem["h%s%d" % (x, t)], T.sem.sent, pid, rid, topo.mask(core, relays[0]))
             send(x, [A("s" + x, w * t, w * t + w)], lambda: g.remote_dma(*a), [A("a" + x, w * t, w * t + w)], n_in[0])
 
+        tt(vec(XV), A("gt"), vec(SU), OP.add, by=A("xi", 0, 1))
+        tt(sn(), vec(XV, 0, 8), vec(XV, 1, 9), OP.subtract)
+        small("n", 8)
         for x, banks in (("b", (3, 4, 5, 6)), ("a", (0, 1, 2, 7))):
             a, b = PIECES[x]
             quant2([A("sq", t * NS + a, t * NS + b), A("sp", p0 + a, p0 + b)], A("xn", 4 * (A0 + a), 4 * (A0 + b)))
@@ -841,16 +877,14 @@ def rank_program(g, core, T, topo):
                  lambda tr=tr: g.remote_dma_fused(tr, local_sem=T.sem.sent), came, sum(n_in[1:]))
             for k in range(4):
                 mm(bank(banks[k], b - a), E(k), came)
-                (act if CFG.get("un", "ssss")[k] == "s" else cp)(A("dn", 4 * a + k, 4 * b, 4), bank(banks[k], b - a))
-        tt(vec(XV), A("gt"), vec(SU), OP.add, by=A("xi", 0, 1))
-        tt(sn(), vec(XV, 0, 8), vec(XV, 1, 9), OP.subtract)
-        small("n", 8)
+                pick(CFG["un"][k], A("dn", 4 * a + k, 4 * b, 4), bank(banks[k], b - a))
         gv = CFG["gv"]
         act(A("gb", 16 * gv, C), A("gt"), AF.Relu, by=A("fw", gv, NB))
-        if gv:
-            ts(A("gb", 0, 16 * gv), A("gt"), 0.5, OP.is_gt, by=A("fw", 0, gv))
+        ts(A("gb", 0, 16 * gv), A("gt"), 0.5, OP.is_gt, by=A("fw", 0, gv))
         scan(A("la"), A("eqr", 0, C), A("gb"), 0.0, OP.mult, OP.add)
         scan(back(A("lb")), back(A("eqr", 1, C + 1)), back(A("gb")), 0.0, OP.mult, OP.add)
+        if t + 1 < R:
+            fill(A("eqr"), 1)
         hold(A("exb"), A("gb"))
         hold(A("h3", 0, 3 * C, 3), A("la"))
         hold(A("h3", 32, 3 * C + 32, 3), A("lb"))
@@ -858,36 +892,37 @@ def rank_program(g, core, T, topo):
         scan(A("wo"), A("h3", 45, 45 + 48 * NB, 16), A("wd"), -4096.0, OP.max, OP.add)
         ts(A("jlw"), A("wo", 2, 3 * NB, 3), 2048.0, OP.add)
         scatter(A("lr"), A("jlw", B0, NB), A("fr", P0, C))
-        for k in range(2):
-            wrap4(A("lr", 64 * k, 64 * k + 64), 64, A("sl", 32 * t + 16 * k, 32 * t + 16 * k + 16), 64 * k, CL4)
+        wrap4(A("lr", 0, L), L, A("sl", 32 * t, 32 * t + 32), 0, CL4)
         small("l", 32)
+        act(A("slc"), A("fr"), by=A("plw"))
+        scan(A("exs"), A("k16"), A("slc"), 0.0, OP.mult, OP.add)
+        lin(W(9), A("exs", 15, C, 16), CF16, None)
         act(A("m2r"), A("cnt"), by=A("jlw"))
-        act(A("slc"), A("fr"), AF.Identity, float(HALF), 0.5, by=A("plw"))
-        tt(A("nxr"), A("m2r"), A("slc"), OP.max, by=A("plw"))
-        scan(A("ex"), A("k4"), A("nxr"), 0.0, OP.mult, OP.add)
-        ts(A("nx4"), A("ex", 3, C, 4), CS4, OP.mult, CT4, OP.add)
         act(A("pcol"), A("m2r"), by=A("plw"))
-        scan(A("xr"), A("k16"), A("pcol"), 0.0, OP.mult, OP.add)
-        lin(W(8), A("xr", 15, C, 16), CH16, 0.0)
-        lin(vec(NH, 0, 8), sn(), -1.0, 0.5)
-        lin(vec(AH, 0, 8), an(), -1.0, 0.5 - C)
+        scan(A("ex"), A("k16"), A("pcol"), 0.0, OP.mult, OP.add)
+        lin(W(8), A("ex", 15, C, 16), CF16, None)
+        tt(W(10), W(8), W(9), OP.max)
+        for k in range(4):
+            ts(A("nx", NB * k, NB * k + NB), W(10), 2.0, OP.mult, 2.0 * C + k, OP.add)
+        lin(vec(NH, 0, 8), sn(), -2.0, 1.0 - C)
+        lin(vec(AH, 0, 8), an(), -2.0, 1.0 - C)
         for k in range(K):
-            act(A("tl", k, LT * NB, LT), W(8), AF.Sign, vec(AH, k, k + 1), 2.0)
-            act(A("tl", LN + k, LT * NB, LT), W(8), AF.Sign, vec(NH, k, k + 1), -2.0)
+            act(A("tl", k, LT * NB, LT), W(8), AF.Sign, vec(AH, k, k + 1), 1.0)
+            act(A("tl", LN + k, LT * NB, LT), W(8), AF.Sign, vec(NH, k, k + 1), -1.0)
         scan(A("to"), A("k13"), A("tl"), 0.0, OP.mult, OP.add)
         if t + 1 < R:
-            lin(A("poff"), A("to", LT - 1, LT * NB, LT), -C / 2.0, 0.0)
+            lin(A("base"), A("to", LT - 1, LT * NB, LT), -C / 2.0, CY)
             ts(vec(NN, 0, 8), sn(), float(L), OP.max, -1.0, OP.mult)
             ts(vec(NN, 8, 16), an(), float(L), OP.min, -float(C + L), OP.add)
-            tt(A("ev", 1, K + 1), vec(NN, 0, K), vec(NN, 8, 8 + K), OP.subtract)
+            tt(EV(1, K + 1), vec(NN, 0, K), vec(NN, 8, 8 + K), OP.subtract)
             brackets(K + 1)
         else:
             ts(A("ttw"), A("to", LT - 1, LT * NB, LT), 0.5, OP.mult, float(K), OP.add)
             act(A("pout"), A("c16"), by=A("ttw"))
         for k, q in enumerate("sv"):
             pick(q, A("xn", 4 * C + 2 * L * k, 4 * C + 2 * L * (k + 1)), A("dn"), A("al", 32 * t + 16 * k, 32 * t + 16 * k + 16))
-        for q, a, b in SHARE:
-            pick(q, A("xs", 4 * a, 4 * b), A("xn"), A("nx4", a // 4, b // 4))
+        for q, k, a, b in SHARE:
+            pick(q, A("xs", 4 * a + k, 4 * b, 4), A("xn"), A("nx", NB * k + a // 16, NB * k + b // 16))
         quant_x("xs")
 
     total = 16 * (6 + len(PIECE))
@@ -897,6 +932,6 @@ def rank_program(g, core, T, topo):
     dma("y", "out", total, T.pts[:], T.pout[0:128:16, :], [A("pout")], [])
     for k, (a, b) in enumerate(PIECE):
         mm(bank(k, b - a), pair("v"), pair("x", a, b))
-        (act if k < 2 else cp)(A("yo", a, b), bank(k, b - a))
-        dma("sy"[k // 2], "out", total, T.y[:, a:b], T.yo[:, a:b], [A("yo", a, b)], [])
+        pick("vs"[k], A("yo", a, b), bank(k, b - a))
+        dma("ys"[k], "out", total, T.y[:, a:b], T.yo[:, a:b], [A("yo", a, b)], [])
     emit()

import math
import numpy as np
from concourse.bass import DstId, RemoteDMATransfer
from concourse.mybir import dt, AluOpType, ActivationFunctionType, AxisListType

C, L, R = 448, 128, 3
HALF = C // 2
NB = C // 16
NV = 19
LOW = 16 * NV
B0 = (C - HALF - L) // 16
P0 = 16 * B0
A0 = P0
NA, NS = HALF - A0, C - A0
SHARE = [("s", 0, 0, C), ("v", 2, 0, C), ("s", 1, 0, C), ("v", 3, 0, C)]
PIECE = [(LOW, C), (0, LOW)]
RUNS = [(A0, HALF, A0), (0, A0, 0)]
ZP = ((24, 32), (32, 44), (44, 56), (0, 16), (16, 24))
CFG = dict(bb="s", un="svsv", lin="s", mg="s", gv=14, ht=("vsvs", "vsvs"), bh=(0, 384, 640, 896), zb="vssss")
BEHIND = dict(a="b", l="n", b="n"), dict(a="b", l="n")
BIG = 2.0 ** 80
F = 2.0 ** 21
LN = 6
LT = 2 * LN
X4, B2, F4, I4, U2, U1 = "float8_e4m3fn_x4", "bfloat16", "float32", "int32", "uint16", "uint8"

W4, ND = C // 4, NV // 2
WR = 4 * ND
GAP = max(W4 - 4 * NV, WR)
DIAG = [(5, 0), (9, 1), (8, 2), (7, 3), (6, 4)]
ROWS = [(27, 19), (26, 25), (24, 23), (22, 21), (20,)]
VROWS = ((), (19,), (19,))
VORD = "yh hh yl 0b hl 19a p1 hx 0a p2 5a 5b 9a s0 p3 9b 1a 1b s5 8a s1 8b 2a 2b p4 7a s2 7b s6 3a 3b 6a s3 6b 4a 4b s7 s4 s8 s9".split()


def _long(x):
    return 4 * x if x >= NV else 4 * NV if x else W4


GROUPS, ZERO, FLQ = [], [], 0
_at, _room = max(WR - 4 * _g[0] for _g in DIAG), []
ZERO.append((0, _at))
for _k in range(3):
    _b = _at + 4 * NV + GAP
    _room.append((_at, _b))
    ZERO += [(_at + 4 * NV, _b), (_b + (W4 if _k == 2 else 4 * NV), _b + 128)]
    _at = _b + 128
for _k, _g in enumerate(DIAG + ROWS):
    if _g[0] < NV:
        _a, _pre = _room[2 if _g[-1] == 0 else _k % 2], WR - 4 * _g[0]
    else:
        _a, _pre = tuple(_at + W4 * _i for _i in range(len(_g))), 0
        ZERO += [(_x + 4 * _b, _x + (128 if _b == _g[-1] else W4)) for _x, _b in zip(_a, _g)]
        _at = _a[-1] + 128
    GROUPS.append((_g, _a, tuple(FLQ + _pre + _x - _a[0] for _x in _a), _pre, 128 - _long(_g[-1])))
    FLQ += _pre + _a[-1] - _a[0] + 128
FLW = _at
SG = sum(16 * b for b in range(NV, NB))

_S = {
    B2: dict(x0=4 * C, xs=4 * C, xh=4 * C, ut=512, vt=512, em=528, eye=512, ones=C, cst=512, cpt=512, pf=512, fl=4 * FLW, zz=528,
             cm=C, k16=C, k4=HALF, kx=C, kr=C, kr4=W4, kb4=W4 - 4 * NV, kb=C, k5=420, k6=LN * NB, sg=SG, sgn=256, sge=256, exb=C, exh=C, exs=C,
             h3=48 * NB + 48, lb=C, win=6 * C, so=6 * C, cne=C, eqr=C + 32, lh=420, lo=420, bh=2 * C, bb=2 * C, zt=2 * C, ht=2 * C,
             xn=4 * (C + L), gt=C + 16, gb=C, la=C, dn=4 * NS, plr=C, orow=C, abr=C, fr=C, lr=C, slc=C, tl=LT * NB, to=LT * NB, k13=LT * NB),
    F4: dict(pc=24, tab=256, g32=32, ex0=W4, cnt=C, c16=16, jw=112, cw=NB, ky=W4, yy=C, hd=C, hx=LOW, rs=NB + 4, base=NB, wf=512,
             ex=C, xr=W4, xb=W4, ev=40, eq=48, vec=256, wi=112, wm=56, wn=56,
             nl=LN * NB, no=LN * NB, m2r=C, pcol=C, wd=3 * NB, wo=3 * NB, pout=C, yo=C),
    I4: dict(pi=16, ei=16),
    U2: dict(ulu=8, go=32, qo=NB, o1=NB, plw=NB, fiw=NB, fw=NB, jlw=NB, eqw=2, ttw=NB, ab4=4 * NB, nx=4 * NB, xi=2),
    X4: dict(wq=512, uq=128, urq=128, vq=128, xq=C, eq4=512, eyq=128, csq=128, cpq=128, pfq=128, flq=FLQ, zq=256, hq=256),
    U1: dict(wp=512, up=128, urp=128, vp=128, xp=C, ep4=512, eyp=128, csp=128, cpp=128, pfp=128, flp=FLQ),
}
SPW = NS + 512
_S[X4].update(sq=R * NS, rq=R * NS, aq=R * NS)
_S[U1].update(sp=R * SPW, rp=R * 2 * NS, ap=R * NS)
_S[F4].update(sn=R * 8, rn=R * 8, an=R * 8)
_S[U2].update(sl=R * 32, rl=R * 32, al=R * 32)
PIECES = {"b": (NA, NS), "a": (0, NA)}
PART = {}
for _d, _b, _names in ((B2, "lanes", "k6 tl to sgn sge k5 lh lo kb4"), (F4, "lanef", "nl no wi wm wn eq"),
                       (U2, "lists", "o1 plw fiw fw jlw eqw ttw xi")):
    _o = 0
    for _n in _names.split():
        PART[_n] = (_b, _o, _S[_d].pop(_n))
        _o += PART[_n][2]
    _S[_d][_b] = _o
SCRATCH = {n: ("sbuf", [128, w], d) for d in _S for n, w in _S[d].items()}
SCRATCH["ps"] = ("psum", [128, 4096], F4)
SEMAPHORES = (["qv", "qs", "qp", "qg", "sent", "lu", "lx", "lh", "lw", "lv", "lf", "out", "acc0", "acc1"]
              + ["%s%d" % (n, t) for t in range(R) for n in ("hn", "hl", "ha", "hb", "an", "al", "aa", "ab")])

OP = AluOpType
AF = ActivationFunctionType
_PLAN = {}
SPEEDS = [dict(e=1.0, g=1.0, s=1.0, p=1.0, n=1.0, w=150.0), dict(e=1.3, g=1.5, s=1.5, p=1.8, n=1.0, w=120.0),
          dict(e=1.1, g=0.9, s=0.8, p=1.3, n=1.25, w=220.0)]
NET = dict(n=3100, l=3100, b=4000, a=3800, add=3300)
SWEEPS, SPAN, TRIES, SOFT = 30, 70, 800, 30.0
FIRST = ("go0 zz0 cpt0 cst0 cm0 urq0 xq%d xq0 urp0 kb0 eye0 cpq0 eyq0 k40 sg0" % PIECE[0][0]).split()
STEPS = (-12, -8, -5, -3, -2, -1, -1, 1, 1, 2, 3, 5, 8, 12)
PASSES, HEAT, WIDE = 6, 0.5, 30.0


def _edges(ops, m):
    w = SPEEDS[m]["w"]
    return [[(d, ops[d][4][m] + (0.0 if o[0] == ops[d][0] == "p" else w)) for d in o[1]] + [(d, ops[d][6][m]) for d in o[2]] for o in ops]


def _fill(order, edges, queue, busy, shift):
    start, slots = [0.0] * len(edges), {}
    for i in order:
        t = max([0.0] + [start[d] + lag for d, lag in edges[i]])
        if busy[i]:
            t += shift[i]
            a, b = slots.setdefault(queue[i], ([], []))
            k = int(np.searchsorted(b, t, "right"))
            while k < len(a) and a[k] < t + busy[i]:
                t = max(t, b[k])
                k += 1
            a.insert(k, t)
            b.insert(k, t + busy[i])
            t -= shift[i]
        start[i] = t
    return start


def _run(order, edges, queue, busy, start, free):
    for i in order:
        q = queue[i]
        t = free[q]
        for d, lag in edges[i]:
            if start[d] + lag > t:
                t = start[d] + lag
        start[i] = t
        if busy[i]:
            free[q] = t + busy[i]


def _plan(ops):
    n, M = len(ops), range(len(SPEEDS))
    names = sorted({o[0] for o in ops})
    queue = [names.index(o[0]) for o in ops]
    edges = [_edges(ops, m) for m in M]
    busy = [[o[6][m] for o in ops] for m in M]
    pre = [[d for d, _ in e] for e in edges[0]]
    post = [[] for _ in ops]
    for i in range(n):
        for d in pre[i]:
            post[d].append(i)

    def moved(key, i, by, pre, post):
        key, todo = key[:], [i]
        key[i] += by
        while todo:
            j = todo.pop()
            for d in (pre if by < 0 else post)[j]:
                if (key[d] - key[j]) * by <= 0:
                    key[d] = key[j] + (1e-3 if by > 0 else -1e-3)
                    todo.append(d)
        return key

    def times(order):
        out = []
        for m in M:
            s = [0.0] * n
            _run(order, edges[m], queue, busy[m], s, [0.0] * len(names))
            out.append((s, max(s[i] + ops[i][4][m] for i in order)))
        return out

    tail = [o[4][0] for o in ops]
    for i in range(n - 1, -1, -1):
        for d, lag in edges[0][i]:
            tail[d] = max(tail[d], lag + tail[i])
    key = [1e-4 * i - tail[i] for i in range(n)]
    for k, name in enumerate(FIRST):
        i = [o[7] for o in ops].index(name)
        key = moved(key, i, min(0.0, k - 1e7 - key[i]), pre, post)
    order = np.argsort(key, kind="stable").tolist()
    now = None
    for m in M:
        ns = [o[4][m] for o in ops]
        rev = [[] for _ in ops]
        for i in range(n):
            for d, lag in edges[m][i]:
                rev[d].append((i, lag + ns[i] - ns[d]))
        seq = order
        for _ in range(PASSES):
            start = _fill(seq, edges[m], queue, busy[m], [0.0] * n)
            rank = {i: k for k, i in enumerate(seq)}
            seq = sorted(seq, key=lambda i: (start[i], rank[i]))
            new = times(seq)
            if now is None or sum(e for _, e in new) < sum(e for _, e in now):
                best_order, now = seq, new
            end = _fill(seq[::-1], rev, queue, busy[m], [ns[i] - busy[m][i] for i in range(n)])
            rank = {i: k for k, i in enumerate(seq)}
            key = [0.0] * n
            for i in seq:
                key[i] = max([-end[i] - ns[i]] + [key[d] + 1e-6 for d in pre[i]])
            seq = sorted(seq, key=lambda i: (key[i], rank[i]))
    order = best_order
    rng = np.random.default_rng(1)
    for sweep in range(SWEEPS):
        soft = SOFT * max(1.0, WIDE ** (1.0 - sweep / (0.6 * SWEEPS)))
        for p0 in range((sweep % 2) * SPAN // 4, n, SPAN // 2):
            rank = {i: k for k, i in enumerate(order)}
            order.sort(key=lambda i: (now[0][0][i], rank[i]))
            win = order[p0:p0 + SPAN]
            at = {i: k for k, i in enumerate(win)}
            ww = range(len(win))
            wq = [queue[i] for i in win]
            wpre = [[at[d] for d in pre[i] if d in at] for i in win]
            wpost = [[at[d] for d in post[i] if d in at] for i in win]
            view = []
            for m in M:
                latest, nxt = [now[m][1] - o[4][m] for o in ops], [1e18] * len(names)
                for i in reversed(order[p0:]):
                    if busy[m][i]:
                        latest[i] = min(latest[i], nxt[queue[i]] - busy[m][i])
                    if i not in at:
                        if busy[m][i]:
                            nxt[queue[i]] = latest[i]
                        for d, lag in edges[m][i]:
                            latest[d] = min(latest[d], latest[i] - lag)
                f = [0.0] * len(names)
                for i in order[:p0]:
                    if busy[m][i]:
                        f[queue[i]] = now[m][0][i] + busy[m][i]
                view.append(([latest[i] for i in win], f, [busy[m][i] for i in win],
                             [max([0.0] + [now[m][0][d] + lag for d, lag in edges[m][i] if d not in at]) for i in win],
                             [[(at[d], lag) for d, lag in edges[m][i] if d in at] for i in win], [0.0] * len(win)))

            def late(key):
                seq, r = sorted(ww, key=lambda i: key[i]), 0.0
                for last, f, b, low, e, s in view:
                    f, x = f[:], 1e-300
                    for i in seq:
                        q = wq[i]
                        t = f[q]
                        if low[i] > t:
                            t = low[i]
                        for d, lag in e[i]:
                            if s[d] + lag > t:
                                t = s[d] + lag
                        s[i] = t
                        if b[i]:
                            f[q] = t + b[i]
                        t -= last[i]
                        if t > -10.0 * soft:
                            x += math.exp(min(t / soft, 500.0))
                    r += math.log(x) * soft / SOFT
                return r

            key = [float(k) for k in ww]
            best = late(key)
            mates = [[j for j in ww if wq[j] == q] for q in range(len(names))]
            held, top, draw = key, best, rng.random((TRIES, 5)).tolist()
            for it, (u0, u1, u2, u3, u4) in enumerate(draw):
                if it % 40 == 0:
                    late(key)
                    last, _, b, _, e, s = view[it // 40 % len(M)]
                    lt, nxt = last[:], [1e18] * len(names)
                    for i in sorted(ww, key=lambda i: -key[i]):
                        if b[i]:
                            lt[i] = nxt[wq[i]] = min(lt[i], nxt[wq[i]] - b[i])
                        for d, lag in e[i]:
                            if lt[i] - lag < lt[d]:
                                lt[d] = lt[i] - lag
                    least = min(lt[i] - s[i] for i in ww)
                    tight = [i for i in ww if lt[i] - s[i] < least + SOFT and b[i]] or list(ww)
                i = tight[int(u0 * len(tight))] if u1 < 0.6 else int(u0 * len(win))
                same = sorted(mates[wq[i]], key=lambda j: key[j])
                k, step = same.index(i), STEPS[int(u2 * len(STEPS))]
                if u1 < 0.3 and k:
                    k = max(0, k - 1 - int(u3 * 3))
                    i, step = same[k], abs(step)
                elif u1 < 0.6:
                    step = -abs(step)
                if not view[0][2][i] or not 0 <= k + step < len(same):
                    continue
                j = same[k + step]
                new = moved(key, i, key[j] - key[i] + (1e-2 if step > 0 else -1e-2) * (0.1 + u3), wpre, wpost)
                r = late(new)
                if r <= best - HEAT * (1.0 - it / TRIES) * math.log(u4 + 1e-12):
                    best, key = r, new
                    if r <= top:
                        top, held = r, new
            trial = order[:p0] + [win[i] for i in sorted(ww, key=lambda i: held[i])] + order[p0 + SPAN:]
            new = times(trial)
            if sum(e for _, e in new) <= sum(e for _, e in now) + 3 * (soft - SOFT):
                order, now = trial, new
    _PLAN["ns"] = [e for _, e in now]
    _PLAN["start"] = now[0][0]
    return order


def _relays(rank_core, nxt, topo):
    c = [k for k in topo.cores_of(rank_core) if k != rank_core and topo.may_write(k, nxt)]
    return sorted(c, key=lambda k: topo.die(k) != topo.die(rank_core))[:4]


def _mask(engs):
    return sum(1 << e for e in engs)


def _share(k, piece, t):
    a, b = PIECES[piece]
    h = (a + b) // 2
    a, b = ((a, h), (h, b), (a, b))[k - 1]
    return t * NS + a, t * NS + b


def hand_on(g, core, T, topo, nxt, k):
    rid, pid = topo.addr(nxt, core)
    m = topo.mask(core, nxt)
    for t in range(R):
        for x in ("n", "l") if k == 0 else PIECES:
            g.wait_ge(T.sem["h%s%d" % (x, t)], 16 if k == 0 else 4)
            if k == 0:
                w = 8 if x == "n" else 32
                dst, src = T["a" + x][:, w * t:w * t + w], T["r" + x][:, w * t:w * t + w]
            elif k < 3:
                a, b = _share(k, x, t)
                dst, src = T.aq[:, a:b].bitcast(dt.uint8), T.rq[:, a:b].bitcast(dt.uint8)
            else:
                a, b = _share(k, x, t)
                o = 2 * (t * NS + PIECES[x][0])
                dst, src = T.ap[:, a:b], T.rp[:, o:o + b - a]
            g.remote_dma(dst, src, T.sem["a%s%d" % (x, t)], T.sem.sent, pid, rid, m)
    g.wait_ge(T.sem.sent, len(topo.engines(core, nxt)) * 2 * R)


def rank_program(g, core, T, topo):
    cores = list(T.cores)
    rank = T.rank_of(core)
    if rank is None:
        for r, c in enumerate(cores):
            nxt = cores[(r + 1) % len(cores)]
            rl = _relays(c, nxt, topo)
            if core in rl:
                hand_on(g, core, T, topo, nxt, rl.index(core))
        return
    relays = _relays(core, cores[(rank + 1) % len(cores)], topo)
    n_in = [len(topo.engines(k, core)) for k in _relays(cores[rank - 1], core, topo)]
    SENT = ("sent", (2 * len(topo.engines(core, relays[0])) + 24) * R)

    Q = {"v": g.vector, "s": g.scalar, "p": g.tensor, "g": g, "y": g.sync}
    QS = {"v": "qv", "s": "qs", "p": "qp", "g": "qg"}
    V, S = g.vector, g.scalar
    ops, lastw, readers, mark, ORDER = [], {}, {}, {}, []

    def A(name, a=0, b=None, s=1):
        name, o, n = PART.get(name) or (name, 0, SCRATCH[name][1][1])
        a, b = a + o, (n if b is None else b) + o
        return (T[name][:, a:b:s] if s != 1 else T[name][:, a:b], name, np.arange(a, b, s))

    def bank(k, n, a=0):
        return (T.ps[:, 512 * k + a:512 * k + n], "ps", np.array([k]), n - a)

    def cost(**parts):
        return tuple(sum(x * sp[k] for k, x in parts.items()) for sp in SPEEDS)

    def op(q, reads, writes, call, ns, token=None, after=(), busy=None):
        reads = [x for x in reads if isinstance(x, tuple)]
        writes = [x for x in writes if isinstance(x, tuple)]
        me, deps = len(ops), set()
        for x in reads + writes:
            deps.update(int(d) for d in np.unique(lastw.setdefault(x[1], np.full(SCRATCH[x[1]][1][1], -1))[x[2]]) if d >= 0)
        for x in reads:
            if x[1] == "ps":
                deps.update(d for d, m in readers.get("ps", []) if m[x[2]].any() and ops[d][0] != q)
        for x in writes:
            name, idx = x[1], x[2]
            for d, m in readers.get(name, []):
                if m[idx].any():
                    deps.add(d)
                    m[idx] = False
            readers[name] = [y for y in readers.get(name, []) if y[1].any()]
            lastw[name][idx] = me
        for x in reads:
            m = np.zeros(SCRATCH[x[1]][1][1], bool)
            m[x[2]] = True
            readers.setdefault(x[1], []).append((me, m))
        deps.discard(me)
        ops.append((q, sorted(deps), list(after), call, ns, token, ns if busy is None else (busy,) * len(SPEEDS),
                    "%s%d" % (writes[0][1], writes[0][2][0]) if writes else None))
        return me

    def raw(x):
        return x[0] if isinstance(x, tuple) else x

    def ind(win, by):
        return win[0].indirect(by[0]) if by else win[0]

    def wide(x):
        return x[3] if x[1] == "ps" else len(x[2])

    def ns_of(o, xs, by=None, k=1.0):
        if by:
            return cost(e=50, g=1.25 * len(o[2]))
        two = all(SCRATCH[x[1]][2] in (B2, U2) for x in [o] + xs)
        return cost(e=50 + 0.83 * k * len(o[2]) * (0.5 if two else 1))

    def memset(o, c):
        return op("v", [], [o], lambda: V.memset(o[0], c), ns_of(o, []))

    def ts(o, i, s1, op0, s2=None, op1=None, by=None):
        more = () if op1 is None else (op1,)
        return op("v", [i, s1, s2, by], [o], lambda: V.tensor_scalar(o[0], ind(i, by), raw(s1), raw(s2), op0, *more), ns_of(o, [i], by))

    def tt(o, a, b, o_, by=None):
        return op("v", [a, b, by], [o], lambda: V.tensor_tensor(o[0], ind(a, by), b[0], o_), ns_of(o, [a, b], by, 1 if a[1] == "ps" else 2))

    def cp(o, i, by=None):
        return op("v", [i, by], [o], lambda: V.tensor_copy(o[0], ind(i, by)), ns_of(o, [i], by))

    def scatter(win, by, i):
        return op("v", [i, by], [win], lambda: V.tensor_copy(ind(win, by), i[0]), cost(e=50, s=2.9 * len(i[2])))

    def scan(o, d0, d1, init, op0, op1):
        return op("v", [d0, d1], [o], lambda: V.tensor_tensor_scan(o[0], d0[0], d1[0], init, op0, op1), ns_of(o, [d0, d1]))

    def total_of(o, i):
        return op("v", [i], [o], lambda: V.tensor_reduce(o[0], i[0], AxisListType.X, OP.add), cost(e=50 + 0.83 * wide(i)))

    def act(o, i, f=AF.Copy, bias=None, scale=1.0, acc=None, by=None):
        kw = {"scale": raw(scale)}
        if bias is not None:
            kw["bias"] = raw(bias)
        if acc:
            kw["accum_out"] = acc[0]
        return op("s", [i, bias, scale, by], [o, acc], lambda: S.activation(o[0], ind(i, by), f, **kw),
                  cost(e=65, g=1.25 * len(o[2])) if by else cost(e=(85 if acc else 65) + 0.83 * len(o[2])))

    def lin(o, i, scale, bias, q=None):
        if (q or CFG["lin"]) == "s":
            return act(o, i, AF.Copy if bias is None else AF.Identity, bias, scale)
        return ts(o, i, scale, OP.mult) if bias is None else ts(o, i, scale, OP.mult, bias, OP.add)

    def pick(q, o, i, by=None):
        return act(o, i, by=by) if q == "s" else cp(o, i, by)

    def quant2(p, i):
        return op("v", [i], p, lambda: V.quantize_mx(p[0][0], p[1][0], i[0]), cost(e=12 + 0.22 * len(i[2])))

    def pair(n, a=0, b=None):
        return [A(n + "q", a, b), A(n + "p", a, b)]

    def quant(n, i, a=0, b=None):
        return quant2(pair(n, a, b), i)

    def mm(o, l, r, start=True, stop=True):
        return op("p", l + r, [o], lambda: g.tensor.matmul_mx(o[0], l[0][0], l[1][0], r[0][0], r[1][0], start, stop), cost(p=40 + 0.6 * len(r[0][2])))

    def iota(o, pattern, base=0, cm=0):
        kw = {} if SCRATCH[o[1]][2] == I4 else {"allow_small_or_imprecise_dtypes": True}
        return op("g", [], [o], lambda: g.iota(o[0], pattern, base, cm, **kw), cost(e=130 + 1.66 * len(o[2])))

    def fill(o, c):
        return iota(o, [[0, len(o[2])]], c)

    def ones_at(o, pattern, base, cm):
        z = A("zz", 0, len(o[2]))
        op("g", [z], [o], lambda: g.affine_select(o[0], z[0], pattern, OP.not_equal, 1.0, base, cm), cost(e=170 + 1.66 * len(o[2])))

    last_dma = {}

    def dma(q, sem, total, out, in_, reads, writes, ns=2200):
        last_dma[q] = op(q, reads, writes, lambda: Q[q].dma_start(out, in_).then_inc(T.sem[sem], 16), cost(n=ns), (sem, total),
                         [last_dma[q]] if q in last_dma else [], 60)

    def renumber():
        for seq in ORDER:
            for x, y in zip(seq, seq[1:]):
                ops[y][2].append(x)
        done, new = {}, []
        for i in range(len(ops)):
            todo = [i]
            while todo:
                j = todo[-1]
                left = [d for d in ops[j][1] + ops[j][2] if d not in done]
                if left:
                    todo.extend(left)
                    continue
                todo.pop()
                if j not in done:
                    done[j] = len(new)
                    new.append(j)
        ops[:] = [(o[0], [done[d] for d in o[1]], [done[d] for d in o[2]]) + tuple(o[3:]) for o in (ops[j] for j in new)]

    def emit():
        renumber()
        if "order" not in _PLAN:
            _PLAN["order"] = _plan(ops)
        count, known, token = {}, {}, {}
        for i in _PLAN["order"]:
            q, deps, _, call, _, tok = ops[i][:6]
            if q != "net":
                w = {}
                for d in deps:
                    if not (q == "p" and ops[d][0] == "p"):
                        w[token[d][0]] = max(w.get(token[d][0], 0), token[d][1])
                for sem, val in w.items():
                    if val > known.get((q, sem), 0):
                        Q[q].wait_ge(T.sem[sem], val)
                        known[(q, sem)] = val
                r = call()
                if tok is None:
                    tok = (QS[q], count.get(QS[q], 0) + 1)
                    r.then_inc(T.sem[tok[0]], 1)
            token[i] = tok
            count[tok[0]] = tok[1]
        for sem, val in count.items():
            g.wait_ge(T.sem[sem], val)

    (CQ, CQ1, CQ4, CQ41, CG, CS16, CS4, CT4, CQ2, CP, CPO, CH16, CH4, CU4, CQ16, CL4,
     CF16, CD, CDN) = [A("pc", k, k + 1) for k in range(19)]
    CB, CY, CZ = A("tab", 32, 33), A("tab", 33, 34), A("tab", 34, 35)
    HALVES = ((0, HALF), (HALF, C))

    def W(k, a=0, b=NB):
        return A("wf", 32 * k + a, 32 * k + b)

    def vec(k, a=0, b=16):
        return A("vec", 16 * k + a, 16 * k + b)

    def back(x):
        a, b = int(x[2][0]), int(x[2][-1])
        return (T[x[1]][:, b::-1] if a == 0 else T[x[1]][:, b:a - 1:-1], x[1], x[2])

    def keep(row, a, b, dst):
        scan(A("exh", a, b), A("k16", a, b), row, 0.0, OP.mult, OP.add)
        ts(dst, A("exh", a + 15, b, 16), CH16, OP.mult, float(HALF), OP.add)

    def wrap4(row, n, dst, a=0, add=CU4):
        scan(A("exh", a, a + n), A("k4", 0, n), row, 0.0, OP.mult, OP.add)
        ts(dst, A("exh", a + 3, a + n, 4), CH4, OP.mult, add, OP.add)

    def hold(dst, row):
        scan(dst, row, A("kx"), -512.0, OP.max, OP.add)

    dma("y", "lu", 16, T.ut[:], T.u[:], [], [A("ut")])
    cut = 4 * PIECE[0][0]
    dma("s", "lh", 16, T.x0[:, cut:4 * C], T.x[:, cut:4 * C], [], [A("x0", cut, 4 * C)], 2400)
    dma("y", "lx", 16, T.x0[:, 0:cut], T.x[:, 0:cut], [], [A("x0", 0, cut)], 2500)
    dma("y", "lw", 32, T.wq[:].bitcast(dt.uint8), T.wc[:], [], [A("wq")])
    dma("y", "lw", 32, T.wp[:], T.ws[:], [], [A("wp")])
    dma("y", "lv", 16, T.vt[:], T.v[:], [], [A("vt")])

    def pi(k):
        return A("pi", k, k + 1)

    def tab(k):
        return A("tab", 16 * k, 16 * k + 16)

    EYE = tab(8)
    iota(pi(0), [[0, 1]], 0, 1)
    J16 = A("c16")
    iota(J16, [[1, 16]])
    iota(A("cw"), [[16, NB]])
    iota(tab(1), [[0, 4], [1, 4]])
    iota(A("g32"), [[-16, 8], [0, 4]], 16, 1)
    iota(tab(15), [[1, 4], [-1, 4]])
    memset(A("tab", 160, 240), 0.0)
    memset(tab(11), 1.0)
    fill(A("ones"), 1)
    memset(A("zz"), 0.0)
    ones_at(A("em"), [[-1, 528]], 3, 4)
    ones_at(A("eye"), [[1, 128], [0, 4]], 0, -1)
    for a, b in ZERO:
        dma("y", "lf", 16 * len(ZERO), T.fl[:, 4 * a:4 * b], T.zz[:, 0:4 * (b - a)], [A("zz", 0, 4 * (b - a))], [A("fl", 4 * a, 4 * b)])
    fill(A("win", 0, 4 * C), 0)
    iota(A("cnt", 0, L), [[2, L]], C)
    iota(A("cnt", L, C), [[-2, C - L]], -C - 2 * L)
    fill(A("eqr"), 1)
    iota(A("kr4"), [[0, NB], [512, 4]])
    fill(A("wm", 0, 56, 2), -4096)
    fill(A("h3", 1, 48 * NB + 48, 3), -1024)
    fill(A("k13"), 1)
    fill(A("k13", 0, LT * NB, LT), 0)
    iota(A("cne"), [[2, C]], -C)
    iota(A("k5"), [[0, 84], [256, 5]])
    fill(A("lh"), 0)
    fill(A("k6"), 1)
    fill(A("k6", 0, LN * NB, LN), 0)
    fill(A("tl"), 0)
    fill(A("nl"), 0)
    fill(A("gt", C, C + 16), 0)
    fill(A("lr"), 0)
    fill(A("sn"), 0)
    fill(A("ev"), 0)
    iota(A("ev", 7, 9), [[-1, 2]], C + 1)

    ts(pi(1), pi(0), 15, OP.bitwise_and)
    cp(CQ, pi(1))
    ts(pi(3), pi(1), 2, OP.arith_shift_right)
    ts(pi(4), pi(1), 3, OP.bitwise_and)
    ts(A("qo"), A("cw"), 0.0, OP.mult, CQ, OP.add)
    ts(EYE, J16, CQ, OP.is_equal)
    lin(CQ1, CQ, 1.0, 1.0)
    ts(CB, pi(1), -BIG, OP.mult)
    iota(A("kr"), [[0, NB], [512, 16]])
    act(A("cm"), A("kr"), AF.Abs, CB, BIG / 512)
    lin(A("kb"), A("kr"), BIG / 256, -BIG)
    ts(tab(4), J16, CQ, OP.is_lt, -512.0, OP.mult)
    lin(tab(3), EYE, 256.0, 0.0)
    ts(tab(7), J16, CQ1, OP.is_equal, F, OP.mult)
    tt(tab(4), tab(4), tab(3), OP.add)
    lin(tab(0), EYE, -1.0, 1.0)
    cp(A("ulu"), A("cw", 0, 8))
    lin(A("tab", 79, 80), A("tab", 79, 80), 1.0, -512.0)
    tt(tab(7), tab(7), tab(0), OP.max)
    act(A("kx"), tab(4), by=A("qo"))
    act(A("k16"), tab(7), by=A("qo"))
    fill(A("pf", C, 512), 0)
    ts(pi(5), pi(1), 1, OP.arith_shift_right)
    cp(CQ4, pi(3))
    lin(CQ41, CQ4, 1.0, 1.0)
    act(CP, CQ, AF.Abs, -2.0)
    cp(CT4, pi(4))
    lin(CU4, CT4, 1.0, 2.0 * C)
    lin(CL4, CT4, 1.0, 2.0 * C - 4.0 * A0)
    cp(CQ2, pi(5))
    ts(CS4, pi(3), 3.0, OP.is_equal, 4.0 - 4.0 / F, OP.mult)
    ts(CP, CP, 1.0, OP.is_le)
    lin(CH16, A("tab", 143, 144), 0.5 - 0.5 / F, 0.5 / F)
    lin(CS4, CS4, 1.0, 4.0 / F)
    lin(CH4, CS4, 0.5, 0.0)
    quant("u", A("ut"))
    op("v", [A("uq"), A("ulu")], [A("urq")], lambda: V.tensor_copy(
        T.urq[:, 0:128].bitcast(dt.uint32), T.uq[:, 0:128].bitcast(dt.uint32).indirect(T.ulu[:, 0:8])), cost(e=50, g=190))
    op("s", [A("up"), A("ulu")], [A("urp")], lambda: S.activation(T.urp[:, 0:128], T.up[:, 0:128].indirect(T.ulu[:, 0:8]), AF.Copy), cost(e=65, g=160))
    ts(A("go"), A("g32"), 0.0, OP.max, 47.0, OP.min)
    ts(tab(13), tab(15), 0.0, OP.is_equal)
    act(A("cst"), A("tab", 160, 208), by=A("go"))
    act(A("cpt"), A("tab", 192, 240), by=A("go"))
    lin(CPO, CS4, -C / 4.0, 0.0)
    lin(A("jw", 42, 70), A("cw"), 1.0, CQ)
    ts(tab(6), tab(1), CQ4, OP.is_lt, -1024.0, OP.mult)
    ts(tab(9), tab(1), CQ4, OP.is_equal, 512.0, OP.mult)
    tt(tab(6), tab(6), tab(9), OP.add)
    act(A("ky"), tab(6), by=A("qo", 0, W4 // 16))
    lin(CF16, CH16, 2.0, 0.0)
    lin(CD, CQ, 1.0, C + 1.0)
    lin(CDN, CQ, -1.0, -C - 1.0)
    quant("ey", A("eye"))
    ts(tab(5), tab(1), CQ41, OP.is_equal, F, OP.mult)
    ts(tab(1), tab(1), CQ4, OP.not_equal)
    quant("cp", A("cpt"))
    quant("cs", A("cst"))
    lin(A("jw", 14, 42), A("cw"), 0.5, CQ2)
    lin(CY, A("tab", 99, 100), 1.0, 16.0 * ND + 15.0 - 512.0 - 4096.0)
    lin(CY, CQ, -1.0, CY)
    lin(CZ, CY, 1.0, float(C * 3))
    fill(A("kb4"), 512)
    iota(A("kb4", 0, W4 - 4 * NV, 4), [[-16, NB - NV]], 16 * (ND - NV))
    lin(A("jw", 0, 14), A("jw", 42, 56), 1.0, 0.0)
    lin(A("jw", 70, 84), A("jw", 42, 56), 1.0, float(HALF))
    lin(A("jw", 84, 112), A("jw", 42, 70), -1.0, float(C))
    tt(tab(5), tab(5), tab(1), OP.max)
    act(A("k4"), tab(5), by=A("qo", 0, HALF // 16))
    quant("v", A("vt"))
    for b in range(4):
        quant2([A("eq4", 128 * b, 128 * b + 128), A("ep4", 128 * b, 128 * b + 128)], A("em", 3 - b, 515 - b))
    PART["cwc"] = ("tab", 144, 16)
    fill(A("cwc"), C)

    def E(b):
        return [A("eq4", 128 * b, 128 * b + 128), A("ep4", 128 * b, 128 * b + 128)]

    JW = A("jw", 42, 70)
    EU, HN, HM, ST, XV, NN, NH, AH, SU, EC, EQ = range(11)
    EV, HH = (lambda a=0, b=16: A("ev", 8 + a, 8 + b)), (lambda a=0, b=16: A("ev", 24 + a, 24 + b))

    def brackets(K):
        ev = EV()
        ts(A("ei"), ev, 0.5, OP.mult, -0.25, OP.add)
        lin(vec(EU), ev, 1.0, -0.5)
        cp(HH(), A("ei"))
        lin(vec(HN), HH(), -1.0, 0.5)
        lin(vec(HM), HH(), 1.0, -float(HALF))
        for k in range(1, K):
            s = A("sgn", 42 * (k - 1), 42 * k)
            act(s, A("jw", 0, 42), AF.Sign, bias=vec(HN, k, k + 1))
            act(A("lh", k - 1, 210, 5), s, scale=HH(k, k + 1))
            act(A("lh", 209 + k, 420, 5), s, scale=vec(HM, k, k + 1))
        scan(A("lo"), A("k5"), A("lh"), 0.0, OP.min, OP.max)
        tt(A("wi", 1, 84, 2), A("jw", 42, 84), A("lo", 74, 280, 5), OP.subtract)
        tt(A("wi", 85, 112, 2), A("jw", 0, 14), A("lo", 4, 70, 5), OP.add)
        cp(A("fiw"), A("wi", 57, 112, 2))
        tt(A("wi", 0, 56, 2), JW, A("lo", 284, 420, 5), OP.add)
        tt(W(2), A("wi", 0, 56, 2), A("lo", 74, 210, 5), OP.subtract)
        lin(A("wm", 1, 56, 2), W(2), 4096.0, -4096.0 * (HALF - 0.5))
        scan(A("wn"), A("wm"), A("wi", 0, 56), 0.0, OP.min, OP.max)
        cp(A("fw"), A("wn", 1, 56, 2))
        act(A("fr"), A("cne"), by=A("fw"))
        scan(A("eq", 0, 32), A("ev", 8, 40), A("kx", 0, 32), -512.0, OP.max, OP.add)
        scan(A("eq", 32, 48), A("ev", 7, 23), A("kx", 0, 16), -512.0, OP.max, OP.add)
        e, h, d = A("eq", 15, 16), A("eq", 31, 32), A("eq", 47, 48)
        x = [vec(EQ, k, k + 1) for k in range(4)]
        act(x[0], e, AF.Sign, d, -1.0)
        lin(x[0], x[0], CDN, CD)
        lin(x[1], e, 1.0, 256.0)
        ts(A("eqw", 0, 1), x[1], x[0], OP.max)
        scatter(A("eqr"), A("eqw", 0, 1), A("zz", 0, 16))
        lin(vec(EC), ev, -1.0, float(C))
        for k in range(1, K):
            act(A("sge", 32 * k, 32 * k + NB), JW, AF.Sign, bias=vec(EU, k, k + 1), scale=-1.0)
            act(A("nl", k, LN * NB, LN), A("sge", 32 * k, 32 * k + NB), scale=vec(EC, k, k + 1))
        scan(A("no"), A("k6"), A("nl"), 0.0, OP.mult, OP.max)
        tt(A("wd", 1, 3 * NB, 3), A("jw", 84, 112), A("no", LN - 1, LN * NB, LN), OP.subtract)
        lin(A("wd", 2, 3 * NB, 3), A("no", LN - 1, LN * NB, LN), 1.0, 255.0 - 2048.0)
        lin(x[2], h, -2.0, x[1])
        lin(x[3], h, 1.0, 256.0 - C)
        lin(x[2], x[2], 1.0, -512.0)
        ts(A("xi", 0, 1), x[3], x[2], OP.mult, float(C), OP.add)
        tt(vec(ST), HH(), ev, OP.subtract)
        tt(vec(ST, 0, 8), vec(ST, 0, 8), HH(1, 9), OP.subtract)
        scan(back(vec(SU)), back(vec(ST)), A("cwc"), 0.0, OP.add, OP.add)

    def quant_x(xb):
        for a, b in PIECE:
            quant("x", A(xb, 4 * a, 4 * b), a, b)

    quant_x("x0")
    sends, sent = [], {}
    for t in range(R):
        K = 4 + t
        xb = "x0" if t == 0 else "xs"
        sn, an = (lambda a=0, b=8, t=t: A("sn", 8 * t + a, 8 * t + b)), (lambda a=0, b=8, t=t: A("an", 8 * t + a, 8 * t + b))
        mm(bank(5, C - LOW), pair("ur"), pair("x", LOW, C))
        mm(bank(0, LOW), pair("ur"), pair("x", 0, LOW))
        mm(bank(1, C - 16), pair("ur"), pair("x", 0, C - 16))
        for n, k, a, b in (("h", 5, LOW, C), ("l", 0, 0, LOW)):
            mark["y" + n] = tt(A("yy", a, b), bank(k, b - a), A("cm", a, b), OP.subtract)
            mark["h" + n] = scan(A("hd", a, b), A("kb", a, b), A("yy", a, b), -BIG, OP.min, OP.max)
        mark["hx"] = scan(back(A("hx")), A("kb", 0, LOW), back(A("hd", 0, LOW)), -BIG, OP.min, OP.max)
        between = {}
        if t == 0:
            mm(bank(7, C), pair("u"), pair("x"))
            mark["p1"] = ts(A("pf", 0, C), bank(7, C), 0.0, OP.is_gt, CP, OP.mult)
            mark["p2"] = quant("pf", A("pf"))
            mm(bank(6, 128), pair("cp"), pair("pf"))
            mark["p3"] = scan(A("ex", 0, W4), A("k4", 0, W4), bank(6, W4), 0.0, OP.mult, OP.add)
            lin(A("base"), A("ex", 3, W4, 4), CPO, CZ)
            between[3] = [act(A("pf", NB * k, NB * (k + 1)), A("ex", 3, W4, 4), AF.Sign, 2.0 - 4.0 * k, CS4) for k in range(1, K)]
            mark["p4"] = quant("pf", A("pf"))
            mm(bank(7, 128), pair("cs"), pair("pf"))
            between[6] = [act(W(11 + k, 0, NB // 4), bank(7, NB // 4 * (k + 1), NB // 4 * k), AF.Identity, 2.0 * C / NB, 0.5, EV(k, k + 1))
                          for k in range(1, K)]
            brackets(K)
        where = {d: 4 * a for tiles, at, _, _, _ in GROUPS for d, a in zip(tiles, at)}
        rows = [d for tiles in ROWS for d in tiles if d not in VROWS[t]]
        o, first, second = 0, [], []
        for d in rows:
            h = A("sg", o, o + 16 * d)
            o += 16 * d
            first.append(act(h, bank(1, 16 * d), AF.Sign, bias=A("hd", 16 * d + 15, 16 * d + 16), scale=-1.0))
            second.append(act(A("fl", where[d], where[d] + 16 * d), h, AF.Relu, acc=A("rs", d, d + 1)))
        ORDER.append(first[:1] + [x for k, y in enumerate(zip(first[1:], second)) for x in list(y) + between.get(k, [])] + second[-1:])

        def sums(m):
            tiles, at, aq, pre, post = GROUPS[m]
            pre, post = (pre, post) if t == 0 or len(tiles) == 1 else (0, 0)
            n = at[-1] - at[0] + _long(tiles[-1])
            mark["s%d" % m] = quant("fl", A("fl", 4 * (at[0] - pre), 4 * (at[0] + n + post)), aq[0] - pre, aq[0] + n + post)
            for d, q0 in zip(tiles, aq):
                if d < NV:
                    c = q0 + 4 * d - WR
                    mm(bank(3, 128), pair("ey"), pair("fl", c, c + 128), d == DIAG[0][0], d == DIAG[-1][-1])
                if d == 0:
                    mm(bank(4, 128), pair("ey"), pair("fl", q0, q0 + 128))
                if d in VROWS[t]:
                    mm(bank(6, 128), pair("ey"), pair("fl", q0, q0 + 128))
                    act(W(11, 0, 4 * d), bank(6, 4 * d), acc=A("rs", d, d + 1))
            for d, q0 in zip(tiles, aq):
                mm(bank(2, 128), pair("cp"), pair("fl", q0, q0 + 128), d == DIAG[0][0], d == ROWS[-1][-1])

        vord = [x for x in VORD if (t == 0 if x[0] == "p" else x[0] in "yhs" or int(x[:-1]) < NV or int(x[:-1]) in VROWS[t])]
        for x in vord:
            if x[0] == "s":
                sums(int(x[1:]))
            elif x[0] not in "yhp":
                d = int(x[:-1])
                a = where[d]
                if d >= NV:
                    mark[x] = ts(A("fl", a, a + 16 * d), bank(0, 16 * d), A("hd", 16 * d + 15, 16 * d + 16), OP.is_lt)
                elif x == "0b":
                    mark[x] = tt(A("fl", a + LOW, a + C), bank(5, C - LOW), A("hd", LOW, C), OP.is_le)
                elif x[-1] == "a":
                    mark[x] = tt(A("fl", a + 16 * d, a + LOW), bank(0, LOW, 16 * d), A("hx" if d else "hd", 0, LOW - 16 * d), OP.is_le)
                else:
                    mark[x] = tt(A("fl", a, a + 16 * d), bank(0, 16 * d), A("hx", LOW - 16 * d, LOW), OP.is_lt)
        ORDER.append([mark[x] for x in vord])
        for a, b in HALVES:
            act(A("xh", 4 * a, 4 * b), A(xb, 4 * a, 4 * b), scale=0.5)
        n = 4 * NV + WR
        scan(A("xb", 4 * NV, W4), A("kb4"), bank(4, W4, 4 * NV), 0.0, OP.min, OP.add)
        scan(A("xr", 0, n), A("kr4", 0, n), bank(3, n), 0.0, OP.min, OP.add)
        tt(A("base", NV, NB), A("base", NV, NB), A("xb", 4 * NV + 3, W4, 4), OP.subtract)
        tt(A("base", NV - ND, NV), A("base", NV - ND, NV), A("xr", 3, WR, 4), OP.subtract)
        tt(A("ky", 3, 4 * NV, 4), A("base", 0, NV), A("xr", WR + 3, n, 4), OP.subtract)
        for a, b in ((NV, rows[-1]), (rows[-1], rows[-1] + 1), (rows[-1] + 1, NB)):
            if b == a + 1:
                lin(A("ky", 4 * a + 3, 4 * a + 4), A("rs", a, b), -1.0, A("base", a, b))
            elif b > a:
                tt(A("ky", 4 * a + 3, 4 * b, 4), A("base", a, b), A("rs", a, b), OP.subtract)
        scan(A("ex0"), bank(2, W4), A("ky"), -1024.0, OP.max, OP.add)
        ts(A("o1"), A("ex0", 3, W4, 4), 4096.0, OP.add)
        n = K * C
        scatter(A("win", 0, n), A("o1"), A("ones", 0, C))
        scan(A("so", 0, n), A("win", 0, n), A("win", 0, n), -C - 2.0, OP.add, OP.add)
        act(A("plr", HALF, C), A("so", 0, n), by=A("o1", 14, NB))
        cp(A("plr", 0, HALF), A("so", 0, n), A("o1", 0, 14))
        if t + 1 < R:
            fill(A("win", 0, n + C), 0)
        keep(A("plr"), 0, C, A("plw"))
        scatter(A("orow"), A("plw"), A("cne"))
        cp(A("abr", HALF, C), A("orow"), by=A("fiw", 0, 14))
        act(A("abr", 0, HALF), A("orow"), by=A("fiw", 14, NB))
        wrap4(A("abr", HALF, C), HALF, A("ab4", 2 * NB, 4 * NB), HALF)
        wrap4(A("abr", 0, HALF), HALF, A("ab4", 0, 2 * NB))
        ORDER.append([pick(q, A("bh", 16 * a, 16 * b), A("xh"), A("ab4", 2 * NB + a, 2 * NB + b)) for q, (a, b) in zip(CFG["zb"], ZP)][CFG["zb"].count("v"):])
        ORDER.append([tt(A("zt", 16 * a, 16 * b), A("xh"), A("bh", 16 * a, 16 * b), OP.add, by=A("ab4", a, b)) for a, b in ZP])
        p0 = t * SPW
        for r, (a, b, c) in enumerate(RUNS):
            act(A("xn", 4 * a, 4 * b), A(xb), by=A("ab4", a // 4, b // 4))
            lin(A("bb", 4 * a, 4 * b), A("bh", 4 * a, 4 * b), 2.0, None, CFG["bb"])
            o = p0 + NS + 128 * r
            qz, qh = [A("zq", 128 * r, 128 * r + 128), A("sp", o, o + 128)], [A("hq", 128 * r, 128 * r + 128), A("sp", o + 256, o + 384)]
            banks = ((3, 4, 5, 6), (0, 1, 2, 7))[r]
            quant2(qz, A("zt", 4 * c, 4 * c + 512))
            for k in range(4):
                mm(bank(banks[k], 128), pair("w", 128 * k, 128 * k + 128), qz)
            for k in range(4):
                lin(A("ht", 4 * a + k, 4 * b, 4), bank(banks[k], b - c, a - c), 0.03125, None, CFG["ht"][r][k])
            quant2(qh, A("ht", 4 * c, 4 * c + 512))
            mm(bank(3 + 2 * r, 128), pair("ur"), qh)
            mm(bank(4 + 2 * r, 128), pair("ur"), qh)
            ts(A("gt", a, b), bank(3 + 2 * r, b - c, a - c), 0.0, OP.is_le)
            act(A("gt", HALF + a, HALF + b), bank(4 + 2 * r, b - c, a - c), AF.Sign)
            sends.append(op("g", [A("ht", 4 * a, 4 * b), A("xn", 4 * a, 4 * b)], [A("xn", 4 * a, 4 * b)],
                            lambda a=4 * a, b=4 * b, s=T.sem["acc%d" % r]: g.dma_start(T.xn[:, a:b], T.ht[:, a:b], accum_op=OP.add).then_inc(s, 16),
                            cost(n=NET["add"]), ("acc%d" % r, 16 * t + 16), sends[-1:], 1000))
        for a, b in zip(CFG["bh"], CFG["bh"][1:]):
            tt(A("xn", 2 * C + a, 2 * C + b), A("bb", a, b), A("ht", a, b), OP.subtract)

        def send(x, reads, call, arrives, n):
            s = op("g", reads, [], call, cost(n=300), SENT, [sent[y] for y in BEHIND[min(t, 1)].get(x, "")])
            sends.append(s)
            sent[x] = s
            op("net", [], arrives, None, cost(n=NET[x]), ("a%s%d" % (x, t), n), [s], 0)

        def small(x, w):
            rid, pid = topo.addr(relays[0], core)
            a = (T["r" + x][:, w * t:w * t + w], T["s" + x][:, w * t:w * t + w], T.sem["h%s%d" % (x, t)], T.sem.sent, pid, rid, topo.mask(core, relays[0]))
            send(x, [A("s" + x, w * t, w * t + w)], lambda: g.remote_dma(*a), [A("a" + x, w * t, w * t + w)], n_in[0])

        tt(vec(XV), A("gt"), vec(SU), OP.add, by=A("xi", 0, 1))
        tt(sn(), vec(XV, 0, 8), vec(XV, 1, 9), OP.subtract)
        small("n", 8)
        for x, banks in (("b", (3, 4, 5, 6)), ("a", (0, 1, 2, 7))):
            a, b = PIECES[x]
            quant2([A("sq", t * NS + a, t * NS + b), A("sp", p0 + a, p0 + b)], A("xn", 4 * (A0 + a), 4 * (A0 + b)))
            tr, w = [], 2 * (b - a)
            for k in (1, 2, 3):
                rid, pid = topo.addr(relays[k], core)
                c, d = _share(k, x, t)
                if k < 3:
                    src, dst = T.sq[:, c:d].bitcast(dt.uint8), T.rq[:, c:d].bitcast(dt.uint8)
                else:
                    src, dst = T.sp[:, p0 + a:p0 + a + w], T.rp[:, 2 * (t * NS + a):2 * (t * NS + a) + w]
                engs = topo.engines(core, relays[k])
                tr.append(RemoteDMATransfer(dst_ids=[DstId(rid=rid, pnc=pid)], dma_engine_mask=_mask((engs[1::4], engs[0::4], engs[2::4])[k - 1]),
                                            remote_sem=T.sem["h%s%d" % (x, t)], src=src, dst=dst))
            came = [A("aq", t * NS + a, t * NS + b), A("ap", t * NS + a, t * NS + b)]
            send(x, [A("sq", t * NS + a, t * NS + b), A("sp", p0 + a, p0 + a + w)],
                 lambda tr=tr: g.remote_dma_fused(tr, local_sem=T.sem.sent), came, sum(n_in[1:]))
            for k in range(4):
                mm(bank(banks[k], b - a), E(k), came)
                pick(CFG["un"][k], A("dn", 4 * a + k, 4 * b, 4), bank(banks[k], b - a))
        gv = CFG["gv"]
        act(A("gb", 16 * gv, C), A("gt"), AF.Relu, by=A("fw", gv, NB))
        ts(A("gb", 0, 16 * gv), A("gt"), 0.5, OP.is_gt, by=A("fw", 0, gv))
        scan(A("la"), A("eqr", 0, C), A("gb"), 0.0, OP.mult, OP.add)
        scan(back(A("lb")), back(A("eqr", 1, C + 1)), back(A("gb")), 0.0, OP.mult, OP.add)
        if t + 1 < R:
            fill(A("eqr"), 1)
        hold(A("exb"), A("gb"))
        hold(A("h3", 0, 3 * C, 3), A("la"))
        hold(A("h3", 32, 3 * C + 32, 3), A("lb"))
        lin(A("wd", 0, 3 * NB, 3), A("exb", 15, C, 16), -1024.0, -1024.0 * 256.0, CFG["mg"])
        scan(A("wo"), A("h3", 45, 45 + 48 * NB, 16), A("wd"), -4096.0, OP.max, OP.add)
        ts(A("jlw"), A("wo", 2, 3 * NB, 3), 2048.0, OP.add)
        scatter(A("lr"), A("jlw", B0, NB), A("fr", P0, C))
        wrap4(A("lr", 0, L), L, A("sl", 32 * t, 32 * t + 32), 0, CL4)
        small("l", 32)
        act(A("slc"), A("fr"), by=A("plw"))
        scan(A("exs"), A("k16"), A("slc"), 0.0, OP.mult, OP.add)
        lin(W(9), A("exs", 15, C, 16), CF16, None)
        act(A("m2r"), A("cnt"), by=A("jlw"))
        act(A("pcol"), A("m2r"), by=A("plw"))
        scan(A("ex"), A("k16"), A("pcol"), 0.0, OP.mult, OP.add)
        lin(W(8), A("ex", 15, C, 16), CF16, None)
        tt(W(10), W(8), W(9), OP.max)
        for k in range(4):
            ts(A("nx", NB * k, NB * k + NB), W(10), 2.0, OP.mult, 2.0 * C + k, OP.add)
        lin(vec(NH, 0, 8), sn(), -2.0, 1.0 - C)
        lin(vec(AH, 0, 8), an(), -2.0, 1.0 - C)
        for k in range(K):
            act(A("tl", k, LT * NB, LT), W(8), AF.Sign, vec(AH, k, k + 1), 1.0)
            act(A("tl", LN + k, LT * NB, LT), W(8), AF.Sign, vec(NH, k, k + 1), -1.0)
        scan(A("to"), A("k13"), A("tl"), 0.0, OP.mult, OP.add)
        if t + 1 < R:
            lin(A("base"), A("to", LT - 1, LT * NB, LT), -C / 2.0, CY)
            ts(vec(NN, 0, 8), sn(), float(L), OP.max, -1.0, OP.mult)
            ts(vec(NN, 8, 16), an(), float(L), OP.min, -float(C + L), OP.add)
            tt(EV(1, K + 1), vec(NN, 0, K), vec(NN, 8, 8 + K), OP.subtract)
            brackets(K + 1)
        else:
            ts(A("ttw"), A("to", LT - 1, LT * NB, LT), 0.5, OP.mult, float(K), OP.add)
            act(A("pout"), A("c16"), by=A("ttw"))
        for k, q in enumerate("sv"):
            pick(q, A("xn", 4 * C + 2 * L * k, 4 * C + 2 * L * (k + 1)), A("dn"), A("al", 32 * t + 16 * k, 32 * t + 16 * k + 16))
        for q, k, a, b in SHARE:
            pick(q, A("xs", 4 * a + k, 4 * b, 4), A("xn"), A("nx", NB * k + a // 16, NB * k + b // 16))
        quant_x("xs")

    total = 16 * (6 + len(PIECE))
    dma("y", "out", total, T.oc[:], T.xq[:].bitcast(dt.uint8), [A("xq")], [])
    for m in range(4):
        dma("y", "out", total, T.osc[4 * m:4 * m + 4, :], T.xp[32 * m:32 * m + 4, :], [A("xp")], [])
    dma("y", "out", total, T.pts[:], T.pout[0:128:16, :], [A("pout")], [])
    for k, (a, b) in enumerate(PIECE):
        mm(bank(k, b - a), pair("v"), pair("x", a, b))
        pick("vs"[k], A("yo", a, b), bank(k, b - a))
        dma("ys"[k], "out", total, T.y[:, a:b], T.yo[:, a:b], [A("yo", a, b)], [])
    emit()
